import numpy as np, ml_dtypes
CORES = [40,41,42,43,44,45,46,47]
N = 8
import mx_ref
BF = ml_dtypes.bfloat16
def gentries(a):
    return np.ascontiguousarray(a.reshape(8, 16, -1).transpose(0, 2, 1)).reshape(8, -1)
def gtable(e):
    e = np.asarray(e); return np.ascontiguousarray(e.reshape(8, -1, 16).transpose(0, 2, 1)).reshape(128, -1).astype(np.int32)
def gcols(t, e):
    v = np.concatenate([t.reshape(8, 16, -1, 4), np.zeros((8, 16, 1, 4), BF)], axis=2)
    return np.ascontiguousarray(np.stack([v[g][:, e[g]] for g in range(8)])).reshape(128, -1)
def tile(rs):
    return np.stack(rs, axis=2).reshape(128, -1).astype(BF)
def pick(q, e):
    c = np.concatenate([q[0].reshape(128, -1, 4), np.zeros((128, 1, 4), np.uint8)], axis=1); s = np.concatenate([q[1], np.ones((16, 1), np.uint8)], axis=1)
    return (np.ascontiguousarray(c[:, e].reshape(128, -1)), np.ascontiguousarray(s[:, e]))
def join(*qs):
    return (np.concatenate([q[0] for q in qs], axis=1), np.concatenate([q[1] for q in qs], axis=1))
def put(q, e, v):
    c, s = q[0].reshape(128, -1, 4).copy(), q[1].copy(); c[:, e] = v[0].reshape(128, -1, 4); s[:, e] = v[1]
    return (c.reshape(128, -1), s)
def pk(c, s):
    return (np.ascontiguousarray(c), mx_ref.live(s))
def emit(q):
    return q[0], q[1]
def packed(v, rng):
    q = [mx_ref.quantize(np.ascontiguousarray(v[r])) for r in range(N)]
    return np.stack([a for a, b in q]), np.stack([mx_ref.plane(b, rng) for a, b in q])
def values_of_codes():
    e, c = np.zeros((128, 128, 4), np.float32), np.zeros((128, 2, 4), np.uint8)
    e[np.arange(128), np.arange(128), 0] = 1
    c[:127, :, 0] = np.arange(256).reshape(2, 128).T[:127]
    return mx_ref.matmul(mx_ref.quantize(e.reshape(128, 512).astype(BF)), (c.reshape(128, 8), np.full((16, 2), 127, np.uint8))).T.reshape(-1).astype(np.float64)
CODE_VALUE, SCALE_VALUE = values_of_codes(), 2.0 ** (np.arange(256) - 127.0)
def decode(q):
    return (CODE_VALUE[q[0]].reshape(16, 8, -1, 4) * SCALE_VALUE[q[1]][:, None, :, None] + 0.0).reshape(128, -1).astype(np.float32)
def f(rng, *shape):
    return mx_ref.flush((rng.standard_normal(shape, dtype=np.float32) * np.exp2(rng.integers(-2, 3, shape[:-1] + (1,)))).astype(BF))
def wide(rng, *shape, cols=0):
    v = rng.standard_normal(shape, dtype=np.float32) * np.exp2(rng.integers(-12, 13, shape)).astype(np.float32)
    if cols: v *= np.repeat(np.exp2(rng.integers(-cols, cols + 1, shape[:-2] + (1, shape[-1] // 4))) * (rng.random(shape[:-2] + (1, shape[-1] // 4)) > 0.0625), 4, axis=-1).astype(np.float32)
    return mx_ref.flush(v.astype(BF))
C, H = 384, 192
STEP = [1, 2, 4]
PLACES = np.arange(C)
def numbers_of(rng):
    return {"x": np.array(f(rng, N, 128, 4 * C)), "u": np.array(f(rng, N, 128, 512)), "v": np.array(f(rng, N, 128, 512))}
def drawn(rng):
    o = rng.permuted(np.tile(PLACES, (N, 8, 3, 1)), axis=3)
    k = np.zeros_like(o)
    np.put_along_axis(k, o, o.reshape(N, 8, 3, H, 2)[..., ::-1].reshape(N, 8, 3, C), axis=3)
    e = np.tile(PLACES, (N, 8, 1))
    return rng.permuted(e, axis=2), rng.permuted(e, axis=2), k
def stored(p, e, k):
    return {"pp": np.stack([gtable(p[r]) for r in range(N)]), "rf": np.stack([gtable(e[r]) for r in range(N)]), "pr": np.stack([gtable(k[r].reshape(8, 3 * C)) for r in range(N)])}
def layers(rng, still=[]):
    w = np.array(f(rng, N, 128, 2048)).reshape(N, 8, 16, 4, 8, 16, 4)
    for i in still:
        w[:, :, i] = 0
        w[:, :, :, :, :, i] = 0
    return w
def weights(rng, w):
    c, s = packed(np.ascontiguousarray(w).reshape(N, 128, 2048), rng)
    return {"wc": c, "ws": s}
def scoring(d):
    u = d["u"].reshape(N, 128, 128, 4)
    u[:, :, ::16] = 0
    u[:, :, 1::16] = 0
    return u
def setup_inputs(rng):
    return {**numbers_of(rng), **stored(*drawn(rng)), **weights(rng, layers(rng))}
def setup_inputs_ties(rng):
    d = numbers_of(rng)
    p, e, k = drawn(rng)
    o = rng.permutation(N)
    k[o[3], :4] = k[o[3], :4, :1]
    a, b = rng.integers(-1, 2, (2, N, 8, C))
    a[o[0]] = 0
    a[o[1]] = 1
    b[o[1], :4] = 1
    b[o[1], 4:] = 0
    for g in range(4): a[o[3], g, p[o[3], g]] = np.where(PLACES < k[o[3], g, 0], 1, -rng.integers(0, 2, C))
    x = d["x"].reshape(N, 8, 16, C, 4)
    x[:, :, 0] = 0
    x[:, :, 0, :, 0] = a.astype(np.float32).astype(BF)
    x[:, :, 0, :, 1] = b.astype(np.float32).astype(BF)
    u = scoring(d)
    for h in range(0, 128, 16):
        u[:, h, h, 0] = 1
        u[:, h, h + 1, 1] = 1
    return {"x": x.reshape(N, 128, 4 * C), "u": u.reshape(N, 128, 512), "v": d["v"], **stored(p, rng.integers(0, C, (N, 8, C)), k), **weights(rng, layers(rng, [0]))}
def setup_inputs_near(rng):
    d = numbers_of(rng)
    o = rng.permutation(N)
    z = int(np.argmax(o))
    k = np.where(o % 2 == 0, 2.0 ** -30, 1.0)
    x = np.zeros((N, 8, 16, C, 4))
    for i in (0, 2):
        s = rng.integers(-1, 2, (N, 8, C)) * k[:, None, None]
        x[:, :, i, :, 0] = 1.125 * s
        x[:, :, i + 1, :, 0] = -1.25 * s
    for r in range(N):
        at_ = [0, C - 1, int(rng.integers(C)), int(rng.integers(C))]
        for g, j in zip(rng.permutation(8)[:4], at_): x[r, g, 0, j, 0] = 2.0 ** 30 * rng.choice([-1.0, 1.0])
    x[:, :, 8:] = rng.choice([-1.0, 1.0], (N, 8, 8, C, 4)) * (1 + 0.125 * rng.integers(0, 8, (N, 8, 8, C, 4))) * 2.0 ** -30
    x[z, :, :8] = 0
    x[:, :, 7, :, 0] = 2.0 ** -30
    x[:, :, 8, :, 3] = 2.0 ** -30
    u = scoring(d)
    w = layers(rng)
    w[:, :, :8] = 0
    w[:, :, :, :, :, :9] = 0
    for h in range(0, 128, 16):
        for i in (0, 1):
            u[:, h + 2 * i, h + i, 0] = (1.125 * k).astype(np.float32).astype(BF)
            u[:, h + 2 * i + 1, h + i, 0] = k.astype(np.float32).astype(BF)
            u[z, :, h + i] = 0
            u[z, h + 5 + i, h + i, 0] = 2.0 ** -30
            w[z, h // 16, 8, 0, h // 16, 5 + i, i] = 2.0 ** -8
    return {"x": x.astype(np.float32).reshape(N, 128, 4 * C).astype(BF), "u": u.reshape(N, 128, 512), "v": d["v"], **stored(*drawn(rng)), **weights(rng, w)}
def setup_inputs_odd(rng):
    d = numbers_of(rng)
    x = (2 * rng.integers(0, 8, (N, 16, 8, C, 4)) + 1) * 2.0 ** -8 * rng.choice([-1.0, 1.0], (N, 16, 8, C, 4))
    x[:, :, 0, :, 0] = 2.0 ** 8 * np.where(rng.random((N, 16, C)) < 0.5, 1.96875, 1.875)
    u = scoring(d)
    for i in (0, 1):
        x[:, ::2, 1 + 2 * i, :, 0] = (8 + rng.integers(0, 2, (N, 8, C))) * 2.0 ** -8
        x[:, ::2, 2 + 2 * i, :, 0] = 8 * 2.0 ** -8
        for h in range(0, 128, 16):
            u[:, h + 1 + 2 * i, h + i, 0] = 1
            u[:, h + 2 + 2 * i, h + i, 0] = -1
    return {"x": x.astype(np.float32).reshape(N, 128, 4 * C).astype(BF), "u": u.reshape(N, 128, 512), "v": d["v"], **stored(*drawn(rng)), **weights(rng, layers(rng, [0, 1, 2, 3, 4, 8]))}
def setup_inputs_ends(rng):
    d = numbers_of(rng)
    p, q, k = drawn(rng)
    o, e = rng.permutation(N) % 4, rng.permutation(N) % 4
    s = rng.choice([-1.0, 1.0], (N, 128, C, 4))
    s[o == 0] = -1
    s[o == 1] = rng.choice([-1.0, 1.0], (N, 1, C, 1))[o == 1]
    x = s * (0.87 + 0.07 * rng.random((N, 128, C, 4))) * 2.0 ** 30
    x[:, 15::16] = 0
    x[o == 3] = 2.0 ** -30
    size = np.where(o == 3, 2.0 ** -30, 2.0 ** 30)
    u = scoring(d)
    for i in (0, 1):
        a = np.stack([rng.permutation(8) % 2 * 2.0 - 1.0 for r in range(N)]) * size[:, None]
        u[:, :, i::16] = a.astype(np.float32).astype(BF)[:, None, :, None]
    v = rng.choice([-1.0, 1.0], (N, 128, 512)) * np.where(o % 2 == 1, 2.0 ** -30, 2.0 ** 30)[:, None, None]
    p[e == 0] = PLACES
    p[e == 1] = PLACES[::-1]
    q[e == 0] = np.where(np.arange(8) % 2 == 0, C - 1, 0)[:, None]
    q[e == 1] = (rng.integers(0, 2, (N, 8, C)) * (C - 1))[e == 1]
    q[e == 2] = PLACES
    q[e == 3] = rng.integers(0, C, (N, 8, C))[e == 3]
    k[e == 0] = PLACES
    k[e == 1] = PLACES[::-1]
    k[e == 2] = PLACES ^ 1
    w = np.zeros((N, 128, 4, 128, 4), np.float32)
    i = np.arange(128)
    for b in range(4): w[:, i, b, i, b] = np.where(o[:, None] == 3, np.where(i % 16 == 15, 2.0 ** 8, 2.0 ** -8), -0.25)
    return {"x": x.astype(np.float32).reshape(N, 128, 4 * C).astype(BF), "u": u.reshape(N, 128, 512), "v": v.astype(np.float32).astype(BF), **stored(p, q, k), **weights(rng, w.astype(BF))}
def setup_inputs_spread(rng):
    d = setup_inputs(rng)
    d["x"] = wide(rng, N, 128, 4 * C, cols=6)
    return d
def check_inputs(d):
    b = []
    for k in ("x", "u", "v"):
        a = np.abs(d[k].astype(np.float32))
        if not (np.isfinite(a).all() and ((a == 0) | (a >= 2.0 ** -30) & (a <= 2.0 ** 30)).all()): b.append("a value of " + k)
    for k in ("pp", "rf", "pr"):
        if not ((d[k] >= 0) & (d[k] < C)).all(): b.append("an entry of " + k)
    none, least, most = [emit(mx_ref.quantize(np.full((128, 16), k, np.float32).astype(BF)))[1][0, 0] for k in (0.0, 2.0 ** -8, 2.0 ** 8)]
    for r in range(N):
        if not (np.sort(gentries(d["pp"][r]), axis=1) == PLACES).all(): b.append("pp: a column not once in a group")
        k = gentries(d["pr"][r]).reshape(8, 3, C)
        if ((k >= 0) & (k < C)).all() and not (np.take_along_axis(k, k, axis=2) == PLACES).all(): b.append("pr: a place that isn't the pair of its pair")
        if ((d["wc"][r] == 0x7F) | (d["wc"][r] == 0xFF)).any(): b.append("wc: a code that is no number")
        s = mx_ref.live(d["ws"][r])
        if ((s != none) & ((s < least) | (s > most))).any(): b.append("ws: a scale out of range")
        if (((d["wc"][r].reshape(16, 8, 512, 4) & 0x7F) != 0) & (s == none)[:, None, :, None]).any(): b.append("wc: a code other than zero under the scale of zeros")
    return b
def at(a, e):
    return np.take_along_axis(a, e, axis=1)
def layer(w, q):
    return tile([mx_ref.matmul(pick(w, np.arange(128 * b, 128 * b + 128)), q) * np.float32(0.03125) for b in range(4)])
def reference(x, u, v, pp, rf, pr, wc, ws):
    qu = [mx_ref.quantize(u[r]) for r in range(N)]
    lay = [pk(wc[r], ws[r]) for r in range(N)]
    place, refs = [gentries(pp[r]) for r in range(N)], [gentries(rf[r]) for r in range(N)]
    pair = [gentries(pr[r]).reshape(8, 3, C) for r in range(N)]
    now = [x[r] for r in range(N)]
    for t, step in enumerate(STEP):
        held, mix = [], []
        for r in range(N):
            q = mx_ref.quantize(now[r])
            s = mx_ref.matmul(qu[r], q)
            sign, mode = s[::16] > 0, s[1::16] > 0
            held.append(decode(q))
            k, here = pair[r][:, t], at(sign, place[r])
            swap = np.where(here == at(here, k), k, PLACES)
            place[r] = at(place[r], swap)
            old = at(refs[r], swap)
            refs[r] = np.where(at(mode, place[r]), at(swap, old), (old + PLACES - swap) % C)
            g = held[r].astype(BF)
            z = gcols(g, place[r]).astype(np.float32) + gcols(g, at(place[r], refs[r])).astype(np.float32)
            mix.append(mx_ref.quantize((z * np.float32(0.5)).astype(BF)))
        for r in range(N):
            h = layer(lay[r], join(pick(mix[r], np.arange(H)), pick(mix[r ^ step], np.arange(H, C))))
            inverse = np.argsort(place[r], axis=1)
            now[r] = (held[r] + gcols(h, at(refs[r ^ step], at(refs[r], inverse))).astype(np.float32)).astype(BF)
    y, pf = np.zeros((N, 128, C), np.float32), np.zeros((N, 8, 2 * C), np.float32)
    oc, osc = np.zeros((N, 128, 4 * C), np.uint8), np.zeros((N, 16, C), np.uint8)
    for r in range(N):
        q = mx_ref.quantize(now[r])
        y[r] = mx_ref.matmul(mx_ref.quantize(v[r]), q)
        pf[r] = np.concatenate([place[r], refs[r]], axis=1)
        oc[r], osc[r] = emit(q)
    return {"y": y, "pf": pf, "oc": oc, "osc": osc}

@@ -1,0 +1,400 @@
+from concourse.mybir import dt, AluOpType as A, ActivationFunctionType as F
+
+C, H, STEP = 384, 192, [1, 2, 4]
+HOLD = 1408.0
+MID = 192.0
+BF, HF, FL, CODE = "bfloat16", "float16", "float32", "float8_e4m3fn_x4"
+
+SCRATCH = {"ps": ("psum", [128, 4096], "float32")}
+for _n, _c, _d in (
+        [("xin", 1536, BF), ("uin", 512, BF), ("vin", 512, BF), ("ppi", 24, "int32"), ("rfi", 24, "int32"), ("pri", 72, "int32")]
+        + [("wq", 512, CODE), ("wp", 512, "uint8"), ("uq", 128, CODE), ("up", 128, "uint8"), ("uuq", 256, CODE), ("uup", 256, "uint8")]
+        + [("vq", 128, CODE), ("vp", 128, "uint8"), ("eq", 512, CODE), ("ep", 512, "uint8"), ("zlq", H, CODE), ("zlp", H, "uint8")]
+        + [("one", 516, BF), ("eye", 516, BF), ("uoi", 16, "int32"), ("uo", 16, "uint16"), ("cm", C, BF), ("pid", 2, "int32")]
+        + [("pmi", 2, "int32"), ("pm", 2, FL), ("cp", 1, FL), ("q16", 24, "int32"), ("qw", 24, FL), ("num", C, FL), ("xd", C, BF)]
+        + [("d1", C, HF), ("d2", C, HF), ("d0", C, HF)]
+        + [(k, 1536, BF) for k in ("fb", "gb", "gc", "bb", "zt", "xt")]
+        + [(k, C, BF) for k in ("aw", "ar", "bw", "br", "pk", "fk", "ir", "ej", "hr", "b3")]
+        + [(k, C, HF) for k in ("er", "rr", "sc", "sc2", "sc3", "sc4", "sc5", "scb", "scp", "scf")]
+        + [(k, C, FL) for k in ("iv0", "tr", "prow", "frow", "fs", "ef", "yo")]
+        + [(k, 96, FL) for k in ("dcp", "bs", "mu", "sel")]
+        + [(k, 24, FL) for k in ("nf", "al", "alc", "mm", "ma", "mx")] + [("pkw", 48, FL), ("ni", 24, "int32")]
+        + [("ku", 72, "uint16"), ("tu", 72, "uint16")] + [(k, 24, "uint16") for k in ("p0", "f0", "iu", "eu", "hu", "pku")]
+        + [("xq%d" % t, C, CODE) for t in range(4)] + [("xp%d" % t, C, "uint8") for t in range(4)]
+        + [("%s%d" % (k, t), 96, FL) for k in ("dd", "ba") for t in range(3)]
+        + [("%s%d" % (k, t), 24, "uint16") for k in ("fu", "lf") for t in range(3)]
+        + [("%s%d" % (k, t), H, CODE) for k in ("zuq", "lq") for t in range(3)]
+        + [("%s%d" % (k, t), H, "uint8") for k in ("zup", "lp") for t in range(3)]):
+    SCRATCH[_n] = ("sbuf", [128, _c], _d)
+LOADS = ["x", "u", "v", "pp", "rf", "pr", "wc", "ws"]
+SEMAPHORES = ["qv", "qs", "qt", "qg", "sent", "out"] + ["ld_" + k for k in LOADS] + ["%s%d" % (k, t) for k in ("af", "aq", "ap") for t in range(3)]
+
+
+def rank_program(g, core, T, topo):
+    rank = T.rank_of(core)
+    if rank is None:
+        return
+    queue = {"v": g.vector, "s": g.scalar, "t": g.tensor, "g": g, "y": g.sync}
+    count, know, acc = {}, {k: {} for k in queue}, {}
+
+    def V(name, lo, hi, step=1):
+        return (name, lo, hi, T[name][:, lo:hi] if step == 1 else T[name][:, lo:hi:step])
+
+    def lane(name, b, lo, hi):
+        return ("%s%d" % (name, b), 4 * lo, 4 * hi, T[name][:, 4 * lo + b:4 * hi:4])
+
+    def row(name):
+        return V(name, 0, C)
+
+    def bits(v, d=dt.uint8):
+        return (v[0], v[1], v[2], v[3].bitcast(d))
+
+    def ind(win, off):
+        return ("*", win, off, win[3].indirect(off[3]))
+
+    def flat(vs):
+        r = []
+        for v in vs:
+            if v[0] in ("zt", "xt"):
+                r += [("%s%d" % (v[0], b), v[1], v[2], None) for b in range(4)]
+            else:
+                r += [v[1], v[2]] if v[0] == "*" else [v]
+        return [(n, a, b) if n != "ps" else (n, a // 512 * 512, -(-b // 512) * 512) for n, a, b, _ in r]
+
+    def uses(w, r):
+        return [(x, True) for x in w] + [(x, x[0] == "ps") for x in r]
+
+    def await_(q, recs):
+        for s, v, snap in recs:
+            if know[q].get(s, 0) >= v:
+                continue
+            if any(o[2].get(s, 0) >= v and (o[0], o[1]) != (s, v) and know[q].get(o[0], 0) < o[1] for o in recs):
+                continue
+            queue[q].wait_ge(T.sem[s], v)
+            know[q][s] = v
+        for s, v, snap in recs:
+            for k in snap:
+                know[q][k] = max(know[q].get(k, 0), snap[k])
+
+    def emit(q, fn, w, r, s=None, n=1):
+        w, r = flat(w), flat(r)
+        recs = {}
+        for (nm, a, b), wr in uses(w, r):
+            for e in acc.get(nm, []):
+                if e[0] < b and a < e[1] and (wr or e[2]):
+                    k = e[3][0]
+                    if k not in recs or recs[k][1] < e[3][1]:
+                        recs[k] = e[3]
+        await_(q, list(recs.values()))
+        s = s or "q" + q
+        fn().then_inc(T.sem[s], n)
+        count[s] = count.get(s, 0) + n
+        snap = dict(know[q])
+        snap[s] = count[s]
+        for (nm, a, b), wr in uses(w, r):
+            l = acc.setdefault(nm, [])
+            if wr:
+                l[:] = [e for e in l if not (a <= e[0] and e[1] <= b)]
+            l.append((a, b, wr, (s, count[s], snap)))
+
+    def copy(out, in_):
+        emit("v", lambda: g.vector.tensor_copy(out[3], in_[3]), [out], [in_])
+
+    def tt(out, a, b, op):
+        emit("v", lambda: g.vector.tensor_tensor(out[3], a[3], b[3], op), [out], [a, b])
+
+    def ts(out, a, s1, op0, s2=None, op1=None):
+        x1 = s1[3] if isinstance(s1, tuple) else s1
+        r = [a] + ([s1] if isinstance(s1, tuple) else [])
+        if op1 is None:
+            emit("v", lambda: g.vector.tensor_scalar(out[3], a[3], x1, None, op0), [out], r)
+        else:
+            emit("v", lambda: g.vector.tensor_scalar(out[3], a[3], x1, s2, op0, op1), [out], r)
+
+    def act(out, in_, func=F.Identity, bias=0.0, scale=1.0):
+        emit("s", lambda: g.scalar.activation(out[3], in_[3], func, bias=bias, scale=scale), [out], [in_])
+
+    def quant(c, p, in_):
+        emit("v", lambda: g.vector.quantize_mx(c[3], p[3], in_[3]), [c, p], [in_])
+
+    def mm(bank, w, wp, x, xp, n):
+        o = V("ps", 512 * bank, 512 * bank + n)
+        emit("t", lambda: g.tensor.matmul_mx(o[3], w[3], wp[3], x[3], xp[3], True, True), [o], [w, wp, x, xp])
+
+    def load(q, name, out, ap):
+        emit(q, lambda: queue[q].dma_start(out[3], ap), [out], [], "ld_" + name, 16)
+
+    def store(ap, in_, q="y"):
+        emit(q, lambda: queue[q].dma_start(ap, in_[3]), [], [in_], "out", 16)
+
+    def iota(out, pattern, cmul, flag=False):
+        emit("g", lambda: g.iota(out[3], pattern, 0, cmul, allow_small_or_imprecise_dtypes=flag), [out], [])
+
+    def scan(out, r):
+        emit("v", lambda: g.vector.tensor_tensor_scan(out[3], row("d0")[3], r[3], 0.0, A.add, A.max), [out], [row("d0"), r])
+
+    def held(name):
+        return V(name, 15, C, 16)
+
+    CP, PM, NUM, QW = V("cp", 0, 1), V("pm", 0, 1), row("num"), V("qw", 0, 24)
+
+    load("s", "pp", V("ppi", 0, 24), T.pp[:])
+    load("y", "u", V("uin", 0, 512), T.u[:])
+    load("s", "pr", V("pri", 0, 72), T.pr[:])
+    load("s", "rf", V("rfi", 0, 24), T.rf[:])
+    load("y", "x", V("xin", 0, 1536), T.x[:])
+    load("y", "wc", bits(V("wq", 0, 512)), T.wc[:])
+    load("y", "ws", V("wp", 0, 512), T.ws[:])
+    load("y", "v", V("vin", 0, 512), T.v[:])
+    ONE, EYE = V("one", 0, 516), V("eye", 0, 516)
+    emit("v", lambda: g.vector.memset(ONE[3], 1.0), [ONE], [])
+    iota(V("pid", 0, 2), [[0, 2]], 1)
+    iota(V("uoi", 0, 16), [[1, 2], [16, 8]], 0)
+    iota(row("cm"), [[0, 24], [1, 16]], 0, True)
+    iota(NUM, [[1, C]], 0, True)
+    emit("g", lambda: g.affine_select(EYE[3], ONE[3], [[-1, 516]], A.is_equal, 0.0, 3, 4), [EYE], [ONE])
+    iota(V("q16", 0, 24), [[16, 24]], 0)
+    ts(V("pmi", 0, 2), V("pid", 0, 2), 15, A.bitwise_and)
+    copy(V("uo", 0, 16), V("uoi", 0, 16))
+    copy(V("pm", 0, 2), V("pmi", 0, 2))
+    ts(CP, PM, 15.0, A.is_lt, HOLD, A.mult)
+    ts(row("xd"), row("cm"), PM, A.subtract)
+    P, FU, INV, PKU = V("p0", 0, 24), V("f0", 0, 24), V("iu", 0, 24), V("pku", 0, 24)
+    ts(row("d1"), row("xd"), 0.0, A.is_equal, -30000.0, A.mult)
+    ts(row("d2"), row("xd"), 1.0, A.is_equal, HOLD, A.mult)
+    copy(P, V("ppi", 0, 24))
+    copy(V("ku", 0, 72), V("pri", 0, 72))
+    copy(FU, V("rfi", 0, 24))
+    iv = ind(row("iv0"), P)
+    emit("v", lambda: g.vector.tensor_copy(iv[3], NUM[3]), [row("iv0")], [NUM, P])
+    quant(V("uq", 0, 128), V("up", 0, 128), V("uin", 0, 512))
+    UO = V("uo", 0, 16)
+
+    def candidates(t, P, FU, part):
+        K = V("ku", 24 * t, 24 * t + 24)
+        if part == 0:
+            act(row("prow"), ind(NUM, P))
+        if part == 1:
+            act(row("pk"), ind(row("prow"), K), bias=-MID)
+
+    def differences(t):
+        D, B = "dd%d" % t, "ba%d" % t
+        if t:
+            scan(row("scp"), row("pk"))
+            ts(PKU, held("scp"), CP, A.subtract, MID, A.add)
+        scan(row("scf"), row("fk"))
+        ts(V("pkw", 0, 24), held("scp"), CP, A.subtract, MID, A.add)
+        ts(V("pkw", 24, 48), held("scf"), CP, A.subtract, MID, A.add)
+        tt(V(D, 24, 72), V("pkw", 0, 48), V(B, 24, 72), A.subtract)
+        ts(V(B, 72, 96), V(B, 48, 72), 0.0, A.add)
+        tt(V(D, 72, 96), V(D, 48, 72), V(D, 0, 24), A.subtract)
+        ts(V("dcp", 0, 96), V(D, 0, 96), CP, A.mult)
+        tt(V("bs", 0, 96), V(B, 0, 96), V("dcp", 0, 96), A.subtract)
+
+    candidates(0, P, FU, 0)
+    copy(bits(V("uuq", 0, 256), dt.uint32), ind(bits(V("uq", 0, 128), dt.uint32), UO))
+    uup, upw = V("uup", 0, 256), ind(V("up", 0, 128), UO)
+    emit("s", lambda: g.scalar.activation(uup[3], upw[3], F.Copy), [uup], [upw])
+    candidates(0, P, FU, 1)
+    act(row("frow"), ind(NUM, FU))
+    quant(V("xq0", 0, C), V("xp0", 0, C), V("xin", 0, 1536))
+    tt(row("d0"), row("d1"), row("d2"), A.add)
+    ts(QW, V("q16", 0, 24), PM, A.add)
+    scan(row("scp"), row("pk"))
+    for b in range(4):
+        quant(V("eq", 128 * b, 128 * b + 128), V("ep", 128 * b, 128 * b + 128), V("eye", 3 - b, 515 - b))
+    copy(V("ba0", 24, 48), V("ppi", 0, 24))
+    copy(V("ba0", 48, 72), V("rfi", 0, 24))
+
+    def own(t):
+        copy(V("ba%d" % t, 0, 24), QW)
+        tt(V("dd%d" % t, 0, 24), V("pri", 24 * t, 24 * t + 24), QW, A.subtract)
+
+    for t in range(3):
+        last = t == 2
+        other = T.cores[rank ^ STEP[t]]
+        eng = topo.engines(core, other)
+        mask = sum(1 << e for e in eng)
+        rid, pnc = topo.addr(other)[:2]
+        X, XP = V("xq%d" % t, 0, C), V("xp%d" % t, 0, C)
+
+        def send(dst, src, s, made):
+            recs = [e[3] for nm, a, b in flat([made]) for e in acc[nm] if e[2] and e[0] < b and a < e[1]]
+            await_("g", recs)
+            g.remote_dma(dst[3], src[3], T.sem[s], T.sem.sent, pnc, rid, mask)
+            count["sent"] = count.get("sent", 0) + len(eng)
+            count[s] = len(eng)
+            acc.setdefault(dst[0], []).append((dst[1], dst[2], True, (s, len(eng), {s: len(eng)})))
+
+        mm(4, V("uuq", 0, 128), V("uup", 0, 128), X, XP, C)
+        mm(5, V("uuq", 128, 256), V("uup", 128, 256), X, XP, C)
+        for b in range(4):
+            mm(b, V("eq", 128 * b, 128 * b + 128), V("ep", 128 * b, 128 * b + 128), X, XP, C)
+        if t:
+            differences(t)
+        else:
+            ts(PKU, held("scp"), CP, A.subtract, MID, A.add)
+            own(0)
+        act(row("aw"), V("ps", 2048, 2048 + C), F.Sign, bias=-2.0 ** -93)
+        pu, ku = V(P[0], P[1], P[1] + 12), V("pku", 0, 12)
+        pv, kv = V(P[0], P[1] + 12, P[2]), V("pku", 12, 24)
+        act(V("ar", 0, H), ind(row("aw"), pu), F.Copy)
+        act(V("ar", H, C), ind(row("aw"), pv), F.Copy)
+        tt(V("er", 0, H), ind(row("aw"), ku), V("ar", 0, H), A.is_equal)
+        tt(V("er", H, C), ind(row("aw"), kv), V("ar", H, C), A.is_equal)
+        if t == 0:
+            act(row("fk"), ind(row("frow"), V("ku", 0, 24)), bias=-MID)
+            differences(0)
+        act(row("bw"), V("ps", 2560, 2560 + C), F.Sign)
+        for b in range(2):
+            act(V("fb", C * b, C * b + C), V("ps", 512 * b, 512 * b + C), F.Copy)
+        scan(row("sc"), row("er"))
+        for i in range(4):
+            tt(V("mu", 24 * i, 24 * i + 24), held("sc"), V("dd%d" % t, 24 * i, 24 * i + 24), A.mult)
+        tt(V("sel", 0, 72), V("mu", 0, 72), V("bs", 0, 72), A.add)
+        tt(V("sel", 72, 96), V("mu", 72, 96), V("bs", 72, 96), A.add)
+        copy(V("tu", 0, 72), V("sel", 0, 72))
+        TU, P, CU = V("tu", 0, 24), V("tu", 24, 48), V("tu", 48, 72)
+        act(row("br"), ind(row("bw"), P), F.Relu)
+        for b in (2, 3):
+            act(V("fb", C * b, C * b + C), V("ps", 512 * b, 512 * b + C), F.Copy)
+        for b in range(3):
+            act(V("gb", C * b, C * b + C), ind(V("fb", C * b, C * b + C), P), F.Copy, scale=0.5)
+        act(V("gb", 3 * C + H, 4 * C), ind(V("fb", 3 * C, 4 * C), V("tu", 36, 48)), F.Copy, scale=0.5)
+        ts(V("ni", 0, 24), V("sel", 72, 96), -191.5, A.add, 1.0 / C, A.mult)
+        copy(row("tr"), ind(NUM, TU))
+        ts(V("nf", 0, 24), V("ni", 0, 24), -float(C), A.mult)
+        tt(row("rr"), ind(row("tr"), CU), row("br"), A.mult)
+        tt(V("al", 0, 24), V("sel", 72, 96), V("nf", 0, 24), A.add)
+        scan(row("scb"), row("br"))
+        ts(V("alc", 0, 24), V("al", 0, 24), CP, A.add)
+        ts(V("mm", 0, 24), held("scb"), CP, A.subtract, 0.5, A.is_lt)
+        scan(row("sc2"), row("rr"))
+        tt(V("ma", 0, 24), V("mm", 0, 24), V("alc", 0, 24), A.mult)
+        if not last:
+            copy(V("ba%d" % (t + 1), 24, 48), V("sel", 24, 48))
+        tt(V("mx", 0, 24), V("ma", 0, 24), held("sc2"), A.max)
+        FU = V("fu%d" % t, 0, 24)
+        ts(FU, V("mx", 0, 24), CP, A.subtract)
+        if t == 0:
+            scan(row("sc3"), row("iv0"))
+            ts(INV, held("sc3"), CP, A.subtract)
+            own(1)
+            own(2)
+        send(V("lf%d" % t, 0, 24), FU, "af%d" % t, FU)
+
+        def twin(b, h):
+            copy(V("gc", C * b + H * h, C * b + H * h + H), V("gb", C * b + H * h, C * b + H * h + H))
+
+        def mix(b, h):
+            o = lane("zt", b, H * h, H * h + H)
+            tt(o, ind(V("gb", C * b, C * b + C), V(FU[0], 12 * h, 12 * h + 12)), V("gc", C * b + H * h, C * b + H * h + H), A.add)
+        ts(V("gb", 3 * C, 3 * C + H), ind(V("fb", 3 * C, 4 * C), V("tu", 24, 36)), 0.5, A.mult)
+        twin(0, 1)
+        twin(1, 1)
+        mix(0, 1)
+        mix(1, 1)
+        twin(2, 1)
+        mix(2, 1)
+        twin(3, 1)
+        mix(3, 1)
+        UQ, UP = V("zuq%d" % t, 0, H), V("zup%d" % t, 0, H)
+        quant(UQ, UP, V("zt", 768, 1536))
+        send(bits(V("lq%d" % t, 0, H)), bits(UQ), "aq%d" % t, UQ)
+        send(V("lp%d" % t, 0, H), UP, "ap%d" % t, UP)
+        act(row("ir"), ind(row("tr"), INV), bias=-MID)
+        scan(row("sc3"), row("ir"))
+        twin(0, 0)
+        ts(INV, held("sc3"), CP, A.subtract, MID, A.add)
+        if t == 0:
+            act(row("prow"), ind(NUM, P))
+            act(row("frow"), ind(NUM, FU))
+            act(row("hr"), ind(row("frow"), INV), bias=-MID)
+            candidates(1, P, FU, 1)
+            act(row("fs"), ind(NUM, V("lf0", 0, 24)))
+        else:
+            act(row("prow"), ind(NUM, P))
+            act(row("fs"), ind(NUM, V("lf%d" % t, 0, 24)))
+            act(row("ef"), ind(row("fs"), FU))
+            act(row("ej"), ind(row("ef"), INV), bias=-MID)
+            if not last:
+                candidates(t + 1, P, FU, 1)
+            else:
+                act(row("frow"), ind(NUM, FU))
+        for b in (1, 2, 3):
+            twin(b, 0)
+        for b in range(4):
+            mix(b, 0)
+            if t == 0 and b == 1:
+                scan(row("sc5"), row("hr"))
+                ts(V("hu", 0, 24), held("sc5"), CP, A.subtract, MID, A.add)
+                act(row("ej"), ind(row("fs"), V("hu", 0, 24)), bias=-MID)
+        quant(V("zlq", 0, H), V("zlp", 0, H), V("zt", 0, 768))
+        low, up = (0, 1, 2, 5), (4, 6, 7, 0)
+
+        def layer(b, h):
+            x = (V("lq%d" % t, 0, H), V("lp%d" % t, 0, H)) if h else (V("zlq", 0, H), V("zlp", 0, H))
+            mm((low, up)[h][b], V("wq", 128 * b, 128 * b + 128), V("wp", 128 * b, 128 * b + 128), x[0], x[1], H)
+
+        def cast(b, h):
+            o, i = V("bb", C * b + H * h, C * b + H * h + H), 512 * (low, up)[h][b]
+            if b == 0:
+                ts(o, V("ps", i, i + H), 0.03125, A.mult)
+            else:
+                act(o, V("ps", i, i + H), F.Copy, scale=0.03125)
+        layer(0, 0)
+        layer(1, 0)
+        layer(0, 1)
+        layer(1, 1)
+        if t:
+            scan(row("sc4"), row("ej"))
+        cast(0, 0)
+        cast(1, 0)
+        if not t:
+            scan(row("sc4"), row("ej"))
+        ts(V("eu", 0, 24), held("sc4"), CP, A.subtract, MID, A.add)
+        if not last:
+            ts(V("ba%d" % (t + 1), 48, 72), V("mx", 0, 24), CP, A.subtract)
+        cast(0, 1)
+        cast(1, 1)
+        for b in (2, 3):
+            for h in (0, 1):
+                layer(b, h)
+                cast(b, h)
+
+        def state(b, h=None):
+            lo, hi = (0, C) if h is None else (H * h, H * h + H)
+            tt(lane("xt", b, lo, hi), ind(V("bb", C * b, C * b + C), V("eu", lo // 16, hi // 16)), V("fb", C * b + lo, C * b + hi), A.add)
+        if not last:
+            act(row("b3"), ind(V("bb", 3 * C, 4 * C), V("eu", 0, 24)), F.Copy)
+            for b in range(3):
+                state(b)
+            tt(lane("xt", 3, 0, C), row("b3"), V("ps", 1536, 1536 + C), A.add)
+            if t:
+                act(row("frow"), ind(NUM, FU))
+            act(row("fk"), ind(row("frow"), V("ku", 24 * t + 24, 24 * t + 48)), bias=-MID)
+            quant(V("xq%d" % (t + 1), 0, C), V("xp%d" % (t + 1), 0, C), V("xt", 0, 1536))
+    store(T.pf[:, 0:C], ("prow", 0, C, T.prow[0:128:16, :]))
+    store(T.pf[:, C:2 * C], ("frow", 0, C, T.frow[0:128:16, :]))
+    quant(V("vq", 0, 128), V("vp", 0, 128), V("vin", 0, 512))
+    for b, h in ((0, 0), (0, 1), (1, 0), (1, 1), (2, 0), (3, 0)):
+        state(b, h)
+
+    def finish(h):
+        X, XP = V("xq3", H * h, H * h + H), V("xp3", H * h, H * h + H)
+        quant(X, XP, V("xt", 768 * h, 768 * h + 768))
+        mm(4 + h, V("vq", 0, 128), V("vp", 0, 128), X, XP, H)
+        store(T.oc[:, 768 * h:768 * h + 768], bits(X))
+    finish(0)
+    act(V("yo", 0, H), V("ps", 2048, 2048 + H), F.Copy)
+    store(T.y[:, 0:H], V("yo", 0, H), "s")
+    state(2, 1)
+    state(3, 1)
+    finish(1)
+    for k in range(4):
+        store(T.osc[4 * k:4 * k + 4, :], ("xp3", 0, C, T.xp3[32 * k:32 * k + 4, :]), "y" if k % 2 else "s")
+    ts(V("yo", H, C), V("ps", 2560, 2560 + H), 1.0, A.mult)
+    store(T.y[:, H:C], V("yo", H, C))
+    for s in count:
+        if know["g"].get(s, 0) < count[s]:
+            g.wait_ge(T.sem[s], count[s])

@@ -1,33 +1,37 @@
 from concourse.mybir import dt, AluOpType as A, ActivationFunctionType as F
 
 C, H, STEP = 384, 192, [1, 2, 4]
-HOLD = 1408.0
 MID = 192.0
-BF, HF, FL, CODE = "bfloat16", "float16", "float32", "float8_e4m3fn_x4"
+BF, FL, U16, I32, CODE = "bfloat16", "float32", "uint16", "int32", "float8_e4m3fn_x4"
+T2 = 384
+R_E, R_N, R_P, R_F = 6, 8, 10, 12
+NBS = (2, 3, 3)
+LAST = 192
+L_AN, L_AW, L_D, L_I, L_B = 0, 4, 8, 14, 18
 
 SCRATCH = {"ps": ("psum", [128, 4096], "float32")}
 for _n, _c, _d in (
-        [("xin", 1536, BF), ("uin", 512, BF), ("vin", 512, BF), ("ppi", 24, "int32"), ("rfi", 24, "int32"), ("pri", 72, "int32")]
-        + [("wq", 512, CODE), ("wp", 512, "uint8"), ("uq", 128, CODE), ("up", 128, "uint8"), ("uuq", 256, CODE), ("uup", 256, "uint8")]
-        + [("vq", 128, CODE), ("vp", 128, "uint8"), ("eq", 512, CODE), ("ep", 512, "uint8"), ("zlq", H, CODE), ("zlp", H, "uint8")]
-        + [("one", 516, BF), ("eye", 516, BF), ("uoi", 16, "int32"), ("uo", 16, "uint16"), ("cm", C, BF), ("pid", 2, "int32")]
-        + [("pmi", 2, "int32"), ("pm", 2, FL), ("cp", 1, FL), ("q16", 24, "int32"), ("qw", 24, FL), ("num", C, FL), ("xd", C, BF)]
-        + [("d1", C, HF), ("d2", C, HF), ("d0", C, HF)]
-        + [(k, 1536, BF) for k in ("fb", "gb", "gc", "bb", "zt", "xt")]
-        + [(k, C, BF) for k in ("aw", "ar", "bw", "br", "pk", "fk", "ir", "ej", "hr", "b3")]
-        + [(k, C, HF) for k in ("er", "rr", "sc", "sc2", "sc3", "sc4", "sc5", "scb", "scp", "scf")]
-        + [(k, C, FL) for k in ("iv0", "tr", "prow", "frow", "fs", "ef", "yo")]
-        + [(k, 96, FL) for k in ("dcp", "bs", "mu", "sel")]
-        + [(k, 24, FL) for k in ("nf", "al", "alc", "mm", "ma", "mx")] + [("pkw", 48, FL), ("ni", 24, "int32")]
-        + [("ku", 72, "uint16"), ("tu", 72, "uint16")] + [(k, 24, "uint16") for k in ("p0", "f0", "iu", "eu", "hu", "pku")]
+        [("xin", 1536, BF), ("uin", 512, BF), ("vin", 512, BF), ("ppi", 24, I32), ("rfi", 24, I32), ("pri", 72, I32)]
+        + [("wq", 512, CODE), ("wp", 512, "uint8"), ("uq", 128, CODE), ("up", 128, "uint8"), ("uuq", 128, CODE), ("uup", 128, "uint8")]
+        + [("vq", 128, CODE), ("vp", 128, "uint8"), ("eq", 512, CODE), ("ep", 512, "uint8")]
+        + [("one", 516, BF), ("eye", 516, BF), ("uoi", 8, I32), ("uo", 8, U16), ("pid", 2, I32), ("pmi", 2, I32), ("p32", 2, I32)]
+        + [("phi", 2, I32), ("col", 8, FL), ("jj", 24, I32), ("jf", 24, FL), ("ge", 24, FL), ("cc", 24, FL), ("ci", 24, I32)]
+        + [("cx", 24, FL), ("cr", 24, FL), ("cl", 24, U16), ("qn", 24, I32), ("qw", 24, I32), ("nm", C, BF)]
+        + [(k, 1536, BF) for k in ("fh", "fb", "gb", "bb", "bg", "zt", "xt")]
+        + [(k, C, BF) for k in ("sg", "rs", "a2", "ef", "eg", "x1")]
+        + [("uu", 768, BF), ("wd", 768, BF), ("rr", 816, BF), ("ta", 800, BF), ("tb", 800, BF)]
+        + [("s0", 384, FL), ("s1", 384, FL), ("so", 96, FL), ("sb", 144, FL), ("w2", 32, FL)]
+        + [("ni", 24, I32), ("nx", 24, FL), ("po", 48, FL), ("yo", C, FL)]
+        + [("ku", 72, U16), ("p0", 48, U16), ("c2", 24, U16), ("iv", 32, U16), ("eu", 32, U16)]
         + [("xq%d" % t, C, CODE) for t in range(4)] + [("xp%d" % t, C, "uint8") for t in range(4)]
-        + [("%s%d" % (k, t), 96, FL) for k in ("dd", "ba") for t in range(3)]
-        + [("%s%d" % (k, t), 24, "uint16") for k in ("fu", "lf") for t in range(3)]
-        + [("%s%d" % (k, t), H, CODE) for k in ("zuq", "lq") for t in range(3)]
-        + [("%s%d" % (k, t), H, "uint8") for k in ("zup", "lp") for t in range(3)]):
+        + [("%s%d" % (k, t), 48, U16) for k in ("tp", "fp", "pk") for t in range(3)]
+        + [("%s%d" % (k, t), 24, BF) for k in ("fw", "lf") for t in range(3)]
+        + [("zq%d" % t, H, CODE) for t in range(3)] + [("yq%d" % t, C, CODE) for t in range(3)]
+        + [("zp%d" % t, H, "uint8") for t in range(3)] + [("yp%d" % t, C, "uint8") for t in range(3)]):
     SCRATCH[_n] = ("sbuf", [128, _c], _d)
 LOADS = ["x", "u", "v", "pp", "rf", "pr", "wc", "ws"]
-SEMAPHORES = ["qv", "qs", "qt", "qg", "sent", "out"] + ["ld_" + k for k in LOADS] + ["%s%d" % (k, t) for k in ("af", "aq", "ap") for t in range(3)]
+SEMAPHORES = (["qv", "qs", "qt", "qg", "sent", "out", "dx", "pa", "pb"] + ["ld_" + k for k in LOADS]
+              + ["%s%d" % (k, t) for k in ("af", "aq", "ap", "dc0", "dc1", "da0", "da1") for t in range(3)])
 
 
 def rank_program(g, core, T, topo):
@@ -38,31 +42,23 @@ def rank_program(g, core, T, topo):
     count, know, acc = {}, {k: {} for k in queue}, {}
 
     def V(name, lo, hi, step=1):
-        return (name, lo, hi, T[name][:, lo:hi] if step == 1 else T[name][:, lo:hi:step])
+        if name == "ps":
+            cols = range(lo // 512, -(-hi // 512))
+        else:
+            cols = range(lo, hi, step)
+        return ([(name, sum(1 << c for c in cols))], T[name][:, lo:hi] if step == 1 else T[name][:, lo:hi:step])
 
     def lane(name, b, lo, hi):
-        return ("%s%d" % (name, b), 4 * lo, 4 * hi, T[name][:, 4 * lo + b:4 * hi:4])
+        return V(name, 4 * lo + b, 4 * hi, 4)
 
     def row(name):
         return V(name, 0, C)
 
     def bits(v, d=dt.uint8):
-        return (v[0], v[1], v[2], v[3].bitcast(d))
+        return (v[0], v[1].bitcast(d))
 
     def ind(win, off):
-        return ("*", win, off, win[3].indirect(off[3]))
-
-    def flat(vs):
-        r = []
-        for v in vs:
-            if v[0] in ("zt", "xt"):
-                r += [("%s%d" % (v[0], b), v[1], v[2], None) for b in range(4)]
-            else:
-                r += [v[1], v[2]] if v[0] == "*" else [v]
-        return [(n, a, b) if n != "ps" else (n, a // 512 * 512, -(-b // 512) * 512) for n, a, b, _ in r]
-
-    def uses(w, r):
-        return [(x, True) for x in w] + [(x, x[0] == "ps") for x in r]
+        return (win[0] + off[0], win[1].indirect(off[1]))
 
     def await_(q, recs):
         for s, v, snap in recs:
@@ -77,324 +73,407 @@ def rank_program(g, core, T, topo):
                 know[q][k] = max(know[q].get(k, 0), snap[k])
 
     def emit(q, fn, w, r, s=None, n=1):
-        w, r = flat(w), flat(r)
+        use = [(x, True) for v in w for x in v[0]] + [(x, x[0] == "ps") for v in r for x in v[0]]
         recs = {}
-        for (nm, a, b), wr in uses(w, r):
+        for (nm, m), wr in use:
             for e in acc.get(nm, []):
-                if e[0] < b and a < e[1] and (wr or e[2]):
-                    k = e[3][0]
-                    if k not in recs or recs[k][1] < e[3][1]:
-                        recs[k] = e[3]
+                if e[0] & m and (wr or e[1]):
+                    k = e[2][0]
+                    if k not in recs or recs[k][1] < e[2][1]:
+                        recs[k] = e[2]
         await_(q, list(recs.values()))
         s = s or "q" + q
         fn().then_inc(T.sem[s], n)
         count[s] = count.get(s, 0) + n
         snap = dict(know[q])
         snap[s] = count[s]
-        for (nm, a, b), wr in uses(w, r):
+        for (nm, m), wr in use:
             l = acc.setdefault(nm, [])
             if wr:
-                l[:] = [e for e in l if not (a <= e[0] and e[1] <= b)]
-            l.append((a, b, wr, (s, count[s], snap)))
+                l[:] = [e for e in l if e[0] & ~m]
+            l.append((m, wr, (s, count[s], snap)))
 
     def copy(out, in_):
-        emit("v", lambda: g.vector.tensor_copy(out[3], in_[3]), [out], [in_])
+        emit("v", lambda: g.vector.tensor_copy(out[1], in_[1]), [out], [in_])
+
+    def fill(out, x):
+        emit("v", lambda: g.vector.memset(out[1], x), [out], [])
 
     def tt(out, a, b, op):
-        emit("v", lambda: g.vector.tensor_tensor(out[3], a[3], b[3], op), [out], [a, b])
+        emit("v", lambda: g.vector.tensor_tensor(out[1], a[1], b[1], op), [out], [a, b])
 
     def ts(out, a, s1, op0, s2=None, op1=None):
-        x1 = s1[3] if isinstance(s1, tuple) else s1
-        r = [a] + ([s1] if isinstance(s1, tuple) else [])
+        r = [a] + [x for x in (s1, s2) if isinstance(x, tuple)]
+        x1, x2 = [x[1] if isinstance(x, tuple) else x for x in (s1, s2)]
         if op1 is None:
-            emit("v", lambda: g.vector.tensor_scalar(out[3], a[3], x1, None, op0), [out], r)
+            emit("v", lambda: g.vector.tensor_scalar(out[1], a[1], x1, None, op0), [out], r)
         else:
-            emit("v", lambda: g.vector.tensor_scalar(out[3], a[3], x1, s2, op0, op1), [out], r)
+            emit("v", lambda: g.vector.tensor_scalar(out[1], a[1], x1, x2, op0, op1), [out], r)
 
-    def act(out, in_, func=F.Identity, bias=0.0, scale=1.0):
-        emit("s", lambda: g.scalar.activation(out[3], in_[3], func, bias=bias, scale=scale), [out], [in_])
+    def act(out, in_, func=F.Copy, **kw):
+        r = [in_] + [x for x in kw.values() if isinstance(x, tuple)]
+        kw = {k: x[1] if isinstance(x, tuple) else x for k, x in kw.items()}
+        emit("s", lambda: g.scalar.activation(out[1], in_[1], func, **kw), [out], r)
 
     def quant(c, p, in_):
-        emit("v", lambda: g.vector.quantize_mx(c[3], p[3], in_[3]), [c, p], [in_])
+        emit("v", lambda: g.vector.quantize_mx(c[1], p[1], in_[1]), [c, p], [in_])
 
     def mm(bank, w, wp, x, xp, n):
         o = V("ps", 512 * bank, 512 * bank + n)
-        emit("t", lambda: g.tensor.matmul_mx(o[3], w[3], wp[3], x[3], xp[3], True, True), [o], [w, wp, x, xp])
+        emit("t", lambda: g.tensor.matmul_mx(o[1], w[1], wp[1], x[1], xp[1], True, True), [o], [w, wp, x, xp])
 
     def load(q, name, out, ap):
-        emit(q, lambda: queue[q].dma_start(out[3], ap), [out], [], "ld_" + name, 16)
+        emit(q, lambda: queue[q].dma_start(out[1], ap), [out], [], "ld_" + name, 16)
 
     def store(ap, in_, q="y"):
-        emit(q, lambda: queue[q].dma_start(ap, in_[3]), [], [in_], "out", 16)
+        emit(q, lambda: queue[q].dma_start(ap, in_[1]), [], [in_], "out", 16)
 
-    def iota(out, pattern, cmul, flag=False):
-        emit("g", lambda: g.iota(out[3], pattern, 0, cmul, allow_small_or_imprecise_dtypes=flag), [out], [])
+    def iota(out, pattern, base, cmul, flag=False):
+        emit("g", lambda: g.iota(out[1], pattern, base, cmul, allow_small_or_imprecise_dtypes=flag), [out], [])
 
-    def scan(out, r):
-        emit("v", lambda: g.vector.tensor_tensor_scan(out[3], row("d0")[3], r[3], 0.0, A.add, A.max), [out], [row("d0"), r])
+    def turn(out, in_):
+        emit("v", lambda: g.vector.transpose(out[1], in_[1]), [out], [in_])
 
-    def held(name):
-        return V(name, 15, C, 16)
+    def scan(out, lo, hi):
+        a, b = V("s0", lo, hi), V("s1", lo, hi)
+        emit("v", lambda: g.vector.tensor_tensor_scan(out[1], a[1], b[1], 0.0, A.mult, A.add), [out], [a, b])
 
-    CP, PM, NUM, QW = V("cp", 0, 1), V("pm", 0, 1), row("num"), V("qw", 0, 24)
+    def bank(b, lo=0, hi=C):
+        return V("ps", 512 * b + lo, 512 * b + hi)
+
+    RA, RB = 16, 416
+
+    def turn2(to, r):
+        turn(V(to, 0, C), V("rr", r, r + C))
+        turn(V(to, T2, T2 + 416), V("rr", r - 16, r + 400))
+
+    def pick(tile, lo, n, wide=800):
+        return ind(V(tile, 0, wide), V("cl", lo, lo + n))
+
+    def ur(r):
+        return V("uu", C + r, 2 * C, 16)
+
+    def ul(r):
+        return V("uu", r, C, 16)
+
+    PM, MC, BC, P32, PH, UX = [V("col", k, k + 1) for k in range(6)]
+    B0 = 192
 
     load("s", "pp", V("ppi", 0, 24), T.pp[:])
-    load("y", "u", V("uin", 0, 512), T.u[:])
+    load("y", "rf", V("rfi", 0, 24), T.rf[:])
     load("s", "pr", V("pri", 0, 72), T.pr[:])
-    load("s", "rf", V("rfi", 0, 24), T.rf[:])
-    load("y", "x", V("xin", 0, 1536), T.x[:])
+    load("y", "u", V("uin", 0, 512), T.u[:])
+    load("s", "x", V("xin", 0, 1536), T.x[:])
     load("y", "wc", bits(V("wq", 0, 512)), T.wc[:])
     load("y", "ws", V("wp", 0, 512), T.ws[:])
     load("y", "v", V("vin", 0, 512), T.v[:])
-    ONE, EYE = V("one", 0, 516), V("eye", 0, 516)
-    emit("v", lambda: g.vector.memset(ONE[3], 1.0), [ONE], [])
-    iota(V("pid", 0, 2), [[0, 2]], 1)
-    iota(V("uoi", 0, 16), [[1, 2], [16, 8]], 0)
-    iota(row("cm"), [[0, 24], [1, 16]], 0, True)
-    iota(NUM, [[1, C]], 0, True)
-    emit("g", lambda: g.affine_select(EYE[3], ONE[3], [[-1, 516]], A.is_equal, 0.0, 3, 4), [EYE], [ONE])
-    iota(V("q16", 0, 24), [[16, 24]], 0)
+    ONE, EYE, NM = V("one", 0, 516), V("eye", 0, 516), row("nm")
+    iota(V("pid", 0, 2), [[0, 2]], 0, 1)
+    iota(V("jj", 0, 8), [[0, 2], [16, 4]], 0, 0)
+    iota(V("jj", 8, 17), [[0, 3], [16, 3]], 0, 0)
+    iota(V("jj", 17, 23), [[16, 6]], -16, 0)
+    iota(NM, [[1, C]], -int(MID), 0, True)
+    iota(V("uoi", 0, 8), [[16, 8]], 0, 0)
+    iota(V("qw", 0, 24), [[32, 12], [0, 2]], -int(MID), 0)
+    iota(V("qn", 0, 24), [[16, 24]], -int(MID), 0)
+    fill(ONE, 1.0)
     ts(V("pmi", 0, 2), V("pid", 0, 2), 15, A.bitwise_and)
-    copy(V("uo", 0, 16), V("uoi", 0, 16))
-    copy(V("pm", 0, 2), V("pmi", 0, 2))
-    ts(CP, PM, 15.0, A.is_lt, HOLD, A.mult)
-    ts(row("xd"), row("cm"), PM, A.subtract)
-    P, FU, INV, PKU = V("p0", 0, 24), V("f0", 0, 24), V("iu", 0, 24), V("pku", 0, 24)
-    ts(row("d1"), row("xd"), 0.0, A.is_equal, -30000.0, A.mult)
-    ts(row("d2"), row("xd"), 1.0, A.is_equal, HOLD, A.mult)
-    copy(P, V("ppi", 0, 24))
-    copy(V("ku", 0, 72), V("pri", 0, 72))
-    copy(FU, V("rfi", 0, 24))
-    iv = ind(row("iv0"), P)
-    emit("v", lambda: g.vector.tensor_copy(iv[3], NUM[3]), [row("iv0")], [NUM, P])
+    ts(V("phi", 0, 2), V("pid", 0, 2), 4, A.arith_shift_right)
+    ts(V("p32", 0, 2), V("pid", 0, 2), 31, A.bitwise_and)
+    emit("g", lambda: g.affine_select(EYE[1], ONE[1], [[-1, 516]], A.is_equal, 0.0, 3, 4), [EYE], [ONE])
+    for lo in (0, 400, 800):
+        iota(V("rr", lo, lo + 16), [[0, 16]], 0, 0, True)
+    act(V("uu", C, 2 * C), V("one", 0, C), scale=0.0)
+    act(V("s1", B0, 384), V("one", 0, 192), scale=0.0)
+    act(V("s0", B0, B0 + 144), V("one", 0, 144), scale=0.0)
+    act(V("s0", B0 + 2, B0 + 144, 6), V("one", 0, 24), scale=2.0)
+    act(V("s0", B0 + 4, B0 + 144, 6), V("one", 0, 24), scale=-2.0)
+    copy(PM, V("pmi", 0, 1))
+    copy(PH, V("phi", 0, 1))
+    copy(P32, V("p32", 0, 1))
+    ts(V("jf", 0, 23), V("jj", 0, 23), PM, A.add)
+    ts(UX, PM, 12.5, A.is_gt)
+    ts(MC, PM, -13.0, A.add, 768.0, A.mult)
+    ts(V("ge", 0, 17), V("jf", 0, 17), 23.5, A.is_gt)
+    ts(V("ci", 17, 23), V("jf", 17, 23), -1.0, A.add, 1.0 / 3, A.mult)
+    fill(V("s0", 0, B0, 2), 0.0)
+    ts(V("cr", 0, 17), V("ge", 0, 17), -24.0, A.mult)
+    ts(V("cr", 17, 23), V("ci", 17, 23), -3.0, A.mult)
+    ts(V("cc", 17, 23), V("ci", 17, 23), 0.0, A.max, 23.0, A.min)
+    tt(V("cc", 0, 17), V("jf", 0, 17), V("cr", 0, 17), A.add)
+    tt(V("ge", 17, 23), V("jf", 17, 23), V("cr", 17, 23), A.add)
+    ts(MC, MC, -1.0, A.max)
+    ts(V("ci", 0, 23), V("cc", 0, 23), PH, A.add)
+    P0, F0 = V("p0", 0, 24), V("p0", 24, 48)
+    copy(P0, V("ppi", 0, 24))
+    copy(F0, V("rfi", 0, 24))
+    act(V("wd", 0, C), ind(NM, P0))
+    act(V("wd", C, 2 * C), ind(NM, F0))
+    act(V("uu", 0, C), V("one", 0, C), scale=0.0)
+    ts(V("cr", 17, 23), V("ge", 17, 23), 0.5, A.is_gt, 13.0, A.add)
+    fill(V("cr", 0, 8), float(R_F))
+    ts(V("cr", 8, 11), V("ge", 8, 11), 2.0, A.mult, float(R_N), A.add)
+    ts(V("ci", 0, 23), V("ci", 0, 23), 1, A.bitwise_and)
+    ts(V("cr", 11, 14), V("ge", 11, 14), -2.0, A.mult, float(R_P), A.add)
+    ts(V("cr", 14, 17), V("ge", 14, 17), 4.0, A.mult, float(R_E), A.add)
+    ts(V("cc", 0, 23), V("cc", 0, 23), 16.0, A.mult)
+    ts(V("cx", 0, 23), V("ci", 0, 23), T2 + 16.0, A.mult)
+    ts(V("uo", 0, 8), V("uoi", 0, 8), UX, A.add)
+    tt(V("cc", 0, 23), V("cc", 0, 23), V("cr", 0, 23), A.add)
+    fill(V("cx", 4, 8), 0.0)
+    fill(V("cx", 11, 14), 0.0)
     quant(V("uq", 0, 128), V("up", 0, 128), V("uin", 0, 512))
-    UO = V("uo", 0, 16)
-
-    def candidates(t, P, FU, part):
-        K = V("ku", 24 * t, 24 * t + 24)
-        if part == 0:
-            act(row("prow"), ind(NUM, P))
-        if part == 1:
-            act(row("pk"), ind(row("prow"), K), bias=-MID)
-
-    def differences(t):
-        D, B = "dd%d" % t, "ba%d" % t
-        if t:
-            scan(row("scp"), row("pk"))
-            ts(PKU, held("scp"), CP, A.subtract, MID, A.add)
-        scan(row("scf"), row("fk"))
-        ts(V("pkw", 0, 24), held("scp"), CP, A.subtract, MID, A.add)
-        ts(V("pkw", 24, 48), held("scf"), CP, A.subtract, MID, A.add)
-        tt(V(D, 24, 72), V("pkw", 0, 48), V(B, 24, 72), A.subtract)
-        ts(V(B, 72, 96), V(B, 48, 72), 0.0, A.add)
-        tt(V(D, 72, 96), V(D, 48, 72), V(D, 0, 24), A.subtract)
-        ts(V("dcp", 0, 96), V(D, 0, 96), CP, A.mult)
-        tt(V("bs", 0, 96), V(B, 0, 96), V("dcp", 0, 96), A.subtract)
-
-    candidates(0, P, FU, 0)
-    copy(bits(V("uuq", 0, 256), dt.uint32), ind(bits(V("uq", 0, 128), dt.uint32), UO))
-    uup, upw = V("uup", 0, 256), ind(V("up", 0, 128), UO)
-    emit("s", lambda: g.scalar.activation(uup[3], upw[3], F.Copy), [uup], [upw])
-    candidates(0, P, FU, 1)
-    act(row("frow"), ind(NUM, FU))
+    ts(ur(R_N), V("qw", 0, 24), P32, A.add)
+    tt(V("cc", 0, 23), V("cc", 0, 23), V("cx", 0, 23), A.add)
+    copy(V("ku", 0, 72), V("pri", 0, 72))
+    turn(V("ta", 0, C), V("wd", 0, C))
+    copy(bits(V("uuq", 0, 128), dt.uint32), ind(bits(V("uq", 0, 128), dt.uint32), V("uo", 0, 8)))
+    turn(V("ta", C, 2 * C), V("wd", C, 2 * C))
+    act(V("uup", 0, 128), ind(V("up", 0, 128), V("uo", 0, 8)))
+    copy(ur(R_P), V("ta", 0, C, 16))
+    copy(ur(R_F), V("ta", C, 2 * C, 16))
+    copy(V("cl", 0, 23), V("cc", 0, 23))
+    ts(BC, PM, 13.0, A.is_equal, -1.0, A.mult)
+    turn(row("a2"), V("uu", C, 2 * C))
     quant(V("xq0", 0, C), V("xp0", 0, C), V("xin", 0, 1536))
-    tt(row("d0"), row("d1"), row("d2"), A.add)
-    ts(QW, V("q16", 0, 24), PM, A.add)
-    scan(row("scp"), row("pk"))
-    for b in range(4):
-        quant(V("eq", 128 * b, 128 * b + 128), V("ep", 128 * b, 128 * b + 128), V("eye", 3 - b, 515 - b))
-    copy(V("ba0", 24, 48), V("ppi", 0, 24))
-    copy(V("ba0", 48, 72), V("rfi", 0, 24))
+    act(V("s1", 97, 144, 2), ur(R_P))
+    act(V("rr", RA, RA + C), ind(row("a2"), V("ku", 0, 24)))
+    ts(V("s1", 145, 192, 2), V("qw", 0, 24), P32, A.add)
+    ts(V("s1", 49, 96, 2), V("ppi", 0, 24), -MID, A.add)
+    copy(V("s1", B0 + 3, B0 + 144, 6), V("rfi", 0, 24))
+    ts(V("s1", 1, 48, 2), V("qn", 0, 24), PM, A.add)
 
-    def own(t):
-        copy(V("ba%d" % t, 0, 24), QW)
-        tt(V("dd%d" % t, 0, 24), V("pri", 24 * t, 24 * t + 24), QW, A.subtract)
+    def ahead(t):
+        turn2("tb", RA)
+        if t == 0:
+            quant(V("eq", 0, 128), V("ep", 0, 128), V("eye", 3, 515))
+        tt(V("s1", 0, 192, 2), pick("tb", L_D, 6), V("s1", 1, 192, 2), A.subtract)
+        ts(V("pk%d" % t, 0, 48), pick("tb", L_I, 3), MID, A.add)
+        tt(V("w2", 0, 32), pick("tb", L_AN, 2), V("s1", 0, 64, 2), A.subtract)
+        tt(V("s1", B0 + 1, B0 + 192, 6), pick("tb", L_AN, 2), V("s1", B0 + 3, B0 + 192, 6), A.subtract)
+        ts(V("ni", 0, 24), V("w2", 0, 24), 0.5, A.add, 1.0 / C, A.mult)
 
+    def signs(t, h):
+        mm((4, 6)[h], V("uuq", 0, 128), V("uup", 0, 128), V("xq%d" % t, H * h, H * h + H), V("xp%d" % t, H * h, H * h + H), H)
+        act(V("sg", H * h, H * h + H), bank((4, 6)[h], 0, H), F.Sign, bias=-2.0 ** -93)
+
+    P = ("p0", 0)
+    mm(4, V("uuq", 0, 128), V("uup", 0, 128), row("xq0"), row("xp0"), C)
+    act(row("sg"), bank(4), F.Sign, bias=-2.0 ** -93)
     for t in range(3):
-        last = t == 2
+        last, NB = t == 2, NBS[t]
         other = T.cores[rank ^ STEP[t]]
         eng = topo.engines(core, other)
         mask = sum(1 << e for e in eng)
         rid, pnc = topo.addr(other)[:2]
         X, XP = V("xq%d" % t, 0, C), V("xp%d" % t, 0, C)
+        tp, fp, pk, YQ, YP = "tp%d" % t, "fp%d" % t, "pk%d" % t, "yq%d" % t, "yp%d" % t
+        TU, FU, FW, UQ, UP = V(tp, 0, 24), V(fp, 0, 24), V("fw%d" % t, 0, 24), V("zq%d" % t, 0, H), V("zp%d" % t, 0, H)
+        cut = (0, LAST if last else H, C)
 
-        def send(dst, src, s, made):
-            recs = [e[3] for nm, a, b in flat([made]) for e in acc[nm] if e[2] and e[0] < b and a < e[1]]
+        def send(dst, src, s):
+            recs = [e[2] for nm, m in src[0] for e in acc[nm] if e[1] and e[0] & m]
             await_("g", recs)
-            g.remote_dma(dst[3], src[3], T.sem[s], T.sem.sent, pnc, rid, mask)
+            g.remote_dma(dst[1], src[1], T.sem[s], T.sem.sent, pnc, rid, mask)
             count["sent"] = count.get("sent", 0) + len(eng)
             count[s] = len(eng)
-            acc.setdefault(dst[0], []).append((dst[1], dst[2], True, (s, len(eng), {s: len(eng)})))
+            for nm, m in dst[0]:
+                acc.setdefault(nm, []).append((m, True, (s, len(eng), {s: len(eng)})))
 
-        mm(4, V("uuq", 0, 128), V("uup", 0, 128), X, XP, C)
-        mm(5, V("uuq", 128, 256), V("uup", 128, 256), X, XP, C)
-        for b in range(4):
-            mm(b, V("eq", 128 * b, 128 * b + 128), V("ep", 128 * b, 128 * b + 128), X, XP, C)
-        if t:
-            differences(t)
-        else:
-            ts(PKU, held("scp"), CP, A.subtract, MID, A.add)
-            own(0)
-        act(row("aw"), V("ps", 2048, 2048 + C), F.Sign, bias=-2.0 ** -93)
-        pu, ku = V(P[0], P[1], P[1] + 12), V("pku", 0, 12)
-        pv, kv = V(P[0], P[1] + 12, P[2]), V("pku", 12, 24)
-        act(V("ar", 0, H), ind(row("aw"), pu), F.Copy)
-        act(V("ar", H, C), ind(row("aw"), pv), F.Copy)
-        tt(V("er", 0, H), ind(row("aw"), ku), V("ar", 0, H), A.is_equal)
-        tt(V("er", H, C), ind(row("aw"), kv), V("ar", H, C), A.is_equal)
-        if t == 0:
-            act(row("fk"), ind(row("frow"), V("ku", 0, 24)), bias=-MID)
-            differences(0)
-        act(row("bw"), V("ps", 2560, 2560 + C), F.Sign)
-        for b in range(2):
-            act(V("fb", C * b, C * b + C), V("ps", 512 * b, 512 * b + C), F.Copy)
-        scan(row("sc"), row("er"))
-        for i in range(4):
-            tt(V("mu", 24 * i, 24 * i + 24), held("sc"), V("dd%d" % t, 24 * i, 24 * i + 24), A.mult)
-        tt(V("sel", 0, 72), V("mu", 0, 72), V("bs", 0, 72), A.add)
-        tt(V("sel", 72, 96), V("mu", 72, 96), V("bs", 72, 96), A.add)
-        copy(V("tu", 0, 72), V("sel", 0, 72))
-        TU, P, CU = V("tu", 0, 24), V("tu", 24, 48), V("tu", 48, 72)
-        act(row("br"), ind(row("bw"), P), F.Relu)
-        for b in (2, 3):
-            act(V("fb", C * b, C * b + C), V("ps", 512 * b, 512 * b + C), F.Copy)
-        for b in range(3):
-            act(V("gb", C * b, C * b + C), ind(V("fb", C * b, C * b + C), P), F.Copy, scale=0.5)
-        act(V("gb", 3 * C + H, 4 * C), ind(V("fb", 3 * C, 4 * C), V("tu", 36, 48)), F.Copy, scale=0.5)
-        ts(V("ni", 0, 24), V("sel", 72, 96), -191.5, A.add, 1.0 / C, A.mult)
-        copy(row("tr"), ind(NUM, TU))
-        ts(V("nf", 0, 24), V("ni", 0, 24), -float(C), A.mult)
-        tt(row("rr"), ind(row("tr"), CU), row("br"), A.mult)
-        tt(V("al", 0, 24), V("sel", 72, 96), V("nf", 0, 24), A.add)
-        scan(row("scb"), row("br"))
-        ts(V("alc", 0, 24), V("al", 0, 24), CP, A.add)
-        ts(V("mm", 0, 24), held("scb"), CP, A.subtract, 0.5, A.is_lt)
-        scan(row("sc2"), row("rr"))
-        tt(V("ma", 0, 24), V("mm", 0, 24), V("alc", 0, 24), A.mult)
-        if not last:
-            copy(V("ba%d" % (t + 1), 24, 48), V("sel", 24, 48))
-        tt(V("mx", 0, 24), V("ma", 0, 24), held("sc2"), A.max)
-        FU = V("fu%d" % t, 0, 24)
-        ts(FU, V("mx", 0, 24), CP, A.subtract)
-        if t == 0:
-            scan(row("sc3"), row("iv0"))
-            ts(INV, held("sc3"), CP, A.subtract)
-            own(1)
-            own(2)
-        send(V("lf%d" % t, 0, 24), FU, "af%d" % t, FU)
+        def unpack(b):
+            act(V("fh", C * b, C * b + C), bank(b), scale=0.5)
 
-        def twin(b, h):
-            copy(V("gc", C * b + H * h, C * b + H * h + H), V("gb", C * b + H * h, C * b + H * h + H))
+        def twice(k, add):
+            if NB > 2 * k:
+                fb, fh = V("fb", 2 * k * C, min(NB, 2 * k + 2) * C), V("fh", 2 * k * C, min(NB, 2 * k + 2) * C)
+                if add:
+                    emit("g", lambda: g.dma_start(fb[1], fh[1], accum_op=A.add), [fb], [fh, fb], "da%d%d" % (k, t), 16)
+                else:
+                    emit("y", lambda: g.sync.dma_start(fb[1], fh[1]), [fb], [fh], "dc%d%d" % (k, t), 16)
+
+        def base(k):
+            if not last:
+                copy(*((V("s1", 49, 96, 2), V("so", 49, 96, 2)), (V("s1", 97, 144, 2), ur(R_P)), (ul(R_P), ur(R_P)), (V("s1", B0 + 3, B0 + 144, 6), FU))[k])
 
         def mix(b, h):
-            o = lane("zt", b, H * h, H * h + H)
-            tt(o, ind(V("gb", C * b, C * b + C), V(FU[0], 12 * h, 12 * h + 12)), V("gc", C * b + H * h, C * b + H * h + H), A.add)
-        ts(V("gb", 3 * C, 3 * C + H), ind(V("fb", 3 * C, 4 * C), V("tu", 24, 36)), 0.5, A.mult)
-        twin(0, 1)
-        twin(1, 1)
-        mix(0, 1)
-        mix(1, 1)
-        twin(2, 1)
-        mix(2, 1)
-        twin(3, 1)
-        mix(3, 1)
-        UQ, UP = V("zuq%d" % t, 0, H), V("zup%d" % t, 0, H)
-        quant(UQ, UP, V("zt", 768, 1536))
-        send(bits(V("lq%d" % t, 0, H)), bits(UQ), "aq%d" % t, UQ)
-        send(V("lp%d" % t, 0, H), UP, "ap%d" % t, UP)
-        act(row("ir"), ind(row("tr"), INV), bias=-MID)
-        scan(row("sc3"), row("ir"))
-        twin(0, 0)
-        ts(INV, held("sc3"), CP, A.subtract, MID, A.add)
+            tt(lane("zt", b, H * h, H * h + H), ind(V("fh", C * b, C * b + C), V(fp, 24 + 12 * h, 36 + 12 * h)), V("gb", C * b + H * h, C * b + H * h + H), A.add)
+
+        def table():
+            copy(ur(R_E), V("lf%d" % t, 0, 24))
+            base(2)
+            turn(row("a2"), V("uu", C, 2 * C))
+            act(row("ef"), ind(row("a2"), FU))
+
+        def layer(b, lo, hi, at):
+            mm(at, V("wq", 128 * b, 128 * b + 128), V("wp", 128 * b, 128 * b + 128), V(YQ, lo, hi), V(YP, lo, hi), hi - lo)
+
+        def cast(q, b, lo, hi, at):
+            o = V("bb", C * b + lo, C * b + hi)
+            if q == "v":
+                ts(o, bank(at, 0, hi - lo), 0.03125, A.mult)
+            else:
+                act(o, bank(at, 0, hi - lo), scale=0.03125)
+
+        def pairs():
+            act(V("rr", RA, RA + C), ind(row("a2"), V("ku", 24 * t + 24, 24 * t + 48)))
+
+        def state(b, h):
+            lo, hi = cut[h], cut[h + 1]
+            if b < NB:
+                tt(lane("xt", b, lo, hi), ind(V("bb", C * b, C * b + C), V("eu", lo // 16, hi // 16)), V("fb", C * b + lo, C * b + hi), A.add)
+            else:
+                tt(lane("xt", b, lo, hi), V("bg", C * b + lo, C * b + hi), bank(b, lo, hi), A.add)
+
+        def look(b, h):
+            lo, hi = cut[h], cut[h + 1]
+            act(V("bg", C * b + lo, C * b + hi), ind(V("bb", C * b, C * b + C), V("eu", lo // 16, hi // 16)))
+
+        def pack(h):
+            lo, hi = cut[h], cut[h + 1]
+            quant(V("xq%d" % (t + 1), lo, hi), V("xp%d" % (t + 1), lo, hi), V("xt", 4 * lo, 4 * hi))
+
+        ahead(t)
+        for h in range(2):
+            act(V("rs", H * h, H * h + H), ind(row("sg"), V(P[0], P[1] + 12 * h, P[1] + 12 * h + 12)), F.Identity, bias=BC, scale=MC)
         if t == 0:
-            act(row("prow"), ind(NUM, P))
-            act(row("frow"), ind(NUM, FU))
-            act(row("hr"), ind(row("frow"), INV), bias=-MID)
-            candidates(1, P, FU, 1)
-            act(row("fs"), ind(NUM, V("lf0", 0, 24)))
-        else:
-            act(row("prow"), ind(NUM, P))
-            act(row("fs"), ind(NUM, V("lf%d" % t, 0, 24)))
-            act(row("ef"), ind(row("fs"), FU))
-            act(row("ej"), ind(row("ef"), INV), bias=-MID)
-            if not last:
-                candidates(t + 1, P, FU, 1)
-            else:
-                act(row("frow"), ind(NUM, FU))
-        for b in (1, 2, 3):
-            twin(b, 0)
+            act(ul(R_P), ur(R_P))
+            for b in range(1, 4):
+                quant(V("eq", 128 * b, 128 * b + 128), V("ep", 128 * b, 128 * b + 128), V("eye", 3 - b, 515 - b))
+        for h in range(2):
+            tt(V("rr", RB + H * h, RB + H * h + H), ind(row("sg"), V(pk, 24 + 12 * h, 36 + 12 * h)), V("rs", H * h, H * h + H), A.add)
+            if h == 0:
+                ts(V("nx", 0, 24), V("ni", 0, 24), float(C), A.mult, -float(C), A.add)
+        tt(V("s0", B0 + 1, B0 + 144, 6), V("nx", 0, 24), V("s1", 0, 48, 2), A.add)
         for b in range(4):
-            mix(b, 0)
-            if t == 0 and b == 1:
-                scan(row("sc5"), row("hr"))
-                ts(V("hu", 0, 24), held("sc5"), CP, A.subtract, MID, A.add)
-                act(row("ej"), ind(row("fs"), V("hu", 0, 24)), bias=-MID)
-        quant(V("zlq", 0, H), V("zlp", 0, H), V("zt", 0, 768))
-        low, up = (0, 1, 2, 5), (4, 6, 7, 0)
-
-        def layer(b, h):
-            x = (V("lq%d" % t, 0, H), V("lp%d" % t, 0, H)) if h else (V("zlq", 0, H), V("zlp", 0, H))
-            mm((low, up)[h][b], V("wq", 128 * b, 128 * b + 128), V("wp", 128 * b, 128 * b + 128), x[0], x[1], H)
-
-        def cast(b, h):
-            o, i = V("bb", C * b + H * h, C * b + H * h + H), 512 * (low, up)[h][b]
-            if b == 0:
-                ts(o, V("ps", i, i + H), 0.03125, A.mult)
-            else:
-                act(o, V("ps", i, i + H), F.Copy, scale=0.03125)
-        layer(0, 0)
-        layer(1, 0)
-        layer(0, 1)
-        layer(1, 1)
+            mm(b, V("eq", 128 * b, 128 * b + 128), V("ep", 128 * b, 128 * b + 128), X, XP, C)
+        unpack(0)
+        unpack(1)
+        twice(0, False)
+        turn2("ta", RB)
+        act(V("s1", B0, B0 + 160, 2), pick("ta", L_B, 5), scale=0.5)
+        unpack(2)
+        unpack(3)
+        twice(1, False)
+        ts(V("s0", 97, 192, 2), pick("ta", L_AW, 3, C), 0.0, A.is_equal)
+        ts(V("s0", 1, 96, 2), pick("ta", L_AN, 3), 0.0, A.is_equal)
+        scan(V("uu", 0, C, 8), 144, 192)
+        scan(V("uu", C + 2, 2 * C, 8), 96, 144)
+        ts(V("s0", B0 + 3, B0 + 192, 6), pick("ta", L_AN, 2), 0.0, A.is_equal, 0.5, A.mult)
+        turn(V("wd", 0, C), V("uu", 0, C))
+        scan(V("sb", 0, 144), B0, B0 + 144)
+        scan(V("so", 0, 96), 0, 96)
+        ts(V("c2", 0, 24), V("sb", 4, 144, 6), -0.5, A.mult, MID, A.add)
+        turn(V("wd", C, 2 * C), V("uu", C, 2 * C))
+        ts(V(tp, 0, 48), V("so", 1, 96, 2), MID, A.add)
+        P = (tp, 24)
+        copy(V("rr", RA, RA + H), ind(V("wd", 0, 768), V("c2", 0, 12)))
+        act(V("rr", RA + H, RA + C), ind(V("wd", 0, 768), V("c2", 12, 24)))
+        base(0)
+        for h in (1, 0):
+            for b in range(4):
+                act(V("gb", C * b + H * h, C * b + H * h + H), ind(V("fh", C * b, C * b + C), V(tp, 24 + 12 * h, 36 + 12 * h)))
+        turn2("tb", RA)
+        copy(FW, V("tb", R_N, C, 16))
+        ts(V(fp, 0, 48), pick("tb", L_D, 3), MID, A.add)
+        send(V("lf%d" % t, 0, 24), FW, "af%d" % t)
         if t:
-            scan(row("sc4"), row("ej"))
-        cast(0, 0)
-        cast(1, 0)
-        if not t:
-            scan(row("sc4"), row("ej"))
-        ts(V("eu", 0, 24), held("sc4"), CP, A.subtract, MID, A.add)
+            twice(0, True)
+        copy(ur(R_F), V("tb", R_N, C, 16))
+        for b in range(4):
+            mix(b, 1)
+        base(1)
+        quant(UQ, UP, V("zt", 768, 1536))
+        send(bits(V(YQ, H, C)), bits(UQ), "aq%d" % t)
+        send(V(YP, H, C), UP, "ap%d" % t)
+        if t == 0:
+            twice(0, True)
+        twice(1, True)
+        EJ = V("rr", RB, RB + C)
+        if t == 0:
+            for b in range(4):
+                mix(b, 0)
+            base(3)
+            fill(V("po", 0, 48), MID)
+            emit("y", lambda: g.sync.dma_start(T.pf[:], T.po[:]), [], [V("po", 0, 48)], "pa", 16)
+            quant(V(YQ, 0, H), V(YP, 0, H), V("zt", 0, 768))
+            emit("v", lambda: g.vector.tensor_copy(ind(EJ, P0)[1], V("wd", 0, C)[1]), [EJ], [V("wd", 0, C), P0])
+            for b, at in ((0, 0), (1, 1), (2, 4), (3, 5)):
+                layer(b, 0, H, at)
+                cast("s", b, 0, H, at)
+            table()
+            turn2("ta", RB)
+            ts(V("iv", 0, 32), pick("ta", L_D, 2), MID, A.add)
+            act(EJ, ind(row("ef"), V("iv", 0, 24)))
+            for b, at in ((0, 6), (1, 7), (3, 0), (2, 1)):
+                layer(b, H, C, at)
+            cast("v", 0, H, C, 6)
+            cast("v", 1, H, C, 7)
+            turn2("ta", RB)
+            cast("s", 3, H, C, 0)
+            cast("s", 2, H, C, 1)
+            ts(V("eu", 0, 32), pick("ta", L_I, 2), MID, A.add)
+        else:
+            table()
+            if last:
+                g.wait_ge(T.sem.pa, 16)
+                for k, r in enumerate((R_P, R_F)):
+                    emit("g", lambda: g.dma_start(T.pf[:, C * k:C * k + C], T.a2[r:128:16, :], accum_op=A.add), [], [row("a2")], "pb", 16)
+            act(row("eg"), ind(row("ef"), TU))
+            act(EJ, ind(row("eg"), V("pk2" if last else "iv", 0, 24)))
+            for b in range(4):
+                mix(b, 0)
+            base(3)
+            if last:
+                quant(V("vq", 0, 128), V("vp", 0, 128), V("vin", 0, 512))
+            quant(V(YQ, 0, H), V(YP, 0, H), V("zt", 0, 768))
+            for b, lo, hi, at in ((0, 0, H, 0), (1, 0, H, 1), (0, H, C, 4), (1, H, C, 5), (2, 0, C, 6), (3, 0, C, 7)):
+                layer(b, lo, hi, at)
+            cast("v", 0, 0, H, 0)
+            if last:
+                cast("s", 0, H, C, 4)
+            else:
+                pairs()
+            turn2("ta", RB)
+            cast("v", 1, 0, H, 1)
+            ts(V("eu", 0, 32), pick("ta", L_I, 2), MID, A.add)
+            if not last:
+                cast("v", 0, H, C, 4)
+            cast("s", 1, H, C, 5)
+            cast("s", 2, 0, C, 6)
+            cast("s", 3, 0, C, 7)
+            if not last:
+                act(row("x1"), ind(V("wd", 0, C), V("iv", 0, 24)))
+                emit("y", lambda: g.sync.dma_start(T.rr[R_E:128:16, RA:RA + C], T.x1[R_N:128:16, :]), [V("rr", RA, RA + C)], [row("x1")], "dx", 16)
+        for h in range(2):
+            for b in range(NB, 4):
+                look(b, h)
+        if t == 0:
+            pairs()
+        for b, h in ((0, 0), (1, 0), (0, 1), (2, 0), (1, 1)) + (((3, 0),) if last else ((2, 1), (3, 0))):
+            state(b, h)
         if not last:
-            ts(V("ba%d" % (t + 1), 48, 72), V("mx", 0, 24), CP, A.subtract)
-        cast(0, 1)
-        cast(1, 1)
-        for b in (2, 3):
-            for h in (0, 1):
-                layer(b, h)
-                cast(b, h)
-
-        def state(b, h=None):
-            lo, hi = (0, C) if h is None else (H * h, H * h + H)
-            tt(lane("xt", b, lo, hi), ind(V("bb", C * b, C * b + C), V("eu", lo // 16, hi // 16)), V("fb", C * b + lo, C * b + hi), A.add)
-        if not last:
-            act(row("b3"), ind(V("bb", 3 * C, 4 * C), V("eu", 0, 24)), F.Copy)
-            for b in range(3):
-                state(b)
-            tt(lane("xt", 3, 0, C), row("b3"), V("ps", 1536, 1536 + C), A.add)
-            if t:
-                act(row("frow"), ind(NUM, FU))
-            act(row("fk"), ind(row("frow"), V("ku", 24 * t + 24, 24 * t + 48)), bias=-MID)
-            quant(V("xq%d" % (t + 1), 0, C), V("xp%d" % (t + 1), 0, C), V("xt", 0, 1536))
-    store(T.pf[:, 0:C], ("prow", 0, C, T.prow[0:128:16, :]))
-    store(T.pf[:, C:2 * C], ("frow", 0, C, T.frow[0:128:16, :]))
-    quant(V("vq", 0, 128), V("vp", 0, 128), V("vin", 0, 512))
-    for b, h in ((0, 0), (0, 1), (1, 0), (1, 1), (2, 0), (3, 0)):
-        state(b, h)
+            pack(0)
+            signs(t + 1, 0)
+            state(3, 1)
+            pack(1)
+            signs(t + 1, 1)
 
     def finish(h):
-        X, XP = V("xq3", H * h, H * h + H), V("xp3", H * h, H * h + H)
-        quant(X, XP, V("xt", 768 * h, 768 * h + 768))
-        mm(4 + h, V("vq", 0, 128), V("vp", 0, 128), X, XP, H)
-        store(T.oc[:, 768 * h:768 * h + 768], bits(X))
+        pack(h)
+        lo, hi = cut[h], cut[h + 1]
+        X, XP = V("xq3", lo, hi), V("xp3", lo, hi)
+        mm(4 + h, V("vq", 0, 128), V("vp", 0, 128), X, XP, hi - lo)
+        store(T.oc[:, 4 * lo:4 * hi], bits(X))
     finish(0)
-    act(V("yo", 0, H), V("ps", 2048, 2048 + H), F.Copy)
-    store(T.y[:, 0:H], V("yo", 0, H), "s")
+    act(V("yo", 0, LAST), bank(4, 0, LAST))
+    store(T.y[:, 0:LAST], V("yo", 0, LAST))
     state(2, 1)
     state(3, 1)
     finish(1)
     for k in range(4):
-        store(T.osc[4 * k:4 * k + 4, :], ("xp3", 0, C, T.xp3[32 * k:32 * k + 4, :]), "y" if k % 2 else "s")
-    ts(V("yo", H, C), V("ps", 2560, 2560 + H), 1.0, A.mult)
-    store(T.y[:, H:C], V("yo", H, C))
+        store(T.osc[4 * k:4 * k + 4, :], (row("xp3")[0], T.xp3[32 * k:32 * k + 4, :]), "s")
+    ts(V("yo", LAST, C), bank(5, 0, C - LAST), 1.0, A.mult)
+    store(T.y[:, LAST:C], V("yo", LAST, C))
     for s in count:
         if know["g"].get(s, 0) < count[s]:
             g.wait_ge(T.sem[s], count[s])

@@ -4,34 +4,34 @@ C, H, STEP = 384, 192, [1, 2, 4]
 MID = 192.0
 BF, FL, U16, I32, CODE = "bfloat16", "float32", "uint16", "int32", "float8_e4m3fn_x4"
 T2 = 384
-R_E, R_N, R_P, R_F = 6, 8, 10, 12
-NBS = (2, 3, 3)
+R_I, R_E, R_N, R_P, R_F = 0, 6, 8, 10, 12
+LOOKS = (((3, 0), (2, 0), (3, 1), (2, 1)), ((3, 0), (3, 1), (2, 1)), ((3, 0), (3, 1), (2, 1)))
 LAST = 192
-L_AN, L_AW, L_D, L_I, L_B = 0, 4, 8, 14, 18
+L_AW, L_AN, L_B, L_Y, L_I, L_D, NL = 0, 4, 8, 12, 16, 20, 26
 
 SCRATCH = {"ps": ("psum", [128, 4096], "float32")}
 for _n, _c, _d in (
-        [("xin", 1536, BF), ("uin", 512, BF), ("vin", 512, BF), ("ppi", 24, I32), ("rfi", 24, I32), ("pri", 72, I32)]
+        [("xin", 1536, BF), ("uin", 512, BF), ("vin", 512, BF), ("pl", C, I32), ("pri", 72, I32), ("sj", 24, I32), ("su", 24, U16)]
         + [("wq", 512, CODE), ("wp", 512, "uint8"), ("uq", 128, CODE), ("up", 128, "uint8"), ("uuq", 128, CODE), ("uup", 128, "uint8")]
         + [("vq", 128, CODE), ("vp", 128, "uint8"), ("eq", 512, CODE), ("ep", 512, "uint8")]
-        + [("one", 516, BF), ("eye", 516, BF), ("uoi", 8, I32), ("uo", 8, U16), ("pid", 2, I32), ("pmi", 2, I32), ("p32", 2, I32)]
-        + [("phi", 2, I32), ("col", 8, FL), ("jj", 24, I32), ("jf", 24, FL), ("ge", 24, FL), ("cc", 24, FL), ("ci", 24, I32)]
-        + [("cx", 24, FL), ("cr", 24, FL), ("cl", 24, U16), ("qn", 24, I32), ("qw", 24, I32), ("nm", C, BF)]
+        + [("one", 516, BF), ("eye", 516, BF), ("uoi", 8, I32), ("uo", 8, U16), ("col", 10, FL)]
+        + [(k, 2, I32) for k in ("pid", "p17", "pmi", "p8", "phi")] + [("jj", NL, I32), ("cl", NL, U16)]
+        + [(k, NL, FL) for k in ("jf", "ge", "cc", "cr")]
         + [(k, 1536, BF) for k in ("fh", "fb", "gb", "bb", "bg", "zt", "xt")]
-        + [(k, C, BF) for k in ("sg", "rs", "a2", "ef", "eg", "x1")]
+        + [(k, C, BF) for k in ("nm", "sg", "rs", "a2", "ef", "eg", "mi")]
         + [("uu", 768, BF), ("wd", 768, BF), ("rr", 816, BF), ("ta", 800, BF), ("tb", 800, BF)]
         + [("s0", 384, FL), ("s1", 384, FL), ("so", 96, FL), ("sb", 144, FL), ("w2", 32, FL)]
         + [("ni", 24, I32), ("nx", 24, FL), ("po", 48, FL), ("yo", C, FL)]
-        + [("ku", 72, U16), ("p0", 48, U16), ("c2", 24, U16), ("iv", 32, U16), ("eu", 32, U16)]
+        + [("ku", 72, U16), ("p0", 48, U16), ("c2", 24, U16), ("iv", 32, U16)]
         + [("xq%d" % t, C, CODE) for t in range(4)] + [("xp%d" % t, C, "uint8") for t in range(4)]
-        + [("%s%d" % (k, t), 48, U16) for k in ("tp", "fp", "pk") for t in range(3)]
+        + [("%s%d" % (k, t), 48, U16) for k in ("tp", "fp", "pk", "eu") for t in range(3)]
         + [("%s%d" % (k, t), 24, BF) for k in ("fw", "lf") for t in range(3)]
         + [("zq%d" % t, H, CODE) for t in range(3)] + [("yq%d" % t, C, CODE) for t in range(3)]
         + [("zp%d" % t, H, "uint8") for t in range(3)] + [("yp%d" % t, C, "uint8") for t in range(3)]):
     SCRATCH[_n] = ("sbuf", [128, _c], _d)
 LOADS = ["x", "u", "v", "pp", "rf", "pr", "wc", "ws"]
-SEMAPHORES = (["qv", "qs", "qt", "qg", "sent", "out", "dx", "pa", "pb"] + ["ld_" + k for k in LOADS]
-              + ["%s%d" % (k, t) for k in ("af", "aq", "ap", "dc0", "dc1", "da0", "da1") for t in range(3)])
+SEMAPHORES = (["qv", "qs", "qt", "qg", "sent", "out", "pa", "pb"] + ["ld_" + k for k in LOADS]
+              + ["%s%d" % (k, t) for k in ("af", "aq", "ap", "dc", "da") for t in range(3)])
 
 
 def rank_program(g, core, T, topo):
@@ -73,11 +73,11 @@ def rank_program(g, core, T, topo):
                 know[q][k] = max(know[q].get(k, 0), snap[k])
 
     def emit(q, fn, w, r, s=None, n=1):
-        use = [(x, True) for v in w for x in v[0]] + [(x, x[0] == "ps") for v in r for x in v[0]]
+        use = [(x, True) for v in w for x in v[0]] + [(x, False) for v in r for x in v[0]]
         recs = {}
         for (nm, m), wr in use:
             for e in acc.get(nm, []):
-                if e[0] & m and (wr or e[1]):
+                if e[0] & m and (wr or e[1] or (nm == "ps" and e[2][0] != "q" + q)):
                     k = e[2][0]
                     if k not in recs or recs[k][1] < e[2][1]:
                         recs[k] = e[2]
@@ -143,9 +143,15 @@ def rank_program(g, core, T, topo):
 
     RA, RB = 16, 416
 
+    def turn1(to, r, k):
+        if k == 0:
+            turn(V(to, 0, C), V("rr", r, r + C))
+        else:
+            turn(V(to, T2, T2 + 416), V("rr", r - 16, r + 400))
+
     def turn2(to, r):
-        turn(V(to, 0, C), V("rr", r, r + C))
-        turn(V(to, T2, T2 + 416), V("rr", r - 16, r + 400))
+        turn1(to, r, 0)
+        turn1(to, r, 1)
 
     def pick(tile, lo, n, wide=800):
         return ind(V(tile, 0, wide), V("cl", lo, lo + n))
@@ -156,99 +162,87 @@ def rank_program(g, core, T, topo):
     def ul(r):
         return V("uu", r, C, 16)
 
-    PM, MC, BC, P32, PH, UX = [V("col", k, k + 1) for k in range(6)]
+    PM, MC, BC, P24, PH, UX, PAR, MS, MB = [V("col", k, k + 1) for k in range(9)]
     B0 = 192
 
-    load("s", "pp", V("ppi", 0, 24), T.pp[:])
-    load("y", "rf", V("rfi", 0, 24), T.rf[:])
-    load("s", "pr", V("pri", 0, 72), T.pr[:])
-    load("y", "u", V("uin", 0, 512), T.u[:])
-    load("s", "x", V("xin", 0, 1536), T.x[:])
+    ONE, EYE, NM, PL = V("one", 0, 516), V("eye", 0, 516), row("nm"), row("pl")
+    load("s", "u", V("uin", 0, 512), T.u[:])
+    fill(PL, 0)
+    for k, (name, r, ap) in enumerate((("pp", R_P, T.pp), ("rf", R_F, T.rf))):
+        emit("y", lambda: g.sync.dma_start(T.pl[r:128:16, :], ap[:]), [([("rows", 1 << k)], None)], [PL], "ld_" + name, 16)
+    load("y", "pr", V("pri", 0, 72), T.pr[:])
+    load("y", "x", V("xin", 0, 1536), T.x[:])
+    await_("y", [e[2] for e in acc["xin"]])
     load("y", "wc", bits(V("wq", 0, 512)), T.wc[:])
     load("y", "ws", V("wp", 0, 512), T.ws[:])
-    load("y", "v", V("vin", 0, 512), T.v[:])
-    ONE, EYE, NM = V("one", 0, 516), V("eye", 0, 516), row("nm")
     iota(V("pid", 0, 2), [[0, 2]], 0, 1)
-    iota(V("jj", 0, 8), [[0, 2], [16, 4]], 0, 0)
-    iota(V("jj", 8, 17), [[0, 3], [16, 3]], 0, 0)
-    iota(V("jj", 17, 23), [[16, 6]], -16, 0)
-    iota(NM, [[1, C]], -int(MID), 0, True)
-    iota(V("uoi", 0, 8), [[16, 8]], 0, 0)
-    iota(V("qw", 0, 24), [[32, 12], [0, 2]], -int(MID), 0)
-    iota(V("qn", 0, 24), [[16, 24]], -int(MID), 0)
+    iota(V("p17", 0, 2), [[0, 2]], 0, 17)
+    iota(V("sj", 0, 24), [[1, 24]], 0, 0)
     fill(ONE, 1.0)
-    ts(V("pmi", 0, 2), V("pid", 0, 2), 15, A.bitwise_and)
-    ts(V("phi", 0, 2), V("pid", 0, 2), 4, A.arith_shift_right)
-    ts(V("p32", 0, 2), V("pid", 0, 2), 31, A.bitwise_and)
+    iota(V("jj", L_AW, L_AN), [[256, 4]], R_F, 0)
+    iota(V("jj", L_AN, L_I), [[1, 3], [256, 4]], R_F, 0)
+    iota(V("jj", L_I, L_D), [[256, 4]], R_E, 0)
+    iota(V("jj", L_D, L_D + 6), [[R_P - R_N, 2], [256, 3]], R_N, 0)
+    iota(V("uoi", 0, 8), [[16, 8]], 0, 0)
     emit("g", lambda: g.affine_select(EYE[1], ONE[1], [[-1, 516]], A.is_equal, 0.0, 3, 4), [EYE], [ONE])
-    for lo in (0, 400, 800):
+    for lo in (400, 800, 0):
         iota(V("rr", lo, lo + 16), [[0, 16]], 0, 0, True)
-    act(V("uu", C, 2 * C), V("one", 0, C), scale=0.0)
+    iota(V("uu", 0, 2 * C), [[0, 2 * C]], 0, 0, True)
+    ts(V("pmi", 0, 2), V("pid", 0, 2), 15, A.bitwise_and)
+    ts(V("p8", 0, 2), V("pid", 0, 2), 7, A.bitwise_and)
+    emit("v", lambda: g.vector.tensor_tensor_scan(NM[1], row("one")[1], row("one")[1], -MID - 1, A.mult, A.add), [NM], [row("one")])
+    ts(PM, V("pmi", 0, 1), -13.0, A.add)
+    ts(MS, V("p8", 0, 1), 0.0, A.is_equal)
+    ts(P24, V("pmi", 0, 1), 24.0, A.mult)
+    ts(MB, PM, R_N - 12.5, A.is_gt, -MID, A.mult)
+    ts(PH, V("pmi", 0, 1), 16.0, A.mult)
+    act(V("s0", 0, B0 + 144), V("one", 0, B0 + 144), scale=0.0)
+    act(row("mi"), NM, F.Identity, scale=MS, bias=MB)
+    ts(V("su", 0, 24), V("sj", 0, 24), P24, A.add)
+    ts(V("phi", 0, 2), V("p17", 0, 2), 4, A.arith_shift_right, 1, A.bitwise_and)
+    ts(V("jf", 0, NL), V("jj", 0, NL), PH, A.add)
+    ts(UX, PM, -0.5, A.is_gt)
+    ts(PAR, V("phi", 0, 1), T2 + 16.0, A.mult)
+    ts(V("ge", 0, NL), V("jf", 0, NL), C - 0.5, A.is_gt)
+    ts(V("uo", 0, 8), V("uoi", 0, 8), UX, A.add)
+    ts(MC, PM, 768.0, A.mult, -1.0, A.max)
+    for lo, hi, step in ((L_AW, L_I, 0), (L_I, L_D, R_I - R_E), (L_D, L_D + 3, R_P - R_N), (L_D + 3, NL, R_N - R_P)):
+        act(V("cr", lo, hi), V("ge", lo, hi), scale=float(step - C))
     act(V("s1", B0, 384), V("one", 0, 192), scale=0.0)
-    act(V("s0", B0, B0 + 144), V("one", 0, 144), scale=0.0)
     act(V("s0", B0 + 2, B0 + 144, 6), V("one", 0, 24), scale=2.0)
     act(V("s0", B0 + 4, B0 + 144, 6), V("one", 0, 24), scale=-2.0)
-    copy(PM, V("pmi", 0, 1))
-    copy(PH, V("phi", 0, 1))
-    copy(P32, V("p32", 0, 1))
-    ts(V("jf", 0, 23), V("jj", 0, 23), PM, A.add)
-    ts(UX, PM, 12.5, A.is_gt)
-    ts(MC, PM, -13.0, A.add, 768.0, A.mult)
-    ts(V("ge", 0, 17), V("jf", 0, 17), 23.5, A.is_gt)
-    ts(V("ci", 17, 23), V("jf", 17, 23), -1.0, A.add, 1.0 / 3, A.mult)
-    fill(V("s0", 0, B0, 2), 0.0)
-    ts(V("cr", 0, 17), V("ge", 0, 17), -24.0, A.mult)
-    ts(V("cr", 17, 23), V("ci", 17, 23), -3.0, A.mult)
-    ts(V("cc", 17, 23), V("ci", 17, 23), 0.0, A.max, 23.0, A.min)
-    tt(V("cc", 0, 17), V("jf", 0, 17), V("cr", 0, 17), A.add)
-    tt(V("ge", 17, 23), V("jf", 17, 23), V("cr", 17, 23), A.add)
-    ts(MC, MC, -1.0, A.max)
-    ts(V("ci", 0, 23), V("cc", 0, 23), PH, A.add)
-    P0, F0 = V("p0", 0, 24), V("p0", 24, 48)
-    copy(P0, V("ppi", 0, 24))
-    copy(F0, V("rfi", 0, 24))
-    act(V("wd", 0, C), ind(NM, P0))
-    act(V("wd", C, 2 * C), ind(NM, F0))
-    act(V("uu", 0, C), V("one", 0, C), scale=0.0)
-    ts(V("cr", 17, 23), V("ge", 17, 23), 0.5, A.is_gt, 13.0, A.add)
-    fill(V("cr", 0, 8), float(R_F))
-    ts(V("cr", 8, 11), V("ge", 8, 11), 2.0, A.mult, float(R_N), A.add)
-    ts(V("ci", 0, 23), V("ci", 0, 23), 1, A.bitwise_and)
-    ts(V("cr", 11, 14), V("ge", 11, 14), -2.0, A.mult, float(R_P), A.add)
-    ts(V("cr", 14, 17), V("ge", 14, 17), 4.0, A.mult, float(R_E), A.add)
-    ts(V("cc", 0, 23), V("cc", 0, 23), 16.0, A.mult)
-    ts(V("cx", 0, 23), V("ci", 0, 23), T2 + 16.0, A.mult)
-    ts(V("uo", 0, 8), V("uoi", 0, 8), UX, A.add)
-    tt(V("cc", 0, 23), V("cc", 0, 23), V("cr", 0, 23), A.add)
-    fill(V("cx", 4, 8), 0.0)
-    fill(V("cx", 11, 14), 0.0)
-    quant(V("uq", 0, 128), V("up", 0, 128), V("uin", 0, 512))
-    ts(ur(R_N), V("qw", 0, 24), P32, A.add)
-    tt(V("cc", 0, 23), V("cc", 0, 23), V("cx", 0, 23), A.add)
+    ts(BC, PM, 0.0, A.is_equal, -1.0, A.mult)
+    A2, P0, rows = V("rr", RB, RB + C), V("p0", 24, 48), ind(PL, V("su", 0, 24))
+    tt(A2, (rows[0] + [("rows", 3)], rows[1]), row("mi"), A.add)
     copy(V("ku", 0, 72), V("pri", 0, 72))
-    turn(V("ta", 0, C), V("wd", 0, C))
-    copy(bits(V("uuq", 0, 128), dt.uint32), ind(bits(V("uq", 0, 128), dt.uint32), V("uo", 0, 8)))
-    turn(V("ta", C, 2 * C), V("wd", C, 2 * C))
+    quant(V("uq", 0, 128), V("up", 0, 128), V("uin", 0, 512))
+    act(V("rr", RA, RA + C), ind(A2, V("ku", 0, 24)))
     act(V("uup", 0, 128), ind(V("up", 0, 128), V("uo", 0, 8)))
-    copy(ur(R_P), V("ta", 0, C, 16))
-    copy(ur(R_F), V("ta", C, 2 * C, 16))
-    copy(V("cl", 0, 23), V("cc", 0, 23))
-    ts(BC, PM, 13.0, A.is_equal, -1.0, A.mult)
-    turn(row("a2"), V("uu", C, 2 * C))
-    quant(V("xq0", 0, C), V("xp0", 0, C), V("xin", 0, 1536))
-    act(V("s1", 97, 144, 2), ur(R_P))
-    act(V("rr", RA, RA + C), ind(row("a2"), V("ku", 0, 24)))
-    ts(V("s1", 145, 192, 2), V("qw", 0, 24), P32, A.add)
-    ts(V("s1", 49, 96, 2), V("ppi", 0, 24), -MID, A.add)
-    copy(V("s1", B0 + 3, B0 + 144, 6), V("rfi", 0, 24))
-    ts(V("s1", 1, 48, 2), V("qn", 0, 24), PM, A.add)
+    tt(V("cc", 0, NL), V("jf", 0, NL), V("cr", 0, NL), A.add)
+    turn1("ta", RB, 0)
+    copy(V("cl", 0, NL), V("cc", 0, NL))
+    turn1("ta", RB, 1)
+    ts(V("cl", L_AN, L_D + 3), V("cc", L_AN, L_D + 3), PAR, A.add)
+    copy(bits(V("uuq", 0, 128), dt.uint32), ind(bits(V("uq", 0, 128), dt.uint32), V("uo", 0, 8)))
+    act(V("s1", 1, 192, 2), pick("ta", L_D, 6))
+    act(V("s1", B0 + 3, B0 + 192, 6), pick("ta", L_AN, 2), F.Identity, bias=MID)
+
+    def eyes(lo, hi):
+        for b in range(lo, hi):
+            quant(V("eq", 128 * b, 128 * b + 128), V("ep", 128 * b, 128 * b + 128), V("eye", 3 - b, 515 - b))
+    turn2("tb", RA)
+    eyes(0, 1)
+    quant(V("xq0", 0, H), V("xp0", 0, H), V("xin", 0, 768))
+    quant(V("xq0", H, C), V("xp0", H, C), V("xin", 768, 1536))
+    ts(V("p0", 0, 48), pick("ta", L_D, 3), MID, A.add)
 
     def ahead(t):
-        turn2("tb", RA)
-        if t == 0:
-            quant(V("eq", 0, 128), V("ep", 0, 128), V("eye", 3, 515))
+        if t:
+            turn2("tb", RA)
         tt(V("s1", 0, 192, 2), pick("tb", L_D, 6), V("s1", 1, 192, 2), A.subtract)
-        ts(V("pk%d" % t, 0, 48), pick("tb", L_I, 3), MID, A.add)
+        ts(V("pk%d" % t, 0, 48), pick("tb", L_D, 3), MID, A.add)
+        if t == 0:
+            eyes(1, 4)
         tt(V("w2", 0, 32), pick("tb", L_AN, 2), V("s1", 0, 64, 2), A.subtract)
         tt(V("s1", B0 + 1, B0 + 192, 6), pick("tb", L_AN, 2), V("s1", B0 + 3, B0 + 192, 6), A.subtract)
         ts(V("ni", 0, 24), V("w2", 0, 24), 0.5, A.add, 1.0 / C, A.mult)
@@ -257,21 +251,22 @@ def rank_program(g, core, T, topo):
         mm((4, 6)[h], V("uuq", 0, 128), V("uup", 0, 128), V("xq%d" % t, H * h, H * h + H), V("xp%d" % t, H * h, H * h + H), H)
         act(V("sg", H * h, H * h + H), bank((4, 6)[h], 0, H), F.Sign, bias=-2.0 ** -93)
 
-    P = ("p0", 0)
-    mm(4, V("uuq", 0, 128), V("uup", 0, 128), row("xq0"), row("xp0"), C)
-    act(row("sg"), bank(4), F.Sign, bias=-2.0 ** -93)
+    P = ("p0", 24)
+    signs(0, 0)
+    signs(0, 1)
     for t in range(3):
-        last, NB = t == 2, NBS[t]
+        last = t == 2
         other = T.cores[rank ^ STEP[t]]
         eng = topo.engines(core, other)
-        mask = sum(1 << e for e in eng)
         rid, pnc = topo.addr(other)[:2]
         X, XP = V("xq%d" % t, 0, C), V("xp%d" % t, 0, C)
-        tp, fp, pk, YQ, YP = "tp%d" % t, "fp%d" % t, "pk%d" % t, "yq%d" % t, "yp%d" % t
+        tp, fp, pk, eu, YQ, YP = ["%s%d" % (k, t) for k in ("tp", "fp", "pk", "eu", "yq", "yp")]
         TU, FU, FW, UQ, UP = V(tp, 0, 24), V(fp, 0, 24), V("fw%d" % t, 0, 24), V("zq%d" % t, 0, H), V("zp%d" % t, 0, H)
         cut = (0, LAST if last else H, C)
+        whole = [(b, h) for b in range(2, 4) for h in range(2) if t and (b, h) not in LOOKS[t]]
 
-        def send(dst, src, s):
+        def send(dst, src, s, eng=eng):
+            mask = sum(1 << e for e in eng)
             recs = [e[2] for nm, m in src[0] for e in acc[nm] if e[1] and e[0] & m]
             await_("g", recs)
             g.remote_dma(dst[1], src[1], T.sem[s], T.sem.sent, pnc, rid, mask)
@@ -283,26 +278,38 @@ def rank_program(g, core, T, topo):
         def unpack(b):
             act(V("fh", C * b, C * b + C), bank(b), scale=0.5)
 
-        def twice(k, add):
-            if NB > 2 * k:
-                fb, fh = V("fb", 2 * k * C, min(NB, 2 * k + 2) * C), V("fh", 2 * k * C, min(NB, 2 * k + 2) * C)
-                if add:
-                    emit("g", lambda: g.dma_start(fb[1], fh[1], accum_op=A.add), [fb], [fh, fb], "da%d%d" % (k, t), 16)
-                else:
-                    emit("y", lambda: g.sync.dma_start(fb[1], fh[1]), [fb], [fh], "dc%d%d" % (k, t), 16)
+        def twice():
+            if whole:
+                b, h = whole.pop(0)
+                ts(V("fb", C * b + cut[h], C * b + cut[h + 1]), V("fh", C * b + cut[h], C * b + cut[h + 1]), 2.0, A.mult)
 
         def base(k):
-            if not last:
+            if last:
+                twice()
+            else:
                 copy(*((V("s1", 49, 96, 2), V("so", 49, 96, 2)), (V("s1", 97, 144, 2), ur(R_P)), (ul(R_P), ur(R_P)), (V("s1", B0 + 3, B0 + 144, 6), FU))[k])
+
+        def place(b, h):
+            act(V("gb", C * b + H * h, C * b + H * h + H), ind(V("fh", C * b, C * b + C), V(tp, 24 + 12 * h, 36 + 12 * h)))
 
         def mix(b, h):
             tt(lane("zt", b, H * h, H * h + H), ind(V("fh", C * b, C * b + C), V(fp, 24 + 12 * h, 36 + 12 * h)), V("gb", C * b + H * h, C * b + H * h + H), A.add)
 
+        def pairs():
+            act(V("rr", RA, RA + C), ind(row("a2"), V("ku", 24 * t + 24, 24 * t + 48)))
+
         def table():
+            if t == 1:
+                twice()
             copy(ur(R_E), V("lf%d" % t, 0, 24))
-            base(2)
+            twice()
             turn(row("a2"), V("uu", C, 2 * C))
-            act(row("ef"), ind(row("a2"), FU))
+            if t == 1:
+                pairs()
+                base(3)
+                tt(row("ef"), ind(row("a2"), FU), row("mi"), A.add)
+            else:
+                act(row("ef"), ind(row("a2"), FU))
 
         def layer(b, lo, hi, at):
             mm(at, V("wq", 128 * b, 128 * b + 128), V("wp", 128 * b, 128 * b + 128), V(YQ, lo, hi), V(YP, lo, hi), hi - lo)
@@ -314,19 +321,16 @@ def rank_program(g, core, T, topo):
             else:
                 act(o, bank(at, 0, hi - lo), scale=0.03125)
 
-        def pairs():
-            act(V("rr", RA, RA + C), ind(row("a2"), V("ku", 24 * t + 24, 24 * t + 48)))
-
         def state(b, h):
             lo, hi = cut[h], cut[h + 1]
-            if b < NB:
-                tt(lane("xt", b, lo, hi), ind(V("bb", C * b, C * b + C), V("eu", lo // 16, hi // 16)), V("fb", C * b + lo, C * b + hi), A.add)
+            if (b, h) not in LOOKS[t]:
+                tt(lane("xt", b, lo, hi), ind(V("bb", C * b, C * b + C), V(eu, lo // 16, hi // 16)), V("fb", C * b + lo, C * b + hi), A.add)
             else:
                 tt(lane("xt", b, lo, hi), V("bg", C * b + lo, C * b + hi), bank(b, lo, hi), A.add)
 
         def look(b, h):
             lo, hi = cut[h], cut[h + 1]
-            act(V("bg", C * b + lo, C * b + hi), ind(V("bb", C * b, C * b + C), V("eu", lo // 16, hi // 16)))
+            act(V("bg", C * b + lo, C * b + hi), ind(V("bb", C * b, C * b + C), V(eu, lo // 16, hi // 16)))
 
         def pack(h):
             lo, hi = cut[h], cut[h + 1]
@@ -335,66 +339,67 @@ def rank_program(g, core, T, topo):
         ahead(t)
         for h in range(2):
             act(V("rs", H * h, H * h + H), ind(row("sg"), V(P[0], P[1] + 12 * h, P[1] + 12 * h + 12)), F.Identity, bias=BC, scale=MC)
-        if t == 0:
-            act(ul(R_P), ur(R_P))
-            for b in range(1, 4):
-                quant(V("eq", 128 * b, 128 * b + 128), V("ep", 128 * b, 128 * b + 128), V("eye", 3 - b, 515 - b))
         for h in range(2):
             tt(V("rr", RB + H * h, RB + H * h + H), ind(row("sg"), V(pk, 24 + 12 * h, 36 + 12 * h)), V("rs", H * h, H * h + H), A.add)
-            if h == 0:
-                ts(V("nx", 0, 24), V("ni", 0, 24), float(C), A.mult, -float(C), A.add)
-        tt(V("s0", B0 + 1, B0 + 144, 6), V("nx", 0, 24), V("s1", 0, 48, 2), A.add)
+        ts(V("nx", 0, 24), V("ni", 0, 24), float(C), A.mult, -float(C), A.add)
         for b in range(4):
             mm(b, V("eq", 128 * b, 128 * b + 128), V("ep", 128 * b, 128 * b + 128), X, XP, C)
         unpack(0)
         unpack(1)
-        twice(0, False)
-        turn2("ta", RB)
-        act(V("s1", B0, B0 + 160, 2), pick("ta", L_B, 5), scale=0.5)
+        FB, FH = V("fb", 0, 2 * C), V("fh", 0, 2 * C)
+        if t:
+            emit("y", lambda: g.sync.dma_start(FB[1], FH[1]), [FB], [FH], "dc%d" % t, 16)
+        turn1("ta", RB, 0)
+        if t == 0:
+            copy(ul(R_P), V("s1", 97, 144, 2))
+        turn1("ta", RB, 1)
+        if t == 0:
+            copy(ur(R_N), V("s1", 145, 192, 2))
+        for k, l in ((0, L_B), (2, L_Y), (4, L_Y)):
+            act(V("s1", B0 + k, B0 + 192, 6), pick("ta", l, 2), scale=0.5)
         unpack(2)
-        unpack(3)
-        twice(1, False)
         ts(V("s0", 97, 192, 2), pick("ta", L_AW, 3, C), 0.0, A.is_equal)
-        ts(V("s0", 1, 96, 2), pick("ta", L_AN, 3), 0.0, A.is_equal)
+        ts(V("s0", B0 + 3, B0 + 192, 6), pick("ta", L_AN, 2), 0.0, A.is_equal, 0.5, A.mult)
         scan(V("uu", 0, C, 8), 144, 192)
         scan(V("uu", C + 2, 2 * C, 8), 96, 144)
-        ts(V("s0", B0 + 3, B0 + 192, 6), pick("ta", L_AN, 2), 0.0, A.is_equal, 0.5, A.mult)
+        tt(V("s0", B0 + 1, B0 + 144, 6), V("nx", 0, 24), V("s1", 0, 48, 2), A.add)
         turn(V("wd", 0, C), V("uu", 0, C))
         scan(V("sb", 0, 144), B0, B0 + 144)
-        scan(V("so", 0, 96), 0, 96)
-        ts(V("c2", 0, 24), V("sb", 4, 144, 6), -0.5, A.mult, MID, A.add)
         turn(V("wd", C, 2 * C), V("uu", C, 2 * C))
-        ts(V(tp, 0, 48), V("so", 1, 96, 2), MID, A.add)
+        ts(V("c2", 0, 24), V("sb", 4, 144, 6), -0.5, A.mult, MID, A.add)
+        ts(V("s0", 1, 96, 2), pick("ta", L_AN, 3), 0.0, A.is_equal)
         P = (tp, 24)
         copy(V("rr", RA, RA + H), ind(V("wd", 0, 768), V("c2", 0, 12)))
         act(V("rr", RA + H, RA + C), ind(V("wd", 0, 768), V("c2", 12, 24)))
-        base(0)
+        unpack(3)
+        scan(V("so", 0, 96), 0, 96)
+        base(1)
+        ts(V(tp, 0, 48), V("so", 1, 96, 2), MID, A.add)
         for h in (1, 0):
             for b in range(4):
-                act(V("gb", C * b + H * h, C * b + H * h + H), ind(V("fh", C * b, C * b + C), V(tp, 24 + 12 * h, 36 + 12 * h)))
+                place(b, h)
         turn2("tb", RA)
         copy(FW, V("tb", R_N, C, 16))
+        send(V("lf%d" % t, 0, 24), FW, "af%d" % t, eng if t else eng[::2])
         ts(V(fp, 0, 48), pick("tb", L_D, 3), MID, A.add)
-        send(V("lf%d" % t, 0, 24), FW, "af%d" % t)
         if t:
-            twice(0, True)
+            emit("g", lambda: g.dma_start(FB[1], FH[1], accum_op=A.add), [FB], [FH, FB], "da%d" % t, 16)
         copy(ur(R_F), V("tb", R_N, C, 16))
         for b in range(4):
             mix(b, 1)
-        base(1)
+        base(0)
         quant(UQ, UP, V("zt", 768, 1536))
         send(bits(V(YQ, H, C)), bits(UQ), "aq%d" % t)
         send(V(YP, H, C), UP, "ap%d" % t)
-        if t == 0:
-            twice(0, True)
-        twice(1, True)
         EJ = V("rr", RB, RB + C)
+        base(2)
         if t == 0:
+            base(3)
+        if t == 0:
+            for b in range(2):
+                act(V("fb", C * b, C * b + C), V("fh", C * b, C * b + C), scale=2.0)
             for b in range(4):
                 mix(b, 0)
-            base(3)
-            fill(V("po", 0, 48), MID)
-            emit("y", lambda: g.sync.dma_start(T.pf[:], T.po[:]), [], [V("po", 0, 48)], "pa", 16)
             quant(V(YQ, 0, H), V(YP, 0, H), V("zt", 0, 768))
             emit("v", lambda: g.vector.tensor_copy(ind(EJ, P0)[1], V("wd", 0, C)[1]), [EJ], [V("wd", 0, C), P0])
             for b, at in ((0, 0), (1, 1), (2, 4), (3, 5)):
@@ -402,16 +407,18 @@ def rank_program(g, core, T, topo):
                 cast("s", b, 0, H, at)
             table()
             turn2("ta", RB)
-            ts(V("iv", 0, 32), pick("ta", L_D, 2), MID, A.add)
-            act(EJ, ind(row("ef"), V("iv", 0, 24)))
             for b, at in ((0, 6), (1, 7), (3, 0), (2, 1)):
                 layer(b, H, C, at)
-            cast("v", 0, H, C, 6)
-            cast("v", 1, H, C, 7)
-            turn2("ta", RB)
+            ts(V("iv", 0, 32), pick("ta", L_D, 2), MID, A.add)
+            act(V("rr", RB, RB + H), ind(row("ef"), V("iv", 0, 12)))
+            copy(V("rr", RB + H, RB + C), ind(row("ef"), V("iv", 12, 24)))
+            cast("s", 0, H, C, 6)
             cast("s", 3, H, C, 0)
             cast("s", 2, H, C, 1)
-            ts(V("eu", 0, 32), pick("ta", L_I, 2), MID, A.add)
+            turn2("ta", RB)
+            fill(V("po", 0, 48), MID)
+            ts(V(eu, 0, 32), pick("ta", L_I, 2), MID, A.add)
+            cast("v", 1, H, C, 7)
         else:
             table()
             if last:
@@ -419,42 +426,45 @@ def rank_program(g, core, T, topo):
                 for k, r in enumerate((R_P, R_F)):
                     emit("g", lambda: g.dma_start(T.pf[:, C * k:C * k + C], T.a2[r:128:16, :], accum_op=A.add), [], [row("a2")], "pb", 16)
             act(row("eg"), ind(row("ef"), TU))
-            act(EJ, ind(row("eg"), V("pk2" if last else "iv", 0, 24)))
+            if last:
+                act(V("rr", RB, RB + H), ind(row("eg"), V("eu1", 24, 36)))
+            else:
+                act(EJ, ind(row("eg"), V("iv", 0, 24)))
             for b in range(4):
                 mix(b, 0)
-            base(3)
+            twice()
+            quant(V(YQ, 0, H), V(YP, 0, H), V("zt", 0, 768))
+            if last:
+                copy(V("rr", RB + H, RB + C), ind(row("eg"), V("eu1", 36, 48)))
+            a, z = ((0, H), (H, C)) if last else ((H, C), (0, H))
+            for b, lo, hi, at in ((0, *a, 0), (1, *a, 1), (0, *z, 4), (1, *z, 5), (2, 0, C, 6), (3, 0, C, 7)):
+                layer(b, lo, hi, at)
+            cast("s", 0, *a, 0)
+            cast("s", 1, *a, 1)
+            turn2("ta", RB)
             if last:
                 quant(V("vq", 0, 128), V("vp", 0, 128), V("vin", 0, 512))
-            quant(V(YQ, 0, H), V(YP, 0, H), V("zt", 0, 768))
-            for b, lo, hi, at in ((0, 0, H, 0), (1, 0, H, 1), (0, H, C, 4), (1, H, C, 5), (2, 0, C, 6), (3, 0, C, 7)):
-                layer(b, lo, hi, at)
-            cast("v", 0, 0, H, 0)
-            if last:
-                cast("s", 0, H, C, 4)
+                ts(V(eu, 0, 32), pick("ta", L_I, 2), MID, A.add)
+                cast("v", 0, *z, 4)
             else:
-                pairs()
-            turn2("ta", RB)
-            cast("v", 1, 0, H, 1)
-            ts(V("eu", 0, 32), pick("ta", L_I, 2), MID, A.add)
-            if not last:
-                cast("v", 0, H, C, 4)
-            cast("s", 1, H, C, 5)
+                cast("v", 0, *z, 4)
+                ts(V(eu, 0, 48), pick("ta", L_I, 3), MID, A.add)
+                twice()
+            cast("s", 1, *z, 5)
             cast("s", 2, 0, C, 6)
             cast("s", 3, 0, C, 7)
-            if not last:
-                act(row("x1"), ind(V("wd", 0, C), V("iv", 0, 24)))
-                emit("y", lambda: g.sync.dma_start(T.rr[R_E:128:16, RA:RA + C], T.x1[R_N:128:16, :]), [V("rr", RA, RA + C)], [row("x1")], "dx", 16)
-        for h in range(2):
-            for b in range(NB, 4):
-                look(b, h)
+        for b, h in LOOKS[t]:
+            look(b, h)
         if t == 0:
             pairs()
-        for b, h in ((0, 0), (1, 0), (0, 1), (2, 0), (1, 1)) + (((3, 0),) if last else ((2, 1), (3, 0))):
+            emit("y", lambda: g.sync.dma_start(T.pf[:], T.po[:]), [], [V("po", 0, 48)], "pa", 16)
+            load("g", "v", V("vin", 0, 512), T.v[:])
+        for b, h in ((0, 0), (0, 1), (1, 0), (1, 1), (2, 0), (3, 0)) + (() if last else ((3, 1),)):
             state(b, h)
         if not last:
             pack(0)
             signs(t + 1, 0)
-            state(3, 1)
+            state(2, 1)
             pack(1)
             signs(t + 1, 1)
 
@@ -466,14 +476,13 @@ def rank_program(g, core, T, topo):
         store(T.oc[:, 4 * lo:4 * hi], bits(X))
     finish(0)
     act(V("yo", 0, LAST), bank(4, 0, LAST))
-    store(T.y[:, 0:LAST], V("yo", 0, LAST))
     state(2, 1)
     state(3, 1)
     finish(1)
     for k in range(4):
         store(T.osc[4 * k:4 * k + 4, :], (row("xp3")[0], T.xp3[32 * k:32 * k + 4, :]), "s")
     ts(V("yo", LAST, C), bank(5, 0, C - LAST), 1.0, A.mult)
-    store(T.y[:, LAST:C], V("yo", LAST, C))
+    store(T.y[:], row("yo"))
     for s in count:
         if know["g"].get(s, 0) < count[s]:
             g.wait_ge(T.sem[s], count[s])

@@ -4,34 +4,33 @@ C, H, STEP = 384, 192, [1, 2, 4]
 MID = 192.0
 BF, FL, U16, I32, CODE = "bfloat16", "float32", "uint16", "int32", "float8_e4m3fn_x4"
 T2 = 384
-R_I, R_E, R_N, R_P, R_F = 0, 6, 8, 10, 12
-LOOKS = (((3, 0), (2, 0), (3, 1), (2, 1)), ((3, 0), (3, 1), (2, 1)), ((3, 0), (3, 1), (2, 1)))
-LAST = 192
-L_AW, L_AN, L_B, L_Y, L_I, L_D, NL = 0, 4, 8, 12, 16, 20, 26
+R_E, R_N, R_P, R_F = 6, 8, 10, 12
+CUT = (256, 256, 192)
+L_A, L_I, L_D, L_W, NL, L_F, L_Y = 0, 4, 8, 12, 16, 16, 20
 
 SCRATCH = {"ps": ("psum", [128, 4096], "float32")}
 for _n, _c, _d in (
         [("xin", 1536, BF), ("uin", 512, BF), ("vin", 512, BF), ("pl", C, I32), ("pri", 72, I32), ("sj", 24, I32), ("su", 24, U16)]
         + [("wq", 512, CODE), ("wp", 512, "uint8"), ("uq", 128, CODE), ("up", 128, "uint8"), ("uuq", 128, CODE), ("uup", 128, "uint8")]
         + [("vq", 128, CODE), ("vp", 128, "uint8"), ("eq", 512, CODE), ("ep", 512, "uint8")]
-        + [("one", 516, BF), ("eye", 516, BF), ("uoi", 8, I32), ("uo", 8, U16), ("col", 10, FL)]
-        + [(k, 2, I32) for k in ("pid", "p17", "pmi", "p8", "phi")] + [("jj", NL, I32), ("cl", NL, U16)]
+        + [("one", 516, BF), ("eye", 516, BF), ("uoi", 8, I32), ("uo", 8, U16), ("col", 18, FL)]
+        + [(k, 2, I32) for k in ("pid", "p17", "pmi", "p8", "phi")] + [("jj", NL + 8, I32), ("cl", NL + 8, U16)]
         + [(k, NL, FL) for k in ("jf", "ge", "cc", "cr")]
-        + [(k, 1536, BF) for k in ("fh", "fb", "gb", "bb", "bg", "zt", "xt")]
-        + [(k, C, BF) for k in ("nm", "sg", "rs", "a2", "ef", "eg", "mi")]
-        + [("uu", 768, BF), ("wd", 768, BF), ("rr", 816, BF), ("ta", 800, BF), ("tb", 800, BF)]
-        + [("s0", 384, FL), ("s1", 384, FL), ("so", 96, FL), ("sb", 144, FL), ("w2", 32, FL)]
+        + [(k, 1536, BF) for k in ("fh", "gb", "bb", "bg", "zt", "xt")] + [("fb", 768, BF)]
+        + [(k, C, BF) for k in ("nm", "sg", "rs", "a2", "ef", "eg", "es", "mk", "mi", "lr")]
+        + [("uu", 784, BF), ("wd", 768, BF), ("rr", 816, BF), ("ta", 800, BF), ("tb", 800, BF)]
+        + [("s0", 384, FL), ("s1", 384, FL), ("sw", 192, FL), ("so", 96, FL), ("sb", 144, FL), ("w2", 32, FL)]
         + [("ni", 24, I32), ("nx", 24, FL), ("po", 48, FL), ("yo", C, FL)]
-        + [("ku", 72, U16), ("p0", 48, U16), ("c2", 24, U16), ("iv", 32, U16)]
+        + [("ku", 72, U16), ("p0", 48, U16), ("c2", 24, U16), ("iv", 48, U16)]
         + [("xq%d" % t, C, CODE) for t in range(4)] + [("xp%d" % t, C, "uint8") for t in range(4)]
         + [("%s%d" % (k, t), 48, U16) for k in ("tp", "fp", "pk", "eu") for t in range(3)]
-        + [("%s%d" % (k, t), 24, BF) for k in ("fw", "lf") for t in range(3)]
+        + [("%s%d" % (k, t), 24, BF) for k in ("fw", "lf") for t in range(2)]
         + [("zq%d" % t, H, CODE) for t in range(3)] + [("yq%d" % t, C, CODE) for t in range(3)]
         + [("zp%d" % t, H, "uint8") for t in range(3)] + [("yp%d" % t, C, "uint8") for t in range(3)]):
     SCRATCH[_n] = ("sbuf", [128, _c], _d)
 LOADS = ["x", "u", "v", "pp", "rf", "pr", "wc", "ws"]
-SEMAPHORES = (["qv", "qs", "qt", "qg", "sent", "out", "pa", "pb"] + ["ld_" + k for k in LOADS]
-              + ["%s%d" % (k, t) for k in ("af", "aq", "ap", "dc", "da") for t in range(3)])
+SEMAPHORES = (["qv", "qs", "qt", "qg", "sent", "out", "pa", "pb", "pc"] + ["ld_" + k for k in LOADS]
+              + ["%s%d" % (k, t) for k in ("af", "aq", "ap") for t in range(3)])
 
 
 def rank_program(g, core, T, topo):
@@ -50,6 +49,9 @@ def rank_program(g, core, T, topo):
 
     def lane(name, b, lo, hi):
         return V(name, 4 * lo + b, 4 * hi, 4)
+
+    def part(name, b, lo=0, hi=C):
+        return V(name, C * b + lo, C * b + hi)
 
     def row(name):
         return V(name, 0, C)
@@ -115,6 +117,12 @@ def rank_program(g, core, T, topo):
         kw = {k: x[1] if isinstance(x, tuple) else x for k, x in kw.items()}
         emit("s", lambda: g.scalar.activation(out[1], in_[1], func, **kw), [out], r)
 
+    def scaled(q, out, in_, x):
+        if q == "v":
+            ts(out, in_, x, A.mult)
+        else:
+            act(out, in_, scale=x)
+
     def quant(c, p, in_):
         emit("v", lambda: g.vector.quantize_mx(c[1], p[1], in_[1]), [c, p], [in_])
 
@@ -128,20 +136,20 @@ def rank_program(g, core, T, topo):
     def store(ap, in_, q="y"):
         emit(q, lambda: queue[q].dma_start(ap, in_[1]), [], [in_], "out", 16)
 
-    def iota(out, pattern, base, cmul, flag=False):
+    def iota(out, pattern, base, cmul=0, flag=False):
         emit("g", lambda: g.iota(out[1], pattern, base, cmul, allow_small_or_imprecise_dtypes=flag), [out], [])
 
     def turn(out, in_):
         emit("v", lambda: g.vector.transpose(out[1], in_[1]), [out], [in_])
 
-    def scan(out, lo, hi):
-        a, b = V("s0", lo, hi), V("s1", lo, hi)
-        emit("v", lambda: g.vector.tensor_tensor_scan(out[1], a[1], b[1], 0.0, A.mult, A.add), [out], [a, b])
+    def scan(out, a, b, first=0.0):
+        emit("v", lambda: g.vector.tensor_tensor_scan(out[1], a[1], b[1], first, A.mult, A.add), [out], [a, b])
 
     def bank(b, lo=0, hi=C):
         return V("ps", 512 * b + lo, 512 * b + hi)
 
     RA, RB = 16, 416
+    UL, UR = 16, 400
 
     def turn1(to, r, k):
         if k == 0:
@@ -156,14 +164,28 @@ def rank_program(g, core, T, topo):
     def pick(tile, lo, n, wide=800):
         return ind(V(tile, 0, wide), V("cl", lo, lo + n))
 
-    def ur(r):
-        return V("uu", C + r, 2 * C, 16)
+    def offsets(name, tile, lo, n):
+        ts(V(name, 0, 16 * n), pick(tile, lo, n), MID, A.add)
+
+    def halves(r, win, off, at):
+        act(V("rr", r, r + H), ind(win, V(off, at, at + 12)))
+        copy(V("rr", r + H, r + C), ind(win, V(off, at + 12, at + 24)))
 
     def ul(r):
-        return V("uu", r, C, 16)
+        return V("uu", UL + r, UL + C, 16)
 
-    PM, MC, BC, P24, PH, UX, PAR, MS, MB = [V("col", k, k + 1) for k in range(9)]
+    def ur(r):
+        return V("uu", UR + r, UR + C, 16)
+
+    def eyes(*bs):
+        for b in bs:
+            quant(V("eq", 128 * b, 128 * b + 128), V("ep", 128 * b, 128 * b + 128), V("eye", 3 - b, 515 - b))
+
+    PM, MC, BC, P24, PH, UX, PAR, MS, MB, MW, SG, QA, QB, QC, QF, QY, PA, PB = [V("col", k, k + 1) for k in range(18)]
     B0 = 192
+
+    def terms(k, n=144, step=6):
+        return V("s1", B0 + k, B0 + n, step)
 
     ONE, EYE, NM, PL = V("one", 0, 516), V("eye", 0, 516), row("nm"), row("pl")
     load("s", "u", V("uin", 0, 512), T.u[:])
@@ -175,95 +197,111 @@ def rank_program(g, core, T, topo):
     await_("y", [e[2] for e in acc["xin"]])
     load("y", "wc", bits(V("wq", 0, 512)), T.wc[:])
     load("y", "ws", V("wp", 0, 512), T.ws[:])
-    iota(V("pid", 0, 2), [[0, 2]], 0, 1)
-    iota(V("p17", 0, 2), [[0, 2]], 0, 17)
-    iota(V("sj", 0, 24), [[1, 24]], 0, 0)
+
     fill(ONE, 1.0)
-    iota(V("jj", L_AW, L_AN), [[256, 4]], R_F, 0)
-    iota(V("jj", L_AN, L_I), [[1, 3], [256, 4]], R_F, 0)
-    iota(V("jj", L_I, L_D), [[256, 4]], R_E, 0)
-    iota(V("jj", L_D, L_D + 6), [[R_P - R_N, 2], [256, 3]], R_N, 0)
-    iota(V("uoi", 0, 8), [[16, 8]], 0, 0)
-    emit("g", lambda: g.affine_select(EYE[1], ONE[1], [[-1, 516]], A.is_equal, 0.0, 3, 4), [EYE], [ONE])
+    iota(V("pid", 0, 1), [[0, 1]], 0, 1)
+    iota(V("pid", 1, 2), [[0, 1]], 0, 128)
+    iota(V("sj", 0, 24), [[1, 24]], 0)
+    iota(V("p17", 0, 2), [[0, 2]], 0, 17)
+    iota(V("jj", L_I, NL), [[2, 3], [256, 4]], R_E)
+    iota(V("jj", L_A, L_I), [[256, 4]], R_F)
+    iota(V("uoi", 0, 8), [[16, 8]], 0)
     for lo in (400, 800, 0):
         iota(V("rr", lo, lo + 16), [[0, 16]], 0, 0, True)
-    iota(V("uu", 0, 2 * C), [[0, 2 * C]], 0, 0, True)
-    ts(V("pmi", 0, 2), V("pid", 0, 2), 15, A.bitwise_and)
-    ts(V("p8", 0, 2), V("pid", 0, 2), 7, A.bitwise_and)
-    emit("v", lambda: g.vector.tensor_tensor_scan(NM[1], row("one")[1], row("one")[1], -MID - 1, A.mult, A.add), [NM], [row("one")])
+    emit("g", lambda: g.affine_select(EYE[1], ONE[1], [[-1, 516]], A.is_equal, 0.0, 3, 4), [EYE], [ONE])
+    iota(V("sw", 0, 192), [[0, 192]], 0, 0, True)
+    iota(V("jj", L_F, L_F + 8), [[14, 2], [128, 4]], 0)
+    iota(V("uu", 0, UR + C), [[0, UR + C]], 0, 0, True)
+    iota(V("s0", 0, 96, 2), [[0, 48]], 0, 0, True)
+    for name, k, x in (("s0", 0, 0), ("s0", 2, 1), ("s0", 3, 1), ("s0", 5, -1), ("s1", 3, 0)):
+        iota(V(name, B0 + k, B0 + 144, 6), [[0, 24]], x, 0, True)
+    ts(V("pmi", 0, 2), V("pid", 0, 2), 15 + 128 * 7, A.bitwise_and)
+    ts(V("p8", 0, 2), V("pid", 0, 2), 18 + 128 * 14, A.bitwise_and)
+    scan(NM, row("one"), row("one"), -MID - 1)
     ts(PM, V("pmi", 0, 1), -13.0, A.add)
-    ts(MS, V("p8", 0, 1), 0.0, A.is_equal)
+    ts(MS, V("pmi", 1, 2), 0.0, A.is_equal)
     ts(P24, V("pmi", 0, 1), 24.0, A.mult)
-    ts(MB, PM, R_N - 12.5, A.is_gt, -MID, A.mult)
     ts(PH, V("pmi", 0, 1), 16.0, A.mult)
-    act(V("s0", 0, B0 + 144), V("one", 0, B0 + 144), scale=0.0)
+    ts(MB, PM, R_N - 12.5, A.is_gt, -MID, A.mult)
+    act(QC, PM, F.Identity, scale=1 / 32, bias=13 / 32)
+    act(MC, PM, F.Relu, scale=768.0, bias=1.0)
     act(row("mi"), NM, F.Identity, scale=MS, bias=MB)
-    ts(V("su", 0, 24), V("sj", 0, 24), P24, A.add)
     ts(V("phi", 0, 2), V("p17", 0, 2), 4, A.arith_shift_right, 1, A.bitwise_and)
-    ts(V("jf", 0, NL), V("jj", 0, NL), PH, A.add)
     ts(UX, PM, -0.5, A.is_gt)
-    ts(PAR, V("phi", 0, 1), T2 + 16.0, A.mult)
-    ts(V("ge", 0, NL), V("jf", 0, NL), C - 0.5, A.is_gt)
+    ts(V("jf", 0, NL), V("jj", 0, NL), PH, A.add)
+    ts(V("su", 0, 24), V("sj", 0, 24), P24, A.add)
+    copy(V("col", 16, 18), V("p8", 0, 2))
     ts(V("uo", 0, 8), V("uoi", 0, 8), UX, A.add)
-    ts(MC, PM, 768.0, A.mult, -1.0, A.max)
-    for lo, hi, step in ((L_AW, L_I, 0), (L_I, L_D, R_I - R_E), (L_D, L_D + 3, R_P - R_N), (L_D + 3, NL, R_N - R_P)):
+    ts(V("ge", 0, NL), V("jf", 0, NL), C - 0.5, A.is_gt)
+    ts(PAR, V("phi", 0, 1), T2 + 16.0, A.mult)
+    act(MC, MC, F.Abs, bias=-1.0)
+    act(MW, MS, F.Identity, scale=-1.0, bias=1.0)
+    act(QC, QC, scale=MS)
+    for lo, hi, step in ((L_A, L_I, 0), (L_I, L_W, R_P - R_N), (L_W, NL, R_N - R_P)):
         act(V("cr", lo, hi), V("ge", lo, hi), scale=float(step - C))
-    act(V("s1", B0, 384), V("one", 0, 192), scale=0.0)
-    act(V("s0", B0 + 2, B0 + 144, 6), V("one", 0, 24), scale=2.0)
-    act(V("s0", B0 + 4, B0 + 144, 6), V("one", 0, 24), scale=-2.0)
-    ts(BC, PM, 0.0, A.is_equal, -1.0, A.mult)
-    A2, P0, rows = V("rr", RB, RB + C), V("p0", 24, 48), ind(PL, V("su", 0, 24))
+    act(MC, MC, F.Identity, scale=MW, bias=QC)
+    act(QA, PA, F.Identity, scale=-(T2 + 16) / 32, bias=18 * (T2 + 16) / 32)
+    act(QB, PA, scale=QA)
+
+    A2, rows = V("rr", RB, RB + C), ind(PL, V("su", 0, 24))
+    quant(V("uq", 0, 128), V("up", 0, 128), V("uin", 0, 512))
     tt(A2, (rows[0] + [("rows", 3)], rows[1]), row("mi"), A.add)
     copy(V("ku", 0, 72), V("pri", 0, 72))
-    quant(V("uq", 0, 128), V("up", 0, 128), V("uin", 0, 512))
     act(V("rr", RA, RA + C), ind(A2, V("ku", 0, 24)))
+    act(QF, PB, F.Identity, scale=9 / 128, bias=QB)
     act(V("uup", 0, 128), ind(V("up", 0, 128), V("uo", 0, 8)))
+    act(BC, MC, F.Sign, bias=-0.5)
     tt(V("cc", 0, NL), V("jf", 0, NL), V("cr", 0, NL), A.add)
-    turn1("ta", RB, 0)
-    copy(V("cl", 0, NL), V("cc", 0, NL))
-    turn1("ta", RB, 1)
-    ts(V("cl", L_AN, L_D + 3), V("cc", L_AN, L_D + 3), PAR, A.add)
     copy(bits(V("uuq", 0, 128), dt.uint32), ind(bits(V("uq", 0, 128), dt.uint32), V("uo", 0, 8)))
-    act(V("s1", 1, 192, 2), pick("ta", L_D, 6))
-    act(V("s1", B0 + 3, B0 + 192, 6), pick("ta", L_AN, 2), F.Identity, bias=MID)
-
-    def eyes(lo, hi):
-        for b in range(lo, hi):
-            quant(V("eq", 128 * b, 128 * b + 128), V("ep", 128 * b, 128 * b + 128), V("eye", 3 - b, 515 - b))
+    copy(V("cl", L_W, NL), V("cc", L_W, NL))
+    eyes(0)
+    ts(V("cl", L_A, L_W), V("cc", L_A, L_W), PAR, A.add)
+    turn2("ta", RB)
+    act(terms(4, 192), pick("ta", L_A, 2), F.Identity, bias=MID)
+    act(V("s1", 1, 96, 2), pick("ta", L_D, 3))
+    act(SG, MS, F.Identity, bias=-2.0 ** -93)
+    act(BC, BC, F.Identity, scale=0.5, bias=-0.5)
+    act(V("sw", 3, 192, 4), pick("ta", L_W, 3, C))
     turn2("tb", RA)
-    eyes(0, 1)
-    quant(V("xq0", 0, H), V("xp0", 0, H), V("xin", 0, 768))
-    quant(V("xq0", H, C), V("xp0", H, C), V("xin", 768, 1536))
-    ts(V("p0", 0, 48), pick("ta", L_D, 3), MID, A.add)
-
-    def ahead(t):
-        if t:
-            turn2("tb", RA)
-        tt(V("s1", 0, 192, 2), pick("tb", L_D, 6), V("s1", 1, 192, 2), A.subtract)
-        ts(V("pk%d" % t, 0, 48), pick("tb", L_D, 3), MID, A.add)
-        if t == 0:
-            eyes(1, 4)
-        tt(V("w2", 0, 32), pick("tb", L_AN, 2), V("s1", 0, 64, 2), A.subtract)
-        tt(V("s1", B0 + 1, B0 + 192, 6), pick("tb", L_AN, 2), V("s1", B0 + 3, B0 + 192, 6), A.subtract)
-        ts(V("ni", 0, 24), V("w2", 0, 24), 0.5, A.add, 1.0 / C, A.mult)
 
     def signs(t, h):
-        mm((4, 6)[h], V("uuq", 0, 128), V("uup", 0, 128), V("xq%d" % t, H * h, H * h + H), V("xp%d" % t, H * h, H * h + H), H)
-        act(V("sg", H * h, H * h + H), bank((4, 6)[h], 0, H), F.Sign, bias=-2.0 ** -93)
+        lo, hi = (0, CUT[t - 1] if t else H, C)[h:h + 2]
+        mm((4, 6)[h], V("uuq", 0, 128), V("uup", 0, 128), V("xq%d" % t, lo, hi), V("xp%d" % t, lo, hi), hi - lo)
+        act(V("sg", lo, hi), bank((4, 6)[h], 0, hi - lo), F.Sign, scale=MW, bias=SG)
 
-    P = ("p0", 24)
-    signs(0, 0)
-    signs(0, 1)
+    ahead = {
+        "wide": lambda: tt(V("sw", 0, 192, 4), pick("tb", L_W, 3, C), V("sw", 3, 192, 4), A.subtract),
+        "pair": lambda: tt(V("s1", 0, 96, 2), pick("tb", L_D, 3), V("s1", 1, 96, 2), A.subtract),
+        "sum": lambda: tt(V("w2", 0, 32), pick("tb", L_A, 2), V("s1", 0, 64, 2), A.subtract),
+        "refs": lambda: tt(terms(1, 192), pick("tb", L_A, 2), terms(4, 192), A.subtract),
+        "turns": lambda: ts(V("ni", 0, 24), V("w2", 0, 24), 0.5, A.add, 1.0 / C, A.mult),
+        "less": lambda: ts(V("nx", 0, 24), V("ni", 0, 24), -float(C), A.mult, float(C), A.add),
+        "rest": lambda: tt(terms(0), V("nx", 0, 24), V("s1", 0, 48, 2), A.subtract)}
+    for h in range(2):
+        quant(V("xq0", H * h, H * h + H), V("xp0", H * h, H * h + H), V("xin", 768 * h, 768 * h + 768))
+        signs(0, h)
+    act(QY, PB, F.Identity, scale=8 / 128, bias=QB)
+    ahead["pair"]()
+    offsets("p0", "ta", L_D, 3)
+    offsets("pk0", "tb", L_D, 3)
+    ahead["sum"]()
+    eyes(1)
+    ts(V("cl", L_F, L_F + 4), V("jj", L_F, L_F + 4), QF, A.add, PM, A.subtract)
+    eyes(2)
+    for k in ("turns", "wide", "less", "refs"):
+        ahead[k]()
+
     for t in range(3):
         last = t == 2
         other = T.cores[rank ^ STEP[t]]
         eng = topo.engines(core, other)
         rid, pnc = topo.addr(other)[:2]
-        X, XP = V("xq%d" % t, 0, C), V("xp%d" % t, 0, C)
         tp, fp, pk, eu, YQ, YP = ["%s%d" % (k, t) for k in ("tp", "fp", "pk", "eu", "yq", "yp")]
-        TU, FU, FW, UQ, UP = V(tp, 0, 24), V(fp, 0, 24), V("fw%d" % t, 0, 24), V("zq%d" % t, 0, H), V("zp%d" % t, 0, H)
-        cut = (0, LAST if last else H, C)
-        whole = [(b, h) for b in range(2, 4) for h in range(2) if t and (b, h) not in LOOKS[t]]
+        P = "tp%d" % (t - 1) if t else "p0"
+        TU, FU, UQ, UP = V(tp, 0, 24), V(fp, 0, 24), V("zq%d" % t, 0, H), V("zp%d" % t, 0, H)
+        WD, FR, EJ = V("wd", 0, 2 * C), V("rr", RA, RA + C), V("rr", RB, RB + C)
+        cut = (0, CUT[t], C)
+        at = ((0, 1, 4, 5), (6, 7, 1, 0)) if t == 0 else ((4, 5, 6, 7), (0, 1, 6, 7))
 
         def send(dst, src, s, eng=eng):
             mask = sum(1 << e for e in eng)
@@ -275,213 +313,218 @@ def rank_program(g, core, T, topo):
             for nm, m in dst[0]:
                 acc.setdefault(nm, []).append((m, True, (s, len(eng), {s: len(eng)})))
 
-        def unpack(b):
-            act(V("fh", C * b, C * b + C), bank(b), scale=0.5)
+        def unpack(b, lo=0, hi=C):
+            act(part("fh", b, lo, hi), bank(b, lo, hi), scale=0.5)
 
-        def twice():
-            if whole:
-                b, h = whole.pop(0)
-                ts(V("fb", C * b + cut[h], C * b + cut[h + 1]), V("fh", C * b + cut[h], C * b + cut[h + 1]), 2.0, A.mult)
+        def twice(b, h):
+            ts(part("fb", b, cut[h], cut[h + 1]), part("fh", b, cut[h], cut[h + 1]), 2.0, A.mult)
 
-        def base(k):
-            if last:
-                twice()
-            else:
-                copy(*((V("s1", 49, 96, 2), V("so", 49, 96, 2)), (V("s1", 97, 144, 2), ur(R_P)), (ul(R_P), ur(R_P)), (V("s1", B0 + 3, B0 + 144, 6), FU))[k])
+        def place(h, *bs):
+            for b in bs:
+                act(part("gb", b, H * h, H * h + H), ind(part("fh", b), V(tp, 24 + 12 * h, 36 + 12 * h)))
 
-        def place(b, h):
-            act(V("gb", C * b + H * h, C * b + H * h + H), ind(V("fh", C * b, C * b + C), V(tp, 24 + 12 * h, 36 + 12 * h)))
+        def mix(h, *bs):
+            for b in bs:
+                tt(lane("zt", b, H * h, H * h + H), ind(part("fh", b), V(fp, 24 + 12 * h, 36 + 12 * h)), part("gb", b, H * h, H * h + H), A.add)
 
-        def mix(b, h):
-            tt(lane("zt", b, H * h, H * h + H), ind(V("fh", C * b, C * b + C), V(fp, 24 + 12 * h, 36 + 12 * h)), V("gb", C * b + H * h, C * b + H * h + H), A.add)
+        def lower():
+            quant(V(YQ, 0, H), V(YP, 0, H), V("zt", 0, 768))
 
-        def pairs():
-            act(V("rr", RA, RA + C), ind(row("a2"), V("ku", 24 * t + 24, 24 * t + 48)))
+        def layer(h, *bs):
+            for b in bs:
+                lo, hi = (0, C) if h == 2 else (H * h, H * h + H)
+                mm(at[h % 2][b], V("wq", 128 * b, 128 * b + 128), V("wp", 128 * b, 128 * b + 128), V(YQ, lo, hi), V(YP, lo, hi), hi - lo)
+
+        def cast(q, h, *bs):
+            for b in bs:
+                lo, hi = (0, C) if h == 2 else (H * h, H * h + H)
+                scaled(q, part("bb", b, lo, hi), bank(at[h % 2][b], 0, hi - lo), 0.03125)
 
         def table():
-            if t == 1:
-                twice()
-            copy(ur(R_E), V("lf%d" % t, 0, 24))
-            twice()
-            turn(row("a2"), V("uu", C, 2 * C))
-            if t == 1:
-                pairs()
-                base(3)
-                tt(row("ef"), ind(row("a2"), FU), row("mi"), A.add)
-            else:
-                act(row("ef"), ind(row("a2"), FU))
+            act(ur(R_E), V("lf%d" % t, 0, 24))
 
-        def layer(b, lo, hi, at):
-            mm(at, V("wq", 128 * b, 128 * b + 128), V("wp", 128 * b, 128 * b + 128), V(YQ, lo, hi), V(YP, lo, hi), hi - lo)
+        def pairs():
+            act(FR, ind(row("a2"), V("ku", 24 * t + 24, 24 * t + 48)))
 
-        def cast(q, b, lo, hi, at):
-            o = V("bb", C * b + lo, C * b + hi)
-            if q == "v":
-                ts(o, bank(at, 0, hi - lo), 0.03125, A.mult)
-            else:
-                act(o, bank(at, 0, hi - lo), scale=0.03125)
-
-        def state(b, h):
-            lo, hi = cut[h], cut[h + 1]
-            if (b, h) not in LOOKS[t]:
-                tt(lane("xt", b, lo, hi), ind(V("bb", C * b, C * b + C), V(eu, lo // 16, hi // 16)), V("fb", C * b + lo, C * b + hi), A.add)
-            else:
-                tt(lane("xt", b, lo, hi), V("bg", C * b + lo, C * b + hi), bank(b, lo, hi), A.add)
-
-        def look(b, h):
-            lo, hi = cut[h], cut[h + 1]
-            act(V("bg", C * b + lo, C * b + hi), ind(V("bb", C * b, C * b + C), V(eu, lo // 16, hi // 16)))
+        def add(b, h):
+            tt(lane("xt", b, cut[h], cut[h + 1]), part("bg", b, cut[h], cut[h + 1]), bank(b, cut[h], cut[h + 1]), A.add)
 
         def pack(h):
             lo, hi = cut[h], cut[h + 1]
             quant(V("xq%d" % (t + 1), lo, hi), V("xp%d" % (t + 1), lo, hi), V("xt", 4 * lo, 4 * hi))
 
-        ahead(t)
-        for h in range(2):
-            act(V("rs", H * h, H * h + H), ind(row("sg"), V(P[0], P[1] + 12 * h, P[1] + 12 * h + 12)), F.Identity, bias=BC, scale=MC)
-        for h in range(2):
-            tt(V("rr", RB + H * h, RB + H * h + H), ind(row("sg"), V(pk, 24 + 12 * h, 36 + 12 * h)), V("rs", H * h, H * h + H), A.add)
-        ts(V("nx", 0, 24), V("ni", 0, 24), float(C), A.mult, -float(C), A.add)
+        base = (lambda f: f(V("s1", 49, 96, 2), V("so", 49, 96, 2)), lambda f: f(V("sw", 3, 96, 4), ur(R_P)),
+                lambda f: f(terms(4), FU), lambda f: f(ul(R_P), ur(R_P)))
+
+        for lo in range(0, C, 128):
+            act(V("rs", lo, lo + 128), ind(row("sg"), V(P, 24 + lo // 16, 32 + lo // 16)), F.Identity, bias=BC, scale=MC)
+        for lo in range(0, C, 128):
+            tt(V("rr", RB + lo, RB + lo + 128), ind(row("sg"), V(pk, 24 + lo // 16, 32 + lo // 16)), V("rs", lo, lo + 128), A.add)
+        if t:
+            ahead["less"]()
+        else:
+            eyes(3)
+            ts(V("cl", L_Y, L_Y + 4), V("jj", L_Y, L_Y + 4), QY, A.add)
+            act(ul(R_P), V("sw", 3, 96, 4))
         for b in range(4):
-            mm(b, V("eq", 128 * b, 128 * b + 128), V("ep", 128 * b, 128 * b + 128), X, XP, C)
+            mm(b, V("eq", 128 * b, 128 * b + 128), V("ep", 128 * b, 128 * b + 128), row("xq%d" % t), row("xp%d" % t), C)
         unpack(0)
         unpack(1)
-        FB, FH = V("fb", 0, 2 * C), V("fh", 0, 2 * C)
-        if t:
-            emit("y", lambda: g.sync.dma_start(FB[1], FH[1]), [FB], [FH], "dc%d" % t, 16)
-        turn1("ta", RB, 0)
         if t == 0:
-            copy(ul(R_P), V("s1", 97, 144, 2))
-        turn1("ta", RB, 1)
-        if t == 0:
-            copy(ur(R_N), V("s1", 145, 192, 2))
-        for k, l in ((0, L_B), (2, L_Y), (4, L_Y)):
-            act(V("s1", B0 + k, B0 + 192, 6), pick("ta", l, 2), scale=0.5)
+            act(ur(R_N), V("sw", 99, 192, 4))
+        turn2("ta", RB)
+        act(V("s0", B0 + 1, B0 + 144, 3), pick("ta", L_F, 3), F.Abs, scale=0.5)
+        act(terms(2, 144, 3), pick("ta", L_Y, 3), scale=0.25)
         unpack(2)
-        ts(V("s0", 97, 192, 2), pick("ta", L_AW, 3, C), 0.0, A.is_equal)
-        ts(V("s0", B0 + 3, B0 + 192, 6), pick("ta", L_AN, 2), 0.0, A.is_equal, 0.5, A.mult)
-        scan(V("uu", 0, C, 8), 144, 192)
-        scan(V("uu", C + 2, 2 * C, 8), 96, 144)
-        tt(V("s0", B0 + 1, B0 + 144, 6), V("nx", 0, 24), V("s1", 0, 48, 2), A.add)
-        turn(V("wd", 0, C), V("uu", 0, C))
-        scan(V("sb", 0, 144), B0, B0 + 144)
-        turn(V("wd", C, 2 * C), V("uu", C, 2 * C))
-        ts(V("c2", 0, 24), V("sb", 4, 144, 6), -0.5, A.mult, MID, A.add)
-        ts(V("s0", 1, 96, 2), pick("ta", L_AN, 3), 0.0, A.is_equal)
-        P = (tp, 24)
-        copy(V("rr", RA, RA + H), ind(V("wd", 0, 768), V("c2", 0, 12)))
-        act(V("rr", RA + H, RA + C), ind(V("wd", 0, 768), V("c2", 12, 24)))
-        unpack(3)
-        scan(V("so", 0, 96), 0, 96)
-        base(1)
-        ts(V(tp, 0, 48), V("so", 1, 96, 2), MID, A.add)
-        for h in (1, 0):
-            for b in range(4):
-                place(b, h)
-        turn2("tb", RA)
-        copy(FW, V("tb", R_N, C, 16))
-        send(V("lf%d" % t, 0, 24), FW, "af%d" % t, eng if t else eng[::2])
-        ts(V(fp, 0, 48), pick("tb", L_D, 3), MID, A.add)
+        unpack(3, 0, H)
+        if t == 0:
+            ahead["rest"]()
+        scan(V("uu", UL + R_N - 12, UL + R_N + 372, 4), V("ta", 0, C, 4), V("sw", 96, 192))
+        scan(V("uu", UR + R_P - 12, UR + R_P + 372, 4), V("ta", 0, C, 4), V("sw", 0, 96))
+        ts(V("s0", 1, 96, 2), pick("ta", L_A, 3), 0.0, A.not_equal)
         if t:
-            emit("g", lambda: g.dma_start(FB[1], FH[1], accum_op=A.add), [FB], [FH, FB], "da%d" % t, 16)
-        copy(ur(R_F), V("tb", R_N, C, 16))
-        for b in range(4):
-            mix(b, 1)
-        base(0)
+            ahead["rest"]()
+        turn(V("wd", 0, C), V("uu", UL, UL + C))
+        scan(V("sb", 0, 144), V("s0", B0, B0 + 144), V("s1", B0, B0 + 144))
+        turn(V("wd", C, 2 * C), V("uu", UR, UR + C))
+        ts(V("c2", 0, 24), V("sb", 5, 144, 6), -1.0, A.mult, MID, A.add)
+        scan(V("so", 0, 96), V("s0", 0, 96), V("s1", 0, 96))
+        halves(RA, WD, "c2", 0)
+        unpack(3, H, C)
+        ts(V(tp, 0, 48), V("so", 1, 96, 2), MID, A.add)
+        place(1, 0, 1, 2, 3)
+        place(0, 0, 1, 2)
+        if last:
+            place(0, 3)
+            send(row("lr"), FR, "af2")
+            g.wait_ge(T.sem.pa, 16)
+            emit("g", lambda: g.dma_start(T.pf[:, 0:C], T.wd[R_P:128:16, C:2 * C], accum_op=A.add), [], [V("wd", C, 2 * C)], "pb", 16)
+            emit("g", lambda: g.dma_start(T.pf[:, C:2 * C], T.rr[R_N:128:16, RA:RA + C], accum_op=A.add), [], [FR], "pb", 16)
+            twice(0, 0)
+            turn2("tb", RA)
+            offsets(fp, "tb", L_D, 3)
+            quant(V("vq", 0, 128), V("vp", 0, 128), V("vin", 0, 512))
+            mix(1, 0, 1, 2, 3)
+            twice(0, 1)
+        else:
+            FW = V("fw%d" % t, 0, 24)
+            turn2("tb", RA)
+            copy(FW, V("tb", R_N, C, 16))
+            send(V("lf%d" % t, 0, 24), FW, "af%d" % t, eng if t else eng[::2])
+            if t:
+                base[1](copy)
+                offsets(fp, "tb", L_D, 3)
+                copy(ur(R_F), V("tb", R_N, C, 16))
+                mix(1, 0, 1, 2, 3)
+                base[0](copy)
+            else:
+                offsets(fp, "tb", L_D, 3)
+                emit("y", lambda: g.sync.dma_start(T.rr[R_P:128:16, RA:RA + C], T.nm[R_P:128:16, :]), [FR], [NM], "pc", 16)
+                base[1](copy)
+                mix(1, 0, 1, 2, 3)
+                base[2](copy)
+                copy(ur(R_F), V("tb", R_N, C, 16))
         quant(UQ, UP, V("zt", 768, 1536))
         send(bits(V(YQ, H, C)), bits(UQ), "aq%d" % t)
         send(V(YP, H, C), UP, "ap%d" % t)
-        EJ = V("rr", RB, RB + C)
-        base(2)
         if t == 0:
-            base(3)
-        if t == 0:
+            place(0, 3)
+            base[3](act)
+            act(row("mk"), row("one"), scale=MS)
+            base[0](act)
             for b in range(2):
-                act(V("fb", C * b, C * b + C), V("fh", C * b, C * b + C), scale=2.0)
-            for b in range(4):
-                mix(b, 0)
-            quant(V(YQ, 0, H), V(YP, 0, H), V("zt", 0, 768))
-            emit("v", lambda: g.vector.tensor_copy(ind(EJ, P0)[1], V("wd", 0, C)[1]), [EJ], [V("wd", 0, C), P0])
-            for b, at in ((0, 0), (1, 1), (2, 4), (3, 5)):
-                layer(b, 0, H, at)
-                cast("s", b, 0, H, at)
+                act(part("fb", b), part("fh", b), scale=2.0)
+            mix(0, 0, 1, 2, 3)
+            lower()
+            layer(0, 0, 1, 2, 3)
+            emit("v", lambda: g.vector.tensor_copy(ind(EJ, V(tp, 24, 48))[1], FR[1]), [EJ], [FR, V(tp, 24, 48)])
+            cast("s", 0, 0, 1, 2, 3)
             table()
             turn2("ta", RB)
-            for b, at in ((0, 6), (1, 7), (3, 0), (2, 1)):
-                layer(b, H, C, at)
-            ts(V("iv", 0, 32), pick("ta", L_D, 2), MID, A.add)
-            act(V("rr", RB, RB + H), ind(row("ef"), V("iv", 0, 12)))
-            copy(V("rr", RB + H, RB + C), ind(row("ef"), V("iv", 12, 24)))
-            cast("s", 0, H, C, 6)
-            cast("s", 3, H, C, 0)
-            cast("s", 2, H, C, 1)
-            turn2("ta", RB)
+            turn(row("a2"), V("uu", UR, UR + C))
+            offsets("iv", "ta", L_D, 3)
             fill(V("po", 0, 48), MID)
-            ts(V(eu, 0, 32), pick("ta", L_I, 2), MID, A.add)
-            cast("v", 1, H, C, 7)
-        else:
-            table()
-            if last:
-                g.wait_ge(T.sem.pa, 16)
-                for k, r in enumerate((R_P, R_F)):
-                    emit("g", lambda: g.dma_start(T.pf[:, C * k:C * k + C], T.a2[r:128:16, :], accum_op=A.add), [], [row("a2")], "pb", 16)
-            act(row("eg"), ind(row("ef"), TU))
-            if last:
-                act(V("rr", RB, RB + H), ind(row("eg"), V("eu1", 24, 36)))
-            else:
-                act(EJ, ind(row("eg"), V("iv", 0, 24)))
-            for b in range(4):
-                mix(b, 0)
-            twice()
-            quant(V(YQ, 0, H), V(YP, 0, H), V("zt", 0, 768))
-            if last:
-                copy(V("rr", RB + H, RB + C), ind(row("eg"), V("eu1", 36, 48)))
-            a, z = ((0, H), (H, C)) if last else ((H, C), (0, H))
-            for b, lo, hi, at in ((0, *a, 0), (1, *a, 1), (0, *z, 4), (1, *z, 5), (2, 0, C, 6), (3, 0, C, 7)):
-                layer(b, lo, hi, at)
-            cast("s", 0, *a, 0)
-            cast("s", 1, *a, 1)
-            turn2("ta", RB)
-            if last:
-                quant(V("vq", 0, 128), V("vp", 0, 128), V("vin", 0, 512))
-                ts(V(eu, 0, 32), pick("ta", L_I, 2), MID, A.add)
-                cast("v", 0, *z, 4)
-            else:
-                cast("v", 0, *z, 4)
-                ts(V(eu, 0, 48), pick("ta", L_I, 3), MID, A.add)
-                twice()
-            cast("s", 1, *z, 5)
-            cast("s", 2, 0, C, 6)
-            cast("s", 3, 0, C, 7)
-        for b, h in LOOKS[t]:
-            look(b, h)
-        if t == 0:
-            pairs()
             emit("y", lambda: g.sync.dma_start(T.pf[:], T.po[:]), [], [V("po", 0, 48)], "pa", 16)
             load("g", "v", V("vin", 0, 512), T.v[:])
-        for b, h in ((0, 0), (0, 1), (1, 0), (1, 1), (2, 0), (3, 0)) + (() if last else ((3, 1),)):
-            state(b, h)
+            layer(1, 0, 1, 3, 2)
+            halves(RB, row("a2"), "iv", 0)
+            pairs()
+            cast("s", 1, 0, 3, 2)
+            turn2("ta", RB)
+            offsets(eu, "ta", L_I, 2)
+            cast("v", 1, 1)
+        elif t == 1:
+            mix(0, 0)
+            table()
+            place(0, 3)
+            turn(row("a2"), V("uu", UR, UR + C))
+            act(row("ef"), ind(row("a2"), FU), F.Identity, scale=MW, bias=MS)
+            pairs()
+            mix(0, 1, 2, 3)
+            scan(row("es"), row("mk"), row("ef"), -MID - 1)
+            act(row("eg"), ind(row("es"), TU))
+            lower()
+            layer(0, 0, 1, 2)
+            twice(1, 0)
+            base[2](copy)
+            base[3](copy)
+            twice(0, 1)
+            cast("v", 0, 0, 1)
+            halves(RB, row("eg"), "iv", 24)
+            cast("s", 0, 2)
+            layer(1, 0, 1, 2)
+            layer(2, 3)
+            cast("s", 1, 0, 1, 2)
+            cast("s", 2, 3)
+            turn2("ta", RB)
+            twice(0, 0)
+            offsets(eu, "ta", L_I, 3)
+            twice(1, 1)
+        else:
+            act(row("ef"), ind(row("lr"), FU))
+            act(row("eg"), ind(row("ef"), TU))
+            mix(0, 0, 1, 2, 3)
+            twice(1, 0)
+            lower()
+            layer(0, 2, 1, 0, 3)
+            halves(RB, row("eg"), "eu1", 24)
+            cast("s", 0, 2, 0, 3)
+            cast("v", 0, 1)
+            layer(1, 0, 1, 2, 3)
+            turn2("ta", RB)
+            twice(1, 1)
+            offsets(eu, "ta", L_D, 2)
+            cast("s", 1, 0)
+            cast("v", 1, 1)
+            cast("s", 1, 2, 3)
+        b1, b2 = (2, 3) if last else (3, 2)
+        for b, h in ((2, 0), (3, 0), (b1, 1), (b2, 1)):
+            act(part("bg", b, cut[h], cut[h + 1]), ind(part("bb", b), V(eu, cut[h] // 16, cut[h + 1] // 16)))
+        for b in range(2):
+            tt(lane("xt", b, 0, C), ind(part("bb", b), V(eu, 0, 24)), part("fb", b), A.add)
+        for b, h in ((2, 0), (3, 0), (b1, 1)):
+            add(b, h)
+        for h in range(2):
+            pack(h)
+            if last:
+                lo, hi = cut[h], cut[h + 1]
+                store(T.oc[:, 4 * lo:4 * hi], bits(V("xq3", lo, hi)))
+                mm(4 + h, V("vq", 0, 128), V("vp", 0, 128), V("xq3", lo, hi), V("xp3", lo, hi), hi - lo)
+                scaled("sv"[h], V("yo", lo, hi), bank(4 + h, 0, hi - lo), 1.0)
+            else:
+                signs(t + 1, h)
+            if h == 0:
+                add(b2, 1)
         if not last:
-            pack(0)
-            signs(t + 1, 0)
-            state(2, 1)
-            pack(1)
-            signs(t + 1, 1)
+            turn2("tb", RA)
+            ahead["wide"]()
+            ahead["pair"]()
+            offsets("pk%d" % (t + 1), "tb", L_D, 3)
+            for k in ("sum", "refs", "turns"):
+                ahead[k]()
 
-    def finish(h):
-        pack(h)
-        lo, hi = cut[h], cut[h + 1]
-        X, XP = V("xq3", lo, hi), V("xp3", lo, hi)
-        mm(4 + h, V("vq", 0, 128), V("vp", 0, 128), X, XP, hi - lo)
-        store(T.oc[:, 4 * lo:4 * hi], bits(X))
-    finish(0)
-    act(V("yo", 0, LAST), bank(4, 0, LAST))
-    state(2, 1)
-    state(3, 1)
-    finish(1)
     for k in range(4):
         store(T.osc[4 * k:4 * k + 4, :], (row("xp3")[0], T.xp3[32 * k:32 * k + 4, :]), "s")
-    ts(V("yo", LAST, C), bank(5, 0, C - LAST), 1.0, A.mult)
     store(T.y[:], row("yo"))
     for s in count:
         if know["g"].get(s, 0) < count[s]:

@@ -5,32 +5,55 @@ MID = 192.0
 BF, FL, U16, I32, CODE = "bfloat16", "float32", "uint16", "int32", "float8_e4m3fn_x4"
 T2 = 384
 R_E, R_N, R_P, R_F = 6, 8, 10, 12
-CUT = (256, 256, 192)
-L_A, L_I, L_D, L_W, NL, L_F, L_Y = 0, 4, 8, 12, 16, 16, 20
+L_A, L_I, L_D, L_W, NL, L_F, L_Y, L_U, L_V = 0, 4, 8, 12, 16, 16, 20, 24, 28
+UP0 = 352
+RA, RB, RC, RD, RE = 16, 416, 816, 1216, 1616
+UL, UR = 16, 400
 
 SCRATCH = {"ps": ("psum", [128, 4096], "float32")}
 for _n, _c, _d in (
         [("xin", 1536, BF), ("uin", 512, BF), ("vin", 512, BF), ("pl", C, I32), ("pri", 72, I32), ("sj", 24, I32), ("su", 24, U16)]
         + [("wq", 512, CODE), ("wp", 512, "uint8"), ("uq", 128, CODE), ("up", 128, "uint8"), ("uuq", 128, CODE), ("uup", 128, "uint8")]
-        + [("vq", 128, CODE), ("vp", 128, "uint8"), ("eq", 512, CODE), ("ep", 512, "uint8")]
-        + [("one", 516, BF), ("eye", 516, BF), ("uoi", 8, I32), ("uo", 8, U16), ("col", 18, FL)]
-        + [(k, 2, I32) for k in ("pid", "p17", "pmi", "p8", "phi")] + [("jj", NL + 8, I32), ("cl", NL + 8, U16)]
-        + [(k, NL, FL) for k in ("jf", "ge", "cc", "cr")]
-        + [(k, 1536, BF) for k in ("fh", "gb", "bb", "bg", "zt", "xt")] + [("fb", 768, BF)]
-        + [(k, C, BF) for k in ("nm", "sg", "rs", "a2", "ef", "eg", "es", "mk", "mi", "lr")]
-        + [("uu", 784, BF), ("wd", 768, BF), ("rr", 816, BF), ("ta", 800, BF), ("tb", 800, BF)]
-        + [("s0", 384, FL), ("s1", 384, FL), ("sw", 192, FL), ("so", 96, FL), ("sb", 144, FL), ("w2", 32, FL)]
-        + [("ni", 24, I32), ("nx", 24, FL), ("po", 48, FL), ("yo", C, FL)]
-        + [("ku", 72, U16), ("p0", 48, U16), ("c2", 24, U16), ("iv", 48, U16)]
+        + [("vq", 128, CODE), ("vp", 128, "uint8"), ("eq", 512, CODE), ("ep", 512, "uint8"), ("lq", C, CODE), ("lp", C, "uint8")]
+        + [("one", 516, BF), ("eye", 516, BF), ("uoi", 8, I32), ("uo", 8, U16), ("col", 24, FL)]
+        + [(k, 2, I32) for k in ("pid", "pse", "pmi", "pei", "phi")] + [("jj", NL + 8, I32), ("cl", NL + 14, U16)]
+        + [(k, NL, FL) for k in ("jf", "ge", "cc", "cr")] + [("cu", 4, FL), ("cv", 4, FL)]
+        + [(k, 1536, BF) for k in ("fh", "fs", "gb", "bb", "bg", "zt", "xt")] + [("fb", 768, BF)]
+        + [(k, C, BF) for k in ("nm", "sg", "rs", "tab", "ef", "eg", "es", "mk", "mi", "lr")]
+        + [("uu", 784, BF), ("wd", 768, BF), ("rr", 2016, BF)] + [(k, 800, BF) for k in ("ta", "tb", "tc", "td", "te")]
+        + [("sf", 384, FL), ("st", 384, FL), ("sw", 192, FL), ("so", 96, FL), ("sb", 144, FL), ("su2", 32, FL)]
+        + [("ni", 24, I32), ("nx", 24, FL), ("po", 48, FL), ("yo", C, FL), ("fw", 24, BF), ("lf", 24, BF), ("lm", 52, U16)]
+        + [("ku", 72, U16), ("pu", 48, U16), ("cw", 24, U16), ("iv", 48, U16), ("iw", 32, U16)]
         + [("xq%d" % t, C, CODE) for t in range(4)] + [("xp%d" % t, C, "uint8") for t in range(4)]
-        + [("%s%d" % (k, t), 48, U16) for k in ("tp", "fp", "pk", "eu") for t in range(3)]
-        + [("%s%d" % (k, t), 24, BF) for k in ("fw", "lf") for t in range(2)]
-        + [("zq%d" % t, H, CODE) for t in range(3)] + [("yq%d" % t, C, CODE) for t in range(3)]
-        + [("zp%d" % t, H, "uint8") for t in range(3)] + [("yp%d" % t, C, "uint8") for t in range(3)]):
+        + [("%s%d" % (k, t), n, U16) for k, n in (("tp", 88), ("fp", 48), ("pk", 48), ("eu", 32)) for t in range(3)]
+        + [("zq%d" % t, H, CODE) for t in (1, 2)] + [("yq%d" % t, C, CODE) for t in range(3)]
+        + [("zp%d" % t, H, "uint8") for t in (1, 2)] + [("yp%d" % t, C, "uint8") for t in range(3)]):
     SCRATCH[_n] = ("sbuf", [128, _c], _d)
 LOADS = ["x", "u", "v", "pp", "rf", "pr", "wc", "ws"]
-SEMAPHORES = (["qv", "qs", "qt", "qg", "sent", "out", "pa", "pb", "pc"] + ["ld_" + k for k in LOADS]
+SEMAPHORES = (["qv", "qs", "qt", "qg", "sent", "out", "pa", "pb"] + ["ld_" + k for k in LOADS]
               + ["%s%d" % (k, t) for k in ("af", "aq", "ap") for t in range(3)])
+
+ORDER = {
+    "v": """@s pl pmi one col1 col0 col2 phi col3 col4 nm jf zero0 col6 col5 ge pei su uo cr2 col7 col23 po uq eq0 eq3 uuq first0 cc ku eq1 first1 cl0
+pack0 pack1 cl1 first2 pair1 first3 pair2 cl2 eq2 pair3 diff1 diff0 @0 there0 @s wrap0 @0 there1 there2 @s cv cl3 wrap1 @0 ta0 ta1 @s wrap2 @0 uu0 uu1
+@s wrap3 diff2 @0 wd0 sb wd1 cw @s cu @0 so ref2 @s cl5 @0 tp @s cl4 @0 tc2 tc3 tc0 tc1 inv0 fw fu fp inv1 z0 z2 inv3 z1 z3 inv2 tab0 q inv4 Z1 Z0 Z2
+Z3 tab1 Q e1 base3 te1 te0 base1 eu base2 twice1 x1 x0 add0 add1 add3 add2 pack0 pack1 pair1 pair2 diff1 pair3 diff2 wrap0 diff0 wrap1 @1 there0
+there1 there2 @0 wrap2 @1 ta0 ta1 uu1 uu0 @0 wrap3 @1 flag0 wd0 sb wd1 cw so ref1 tp twice2 tc0 tc1 base1 tc2 fu tc3 fw Z0 Z1 Z2 Z3 fp Q z2 z3 z0 z1
+inv3 tab1 q inv2 e1 inv4 b2 e3 b3 te1 te0 base2 twice0 eu B1 x0 x1 add0 add1 add2 add3 pack0 pack1 pair1 pair2 diff0 diff1 base3 pair3 wrap0 diff2
+wrap1 @2 there0 there1 there2 @1 wrap2 @2 ta0 ta1 uu0 uu1 @1 wrap3 @2 flag0 wd0 sb so wd1 cw twice3 tp ref1 ref2 tc0 tc1 tc2 fu tc3 Z3 Z2 Z1 Z0 fp Q
+z0 z1 z2 z3 twice0 q vq e3 b2 te1 te0 twice2 eu B1 x0 x1 add0 add1 add2 add3 pack0 pack1 sign1""",
+    "s": """@s load0 zero14 zero10 col12 zero6 col10 zero12 col8 mi col13 zero9 col11 col22 zero4 col14 col17 cr1 cr0 col18 col9 col15 zero13 col24 col19 mk uup
+zero1 col21 pair0 first6 col16 sign0 sign1 first5 first8 @0 here0 here1 here2 @s first7 col20 @0 fh2 fh1 @s first4 @0 twice3 flag0 flag1 twice2 flag2 fh0
+ref0 ref1 fh3 g1 base4 g0 g3 g2 twice0 fs1 fs2 fs3 fs0 G1 G0 G2 G3 b1 b0 base0 e0 b2 B0 B1 B2 b3 B3 bg0 bg1 bg3 bg2 pair0 sign0 sign1 @1 here0 here1
+here2 fh2 fh1 fh0 flag1 fh3 flag2 ref0 ref2 G0 G1 G2 G3 g2 g3 inv1 g0 g1 inv0 base4 tab0 e0 twice1 e2 base0 b1 twice3 b0 B0 B2 B3 bg0 bg1 bg2 bg3
+pair0 sign0 sign1 @2 here0 here1 here2 fh2 fh3 fh1 flag1 flag2 fh0 twice1 ref0 G3 G2 G1 G0 g2 g3 g0 g1 e0 e1 e2 b3 b0 b1 B0 B2 B3 bg0 bg1 bg2 bg3
+sign0 store4 store5 store6 store7""",
+    "t": """@s score0 score1 @0 eye1 eye0 eye2 eye3 eye5 eye6 eye7 eye4 w1 w0 w2 W0 W1 W2 w3 W3 score0 score1 @1 eye0 eye2 eye1 eye3 w2 w3 w1 w0 W0 W1 W2 W3
+score0 score1 @2 eye3 eye2 eye1 eye0 w2 w3 w0 w1 W0 W2 W1 W3 score0 score1""",
+    "g": """@s pid0 pid1 jj0 sj pse uoi jj1 eye zero3 jj2 zero5 zero7 zero2 zero11 zero8 @0 send0 send1 send2 @1 send0 send1 send2 @2 send0 send1 send2 store0
+store1""",
+    "y": """@s load1 load2 load3 load4 load5 load6 @0 load0 load1 @2 store2 store3 store8""",
+}
 
 
 def rank_program(g, core, T, topo):
@@ -38,14 +61,14 @@ def rank_program(g, core, T, topo):
     if rank is None:
         return
     queue = {"v": g.vector, "s": g.scalar, "t": g.tensor, "g": g, "y": g.sync}
-    count, know, acc = {}, {k: {} for k in queue}, {}
+    calls, acc, now = [], {}, {"stage": "s", "name": None}
 
     def V(name, lo, hi, step=1):
-        if name == "ps":
-            cols = range(lo // 512, -(-hi // 512))
-        else:
-            cols = range(lo, hi, step)
+        cols = range(lo // 512, -(-hi // 512)) if name == "ps" else range(lo, hi, step)
         return ([(name, sum(1 << c for c in cols))], T[name][:, lo:hi] if step == 1 else T[name][:, lo:hi:step])
+
+    def mark(name, k=0):
+        return ([(name, 1 << k)], None)
 
     def lane(name, b, lo, hi):
         return V(name, 4 * lo + b, 4 * hi, 4)
@@ -56,110 +79,104 @@ def rank_program(g, core, T, topo):
     def row(name):
         return V(name, 0, C)
 
+    def rows(r, lo=0, hi=C):
+        return V("rr", r + lo, r + hi)
+
+    def bank(b, lo=0, hi=C):
+        return V("ps", 512 * b + lo, 512 * b + hi)
+
     def bits(v, d=dt.uint8):
         return (v[0], v[1].bitcast(d))
 
     def ind(win, off):
         return (win[0] + off[0], win[1].indirect(off[1]))
 
-    def await_(q, recs):
-        for s, v, snap in recs:
-            if know[q].get(s, 0) >= v:
-                continue
-            if any(o[2].get(s, 0) >= v and (o[0], o[1]) != (s, v) and know[q].get(o[0], 0) < o[1] for o in recs):
-                continue
-            queue[q].wait_ge(T.sem[s], v)
-            know[q][s] = v
-        for s, v, snap in recs:
-            for k in snap:
-                know[q][k] = max(know[q].get(k, 0), snap[k])
+    def named(name):
+        now["name"] = name
 
-    def emit(q, fn, w, r, s=None, n=1):
+    def emit(ways, w, r, s=None, n=1, far=False):
+        hard, soft = set(), set()
         use = [(x, True) for v in w for x in v[0]] + [(x, False) for v in r for x in v[0]]
-        recs = {}
         for (nm, m), wr in use:
             for e in acc.get(nm, []):
-                if e[0] & m and (wr or e[1] or (nm == "ps" and e[2][0] != "q" + q)):
-                    k = e[2][0]
-                    if k not in recs or recs[k][1] < e[2][1]:
-                        recs[k] = e[2]
-        await_(q, list(recs.values()))
-        s = s or "q" + q
-        fn().then_inc(T.sem[s], n)
-        count[s] = count.get(s, 0) + n
-        snap = dict(know[q])
-        snap[s] = count[s]
+                if e[0] & m and (wr or e[1]):
+                    hard.add(e[2])
+                elif e[0] & m and nm == "ps":
+                    soft.add(e[2])
         for (nm, m), wr in use:
             l = acc.setdefault(nm, [])
             if wr:
                 l[:] = [e for e in l if e[0] & ~m]
-            l.append((m, wr, (s, count[s], snap)))
+            l.append((m, wr, len(calls)))
+        name = now["name"] or use[0][0][0].rstrip("0123")
+        calls.append(dict(ways=ways, hard=hard, soft=soft - hard, s=s, n=n, far=far, name=(now["stage"], name)))
 
     def copy(out, in_):
-        emit("v", lambda: g.vector.tensor_copy(out[1], in_[1]), [out], [in_])
+        emit({"v": lambda: g.vector.tensor_copy(out[1], in_[1])}, [out], [in_])
 
     def fill(out, x):
-        emit("v", lambda: g.vector.memset(out[1], x), [out], [])
+        emit({"v": lambda: g.vector.memset(out[1], x)}, [out], [])
 
     def tt(out, a, b, op):
-        emit("v", lambda: g.vector.tensor_tensor(out[1], a[1], b[1], op), [out], [a, b])
+        emit({"v": lambda: g.vector.tensor_tensor(out[1], a[1], b[1], op)}, [out], [a, b])
 
-    def ts(out, a, s1, op0, s2=None, op1=None):
-        r = [a] + [x for x in (s1, s2) if isinstance(x, tuple)]
+    def ts_way(out, a, s1, op0, s2=None, op1=None):
         x1, x2 = [x[1] if isinstance(x, tuple) else x for x in (s1, s2)]
         if op1 is None:
-            emit("v", lambda: g.vector.tensor_scalar(out[1], a[1], x1, None, op0), [out], r)
-        else:
-            emit("v", lambda: g.vector.tensor_scalar(out[1], a[1], x1, x2, op0, op1), [out], r)
+            return lambda: g.vector.tensor_scalar(out[1], a[1], x1, None, op0)
+        return lambda: g.vector.tensor_scalar(out[1], a[1], x1, x2, op0, op1)
+
+    def ts(out, a, s1, op0, s2=None, op1=None):
+        emit({"v": ts_way(out, a, s1, op0, s2, op1)}, [out], [a] + [x for x in (s1, s2) if isinstance(x, tuple)])
+
+    def act_way(out, in_, func, **kw):
+        kw = {k: x[1] if isinstance(x, tuple) else x for k, x in kw.items()}
+        return lambda: g.scalar.activation(out[1], in_[1], func, **kw)
 
     def act(out, in_, func=F.Copy, **kw):
-        r = [in_] + [x for x in kw.values() if isinstance(x, tuple)]
-        kw = {k: x[1] if isinstance(x, tuple) else x for k, x in kw.items()}
-        emit("s", lambda: g.scalar.activation(out[1], in_[1], func, **kw), [out], r)
+        emit({"s": act_way(out, in_, func, **kw)}, [out], [in_] + [x for x in kw.values() if isinstance(x, tuple)])
 
-    def scaled(q, out, in_, x):
-        if q == "v":
-            ts(out, in_, x, A.mult)
+    def move(out, in_, scale=None, bias=None):
+        if scale is None and bias is None:
+            ways = {"v": lambda: g.vector.tensor_copy(out[1], in_[1]), "s": act_way(out, in_, F.Copy)}
+        elif bias is None:
+            ways = {"v": ts_way(out, in_, scale, A.mult), "s": act_way(out, in_, F.Copy, scale=scale)}
+        elif scale is None:
+            ways = {"v": ts_way(out, in_, bias, A.add), "s": act_way(out, in_, F.Identity, bias=bias)}
         else:
-            act(out, in_, scale=x)
+            ways = {"v": ts_way(out, in_, scale, A.mult, bias, A.add), "s": act_way(out, in_, F.Identity, scale=scale, bias=bias)}
+        emit(ways, [out], [in_] + [x for x in (scale, bias) if isinstance(x, tuple)])
+
+    def flag(out, in_):
+        emit({"v": ts_way(out, in_, 0.0, A.not_equal), "s": act_way(out, in_, F.Abs, scale=0.5)}, [out], [in_])
+
+    def const(name, lo, hi, step, x):
+        out, n = V(name, lo, hi, step), len(range(lo, hi, step))
+        emit({"g": lambda: g.iota(out[1], [[0, n]], x, 0, allow_small_or_imprecise_dtypes=True), "v": ts_way(out, V("one", 0, n), float(x), A.mult),
+              "s": act_way(out, V("one", 0, n), F.Copy, scale=float(x))}, [out], [V("one", 0, n)])
 
     def quant(c, p, in_):
-        emit("v", lambda: g.vector.quantize_mx(c[1], p[1], in_[1]), [c, p], [in_])
+        emit({"v": lambda: g.vector.quantize_mx(c[1], p[1], in_[1])}, [c, p], [in_])
 
-    def mm(bank, w, wp, x, xp, n):
-        o = V("ps", 512 * bank, 512 * bank + n)
-        emit("t", lambda: g.tensor.matmul_mx(o[1], w[1], wp[1], x[1], xp[1], True, True), [o], [w, wp, x, xp])
+    def mm(b, w, lo, x, xp, n):
+        o, wq, wp = bank(b, 0, n), V(w + "q", lo, lo + 128), V(w + "p", lo, lo + 128)
+        emit({"t": lambda: g.tensor.matmul_mx(o[1], wq[1], wp[1], x[1], xp[1], True, True)}, [o], [wq, wp, x, xp])
 
-    def load(q, name, out, ap):
-        emit(q, lambda: queue[q].dma_start(out[1], ap), [out], [], "ld_" + name, 16)
+    def dma(q, s, out, in_, w, r, **kw):
+        emit({q: lambda: queue[q].dma_start(out, in_, **kw)}, w, r, s, 16)
 
-    def store(ap, in_, q="y"):
-        emit(q, lambda: queue[q].dma_start(ap, in_[1]), [], [in_], "out", 16)
-
-    def iota(out, pattern, base, cmul=0, flag=False):
-        emit("g", lambda: g.iota(out[1], pattern, base, cmul, allow_small_or_imprecise_dtypes=flag), [out], [])
+    def iota(out, pattern, base, cmul=0):
+        emit({"g": lambda: g.iota(out[1], pattern, base, cmul)}, [out], [])
 
     def turn(out, in_):
-        emit("v", lambda: g.vector.transpose(out[1], in_[1]), [out], [in_])
+        emit({"v": lambda: g.vector.transpose(out[1], in_[1])}, [out], [in_])
 
     def scan(out, a, b, first=0.0):
-        emit("v", lambda: g.vector.tensor_tensor_scan(out[1], a[1], b[1], first, A.mult, A.add), [out], [a, b])
-
-    def bank(b, lo=0, hi=C):
-        return V("ps", 512 * b + lo, 512 * b + hi)
-
-    RA, RB = 16, 416
-    UL, UR = 16, 400
-
-    def turn1(to, r, k):
-        if k == 0:
-            turn(V(to, 0, C), V("rr", r, r + C))
-        else:
-            turn(V(to, T2, T2 + 416), V("rr", r - 16, r + 400))
+        emit({"v": lambda: g.vector.tensor_tensor_scan(out[1], a[1], b[1], first, A.mult, A.add)}, [out], [a, b])
 
     def turn2(to, r):
-        turn1(to, r, 0)
-        turn1(to, r, 1)
+        turn(V(to, 0, C), rows(r))
+        turn(V(to, T2, T2 + 416), rows(r, -16, 400))
 
     def pick(tile, lo, n, wide=800):
         return ind(V(tile, 0, wide), V("cl", lo, lo + n))
@@ -167,9 +184,9 @@ def rank_program(g, core, T, topo):
     def offsets(name, tile, lo, n):
         ts(V(name, 0, 16 * n), pick(tile, lo, n), MID, A.add)
 
-    def halves(r, win, off, at):
-        act(V("rr", r, r + H), ind(win, V(off, at, at + 12)))
-        copy(V("rr", r + H, r + C), ind(win, V(off, at + 12, at + 24)))
+    def halves(to, win, off, at):
+        for lo in (0, H):
+            move(to(lo, lo + H), ind(win, V(off, at + lo // 16, at + lo // 16 + 12)))
 
     def ul(r):
         return V("uu", UL + r, UL + C, 16)
@@ -177,355 +194,338 @@ def rank_program(g, core, T, topo):
     def ur(r):
         return V("uu", UR + r, UR + C, 16)
 
-    def eyes(*bs):
-        for b in bs:
-            quant(V("eq", 128 * b, 128 * b + 128), V("ep", 128 * b, 128 * b + 128), V("eye", 3 - b, 515 - b))
+    def send(dst, src, s, t):
+        other = T.cores[rank ^ STEP[t]]
+        (rid, pnc), eng = topo.addr(other)[:2], topo.engines(core, other)
+        emit({"g": lambda: g.remote_dma(dst[1], src[1], T.sem[s], T.sem.sent, pnc, rid, topo.mask(core, other))}, [dst], [src], s, len(eng), True)
 
-    PM, MC, BC, P24, PH, UX, PAR, MS, MB, MW, SG, QA, QB, QC, QF, QY, PA, PB = [V("col", k, k + 1) for k in range(18)]
+    PM, MC, BC, P24, PH, UX, PAR, MS, MB, MW, SG, QA, QB, QC, QF, QY, PA, PB, PU, PV, ME, WE = [V("col", k, k + 1) for k in range(22)]
     B0 = 192
 
     def terms(k, n=144, step=6):
-        return V("s1", B0 + k, B0 + n, step)
+        return V("st", B0 + k, B0 + n, step)
 
     ONE, EYE, NM, PL = V("one", 0, 516), V("eye", 0, 516), row("nm"), row("pl")
-    load("s", "u", V("uin", 0, 512), T.u[:])
     fill(PL, 0)
-    for k, (name, r, ap) in enumerate((("pp", R_P, T.pp), ("rf", R_F, T.rf))):
-        emit("y", lambda: g.sync.dma_start(T.pl[r:128:16, :], ap[:]), [([("rows", 1 << k)], None)], [PL], "ld_" + name, 16)
-    load("y", "pr", V("pri", 0, 72), T.pr[:])
-    load("y", "x", V("xin", 0, 1536), T.x[:])
-    await_("y", [e[2] for e in acc["xin"]])
-    load("y", "wc", bits(V("wq", 0, 512)), T.wc[:])
-    load("y", "ws", V("wp", 0, 512), T.ws[:])
+    named("load")
+    dma("s", "ld_u", T.uin[:], T.u[:], [V("uin", 0, 512)], [])
+    dma("y", "ld_pp", T.pl[R_P:128:16, :], T.pp[:], [mark("rows", 0)], [PL])
+    dma("y", "ld_rf", T.pl[R_F:128:16, :], T.rf[:], [mark("rows", 1)], [PL])
+    dma("y", "ld_pr", T.pri[:], T.pr[:], [V("pri", 0, 72)], [])
+    dma("y", "ld_x", T.xin[:], T.x[:], [V("xin", 0, 1536)], [])
+    XIN = V("xin", 0, 1)
+    dma("y", "ld_wc", bits(V("wq", 0, 512))[1], T.wc[:], [V("wq", 0, 512)], [XIN])
+    dma("y", "ld_ws", T.wp[:], T.ws[:], [V("wp", 0, 512)], [XIN])
+    named(None)
 
     fill(ONE, 1.0)
     iota(V("pid", 0, 1), [[0, 1]], 0, 1)
     iota(V("pid", 1, 2), [[0, 1]], 0, 128)
     iota(V("sj", 0, 24), [[1, 24]], 0)
-    iota(V("p17", 0, 2), [[0, 2]], 0, 17)
+    iota(V("pse", 0, 2), [[0, 2]], 0, 17)
     iota(V("jj", L_I, NL), [[2, 3], [256, 4]], R_E)
     iota(V("jj", L_A, L_I), [[256, 4]], R_F)
-    iota(V("uoi", 0, 8), [[16, 8]], 0)
-    for lo in (400, 800, 0):
-        iota(V("rr", lo, lo + 16), [[0, 16]], 0, 0, True)
-    emit("g", lambda: g.affine_select(EYE[1], ONE[1], [[-1, 516]], A.is_equal, 0.0, 3, 4), [EYE], [ONE])
-    iota(V("sw", 0, 192), [[0, 192]], 0, 0, True)
     iota(V("jj", L_F, L_F + 8), [[14, 2], [128, 4]], 0)
-    iota(V("uu", 0, UR + C), [[0, UR + C]], 0, 0, True)
-    iota(V("s0", 0, 96, 2), [[0, 48]], 0, 0, True)
-    for name, k, x in (("s0", 0, 0), ("s0", 2, 1), ("s0", 3, 1), ("s0", 5, -1), ("s1", 3, 0)):
-        iota(V(name, B0 + k, B0 + 144, 6), [[0, 24]], x, 0, True)
+    iota(V("uoi", 0, 8), [[16, 8]], 0)
+    emit({"g": lambda: g.affine_select(EYE[1], ONE[1], [[-1, 516]], A.is_equal, 0.0, 3, 4)}, [EYE], [ONE])
+    named("zero")
+    for lo in range(0, 2016, 400):
+        const("rr", lo, lo + 16, 1, 0)
+    for name, lo, hi, step in (("sw", 0, 192, 1), ("uu", 0, UR, 1), ("uu", UR, UR + C, 1), ("sf", 0, 96, 2)):
+        const(name, lo, hi, step, 0)
+    for name, k, x in (("sf", 0, 0), ("sf", 2, 1), ("sf", 3, 1), ("sf", 5, -1), ("st", 3, 0)):
+        const(name, B0 + k, B0 + 144, 6, x)
+    named(None)
     ts(V("pmi", 0, 2), V("pid", 0, 2), 15 + 128 * 7, A.bitwise_and)
-    ts(V("p8", 0, 2), V("pid", 0, 2), 18 + 128 * 14, A.bitwise_and)
+    ts(V("pei", 0, 2), V("pid", 0, 2), 18 + 128 * 14, A.bitwise_and)
+    ts(V("phi", 0, 2), V("pse", 0, 2), 4, A.arith_shift_right, 1, A.bitwise_and)
     scan(NM, row("one"), row("one"), -MID - 1)
     ts(PM, V("pmi", 0, 1), -13.0, A.add)
     ts(MS, V("pmi", 1, 2), 0.0, A.is_equal)
     ts(P24, V("pmi", 0, 1), 24.0, A.mult)
     ts(PH, V("pmi", 0, 1), 16.0, A.mult)
     ts(MB, PM, R_N - 12.5, A.is_gt, -MID, A.mult)
-    act(QC, PM, F.Identity, scale=1 / 32, bias=13 / 32)
-    act(MC, PM, F.Relu, scale=768.0, bias=1.0)
-    act(row("mi"), NM, F.Identity, scale=MS, bias=MB)
-    ts(V("phi", 0, 2), V("p17", 0, 2), 4, A.arith_shift_right, 1, A.bitwise_and)
     ts(UX, PM, -0.5, A.is_gt)
-    ts(V("jf", 0, NL), V("jj", 0, NL), PH, A.add)
-    ts(V("su", 0, 24), V("sj", 0, 24), P24, A.add)
-    copy(V("col", 16, 18), V("p8", 0, 2))
-    ts(V("uo", 0, 8), V("uoi", 0, 8), UX, A.add)
-    ts(V("ge", 0, NL), V("jf", 0, NL), C - 0.5, A.is_gt)
     ts(PAR, V("phi", 0, 1), T2 + 16.0, A.mult)
+    copy(V("col", 16, 18), V("pei", 0, 2))
+    move(MW, MS, -1.0, 1.0)
+    move(SG, MS, None, -2.0 ** -93)
+    move(QC, PM, 1 / 32, 13 / 32)
+    move(QC, QC, MS)
+    act(MC, PM, F.Relu, scale=768.0, bias=1.0)
     act(MC, MC, F.Abs, bias=-1.0)
-    act(MW, MS, F.Identity, scale=-1.0, bias=1.0)
-    act(QC, QC, scale=MS)
-    for lo, hi, step in ((L_A, L_I, 0), (L_I, L_W, R_P - R_N), (L_W, NL, R_N - R_P)):
-        act(V("cr", lo, hi), V("ge", lo, hi), scale=float(step - C))
-    act(MC, MC, F.Identity, scale=MW, bias=QC)
-    act(QA, PA, F.Identity, scale=-(T2 + 16) / 32, bias=18 * (T2 + 16) / 32)
-    act(QB, PA, scale=QA)
-
-    A2, rows = V("rr", RB, RB + C), ind(PL, V("su", 0, 24))
-    quant(V("uq", 0, 128), V("up", 0, 128), V("uin", 0, 512))
-    tt(A2, (rows[0] + [("rows", 3)], rows[1]), row("mi"), A.add)
-    copy(V("ku", 0, 72), V("pri", 0, 72))
-    act(V("rr", RA, RA + C), ind(A2, V("ku", 0, 24)))
-    act(QF, PB, F.Identity, scale=9 / 128, bias=QB)
-    act(V("uup", 0, 128), ind(V("up", 0, 128), V("uo", 0, 8)))
+    move(MC, MC, MW, QC)
     act(BC, MC, F.Sign, bias=-0.5)
+    move(BC, BC, 0.5, -0.5)
+    move(QA, PA, -(T2 + 16) / 32, 18 * (T2 + 16) / 32)
+    move(QB, PA, QA)
+    move(QF, PB, 9 / 128, QB)
+    move(QY, PB, 8 / 128, QB)
+    move(PU, PAR, -176.0 / (T2 + 16), float(H))
+    move(PV, PAR, float(C) / (T2 + 16))
+    ts(ME, PM, R_E - 13.0, A.is_equal)
+    move(WE, ME, -1.0, 1.0)
+    move(row("mi"), NM, MS, MB)
+    move(row("mk"), row("one"), ME)
+    ts(V("su", 0, 24), V("sj", 0, 24), P24, A.add)
+    ts(V("uo", 0, 8), V("uoi", 0, 8), UX, A.add)
+    ts(V("jf", 0, NL), V("jj", 0, NL), PH, A.add)
+    ts(V("ge", 0, NL), V("jf", 0, NL), C - 0.5, A.is_gt)
+    for lo, hi, step in ((L_A, L_I, 0), (L_I, L_W, R_P - R_N), (L_W, NL, R_N - R_P)):
+        move(V("cr", lo, hi), V("ge", lo, hi), float(step - C))
     tt(V("cc", 0, NL), V("jf", 0, NL), V("cr", 0, NL), A.add)
-    copy(bits(V("uuq", 0, 128), dt.uint32), ind(bits(V("uq", 0, 128), dt.uint32), V("uo", 0, 8)))
+    ts(V("cv", 0, 4), V("cc", L_D, L_D + 4), 175.5, A.is_gt, PV, A.mult)
+    tt(V("cu", 0, 4), V("cc", L_D, L_D + 4), V("cv", 0, 4), A.add)
     copy(V("cl", L_W, NL), V("cc", L_W, NL))
-    eyes(0)
     ts(V("cl", L_A, L_W), V("cc", L_A, L_W), PAR, A.add)
-    turn2("ta", RB)
-    act(terms(4, 192), pick("ta", L_A, 2), F.Identity, bias=MID)
-    act(V("s1", 1, 96, 2), pick("ta", L_D, 3))
-    act(SG, MS, F.Identity, bias=-2.0 ** -93)
-    act(BC, BC, F.Identity, scale=0.5, bias=-0.5)
-    act(V("sw", 3, 192, 4), pick("ta", L_W, 3, C))
-    turn2("tb", RA)
-
-    def signs(t, h):
-        lo, hi = (0, CUT[t - 1] if t else H, C)[h:h + 2]
-        mm((4, 6)[h], V("uuq", 0, 128), V("uup", 0, 128), V("xq%d" % t, lo, hi), V("xp%d" % t, lo, hi), hi - lo)
-        act(V("sg", lo, hi), bank((4, 6)[h], 0, hi - lo), F.Sign, scale=MW, bias=SG)
-
-    ahead = {
-        "wide": lambda: tt(V("sw", 0, 192, 4), pick("tb", L_W, 3, C), V("sw", 3, 192, 4), A.subtract),
-        "pair": lambda: tt(V("s1", 0, 96, 2), pick("tb", L_D, 3), V("s1", 1, 96, 2), A.subtract),
-        "sum": lambda: tt(V("w2", 0, 32), pick("tb", L_A, 2), V("s1", 0, 64, 2), A.subtract),
-        "refs": lambda: tt(terms(1, 192), pick("tb", L_A, 2), terms(4, 192), A.subtract),
-        "turns": lambda: ts(V("ni", 0, 24), V("w2", 0, 24), 0.5, A.add, 1.0 / C, A.mult),
-        "less": lambda: ts(V("nx", 0, 24), V("ni", 0, 24), -float(C), A.mult, float(C), A.add),
-        "rest": lambda: tt(terms(0), V("nx", 0, 24), V("s1", 0, 48, 2), A.subtract)}
-    for h in range(2):
-        quant(V("xq0", H * h, H * h + H), V("xp0", H * h, H * h + H), V("xin", 768 * h, 768 * h + 768))
-        signs(0, h)
-    act(QY, PB, F.Identity, scale=8 / 128, bias=QB)
-    ahead["pair"]()
-    offsets("p0", "ta", L_D, 3)
-    offsets("pk0", "tb", L_D, 3)
-    ahead["sum"]()
-    eyes(1)
     ts(V("cl", L_F, L_F + 4), V("jj", L_F, L_F + 4), QF, A.add, PM, A.subtract)
-    eyes(2)
-    for k in ("turns", "wide", "less", "refs"):
-        ahead[k]()
+    ts(V("cl", L_Y, L_Y + 4), V("jj", L_Y, L_Y + 4), QY, A.add)
+    ts(V("cl", L_U, L_U + 4), V("cu", 0, 4), PU, A.add)
+    ts(V("cl", L_V, L_V + 1), V("cu", 2, 3), PU, A.add, -float(UP0), A.add)
+    fill(V("po", 0, 48), MID)
+    for b in range(4):
+        quant(V("eq", 128 * b, 128 * b + 128), V("ep", 128 * b, 128 * b + 128), V("eye", 3 - b, 515 - b))
+
+    quant(V("uq", 0, 128), V("up", 0, 128), V("uin", 0, 512))
+    act(V("uup", 0, 128), ind(V("up", 0, 128), V("uo", 0, 8)))
+    copy(bits(V("uuq", 0, 128), dt.uint32), ind(bits(V("uq", 0, 128), dt.uint32), V("uo", 0, 8)))
+    copy(V("ku", 0, 72), V("pri", 0, 72))
+    named("first")
+    first = ind(PL, V("su", 0, 24))
+    tt(rows(RC), (first[0] + [("rows", 3)], first[1]), row("mi"), A.add)
+    turn2("td", RC)
+    offsets("pu", "td", L_D, 3)
+    move(terms(4, 192), pick("td", L_A, 2), None, MID)
+    move(V("st", 1, 96, 2), pick("td", L_D, 3))
+    move(V("sw", 3, 192, 4), pick("td", L_W, 3, C))
+    move(ul(R_P), V("sw", 3, 96, 4))
+    move(ur(R_N), V("sw", 99, 192, 4))
+
+    def pairs(t, table):
+        named("pair")
+        move(rows(RE), ind(table, V("ku", 24 * t, 24 * t + 24)))
+        turn2("tb", RE)
+        offsets("pk%d" % t, "tb", L_D, 3)
+        named("diff")
+        tt(V("sw", 0, 192, 4), pick("tb", L_W, 3, C), V("sw", 3, 192, 4), A.subtract)
+        tt(V("st", 0, 96, 2), pick("tb", L_D, 3), V("st", 1, 96, 2), A.subtract)
+        tt(terms(1, 192), pick("tb", L_A, 2), terms(4, 192), A.subtract)
+        named("wrap")
+        tt(V("su2", 0, 32), pick("tb", L_A, 2), V("st", 0, 64, 2), A.subtract)
+        ts(V("ni", 0, 24), V("su2", 0, 24), 0.5, A.add, 1.0 / C, A.mult)
+        ts(V("nx", 0, 24), V("ni", 0, 24), -float(C), A.mult, float(C), A.add)
+        tt(terms(0), V("nx", 0, 24), V("st", 0, 48, 2), A.subtract)
+
+    def state(t, h, tile):
+        lo, hi = H * h, H * h + H
+        XQ, XP = V("xq%d" % t, lo, hi), V("xp%d" % t, lo, hi)
+        named("pack")
+        quant(XQ, XP, V(tile, 4 * lo, 4 * hi))
+        named("score")
+        mm(4 + 2 * h, "uu" if t < 3 else "v", 0, XQ, XP, H)
+        named("sign")
+        if t < 3:
+            act(V("sg", lo, hi), bank(4 + 2 * h, 0, H), F.Sign, scale=MW, bias=SG)
+        else:
+            move(V("yo", lo, hi), bank(4 + 2 * h, 0, H))
+            named("store")
+            dma("y", "out", T.oc[:, 4 * lo:4 * hi], bits(XQ)[1], [], [XQ])
+
+    def unpack(name, at, xq, xp):
+        for b in range(4):
+            named("eye")
+            mm(at + b, "e", 128 * b, row(xq), row(xp), C)
+            named(name)
+            move(part(name, b), bank(at + b), 0.5)
+
+    pairs(0, rows(RC))
+    for h in range(2):
+        state(0, h, "xin")
 
     for t in range(3):
-        last = t == 2
-        other = T.cores[rank ^ STEP[t]]
-        eng = topo.engines(core, other)
-        rid, pnc = topo.addr(other)[:2]
+        now["stage"], last = str(t), t == 2
         tp, fp, pk, eu, YQ, YP = ["%s%d" % (k, t) for k in ("tp", "fp", "pk", "eu", "yq", "yp")]
-        P = "tp%d" % (t - 1) if t else "p0"
-        TU, FU, UQ, UP = V(tp, 0, 24), V(fp, 0, 24), V("zq%d" % t, 0, H), V("zp%d" % t, 0, H)
-        WD, FR, EJ = V("wd", 0, 2 * C), V("rr", RA, RA + C), V("rr", RB, RB + C)
-        cut = (0, CUT[t], C)
-        at = ((0, 1, 4, 5), (6, 7, 1, 0)) if t == 0 else ((4, 5, 6, 7), (0, 1, 6, 7))
+        P = "tp%d" % (t - 1) if t else "pu"
+        WD, FR, WF = V("wd", 0, 2 * C), rows(RA), V("tc", H + R_N, H + C, 16)
+        at = ((0, 1, 0, 1), (4, 5, 6, 7)) if t == 0 else ((4, 5, 6, 7), (0, 1, 6, 7))
 
-        def send(dst, src, s, eng=eng):
-            mask = sum(1 << e for e in eng)
-            recs = [e[2] for nm, m in src[0] for e in acc[nm] if e[1] and e[0] & m]
-            await_("g", recs)
-            g.remote_dma(dst[1], src[1], T.sem[s], T.sem.sent, pnc, rid, mask)
-            count["sent"] = count.get("sent", 0) + len(eng)
-            count[s] = len(eng)
-            for nm, m in dst[0]:
-                acc.setdefault(nm, []).append((m, True, (s, len(eng), {s: len(eng)})))
-
-        def unpack(b, lo=0, hi=C):
-            act(part("fh", b, lo, hi), bank(b, lo, hi), scale=0.5)
-
-        def twice(b, h):
-            ts(part("fb", b, cut[h], cut[h + 1]), part("fh", b, cut[h], cut[h + 1]), 2.0, A.mult)
-
-        def place(h, *bs):
-            for b in bs:
-                act(part("gb", b, H * h, H * h + H), ind(part("fh", b), V(tp, 24 + 12 * h, 36 + 12 * h)))
-
-        def mix(h, *bs):
-            for b in bs:
-                tt(lane("zt", b, H * h, H * h + H), ind(part("fh", b), V(fp, 24 + 12 * h, 36 + 12 * h)), part("gb", b, H * h, H * h + H), A.add)
-
-        def lower():
-            quant(V(YQ, 0, H), V(YP, 0, H), V("zt", 0, 768))
-
-        def layer(h, *bs):
-            for b in bs:
-                lo, hi = (0, C) if h == 2 else (H * h, H * h + H)
-                mm(at[h % 2][b], V("wq", 128 * b, 128 * b + 128), V("wp", 128 * b, 128 * b + 128), V(YQ, lo, hi), V(YP, lo, hi), hi - lo)
-
-        def cast(q, h, *bs):
-            for b in bs:
-                lo, hi = (0, C) if h == 2 else (H * h, H * h + H)
-                scaled(q, part("bb", b, lo, hi), bank(at[h % 2][b], 0, hi - lo), 0.03125)
-
-        def table():
-            act(ur(R_E), V("lf%d" % t, 0, 24))
-
-        def pairs():
-            act(FR, ind(row("a2"), V("ku", 24 * t + 24, 24 * t + 48)))
-
-        def add(b, h):
-            tt(lane("xt", b, cut[h], cut[h + 1]), part("bg", b, cut[h], cut[h + 1]), bank(b, cut[h], cut[h + 1]), A.add)
-
-        def pack(h):
-            lo, hi = cut[h], cut[h + 1]
-            quant(V("xq%d" % (t + 1), lo, hi), V("xp%d" % (t + 1), lo, hi), V("xt", 4 * lo, 4 * hi))
-
-        base = (lambda f: f(V("s1", 49, 96, 2), V("so", 49, 96, 2)), lambda f: f(V("sw", 3, 96, 4), ur(R_P)),
-                lambda f: f(terms(4), FU), lambda f: f(ul(R_P), ur(R_P)))
-
-        for lo in range(0, C, 128):
-            act(V("rs", lo, lo + 128), ind(row("sg"), V(P, 24 + lo // 16, 32 + lo // 16)), F.Identity, bias=BC, scale=MC)
-        for lo in range(0, C, 128):
-            tt(V("rr", RB + lo, RB + lo + 128), ind(row("sg"), V(pk, 24 + lo // 16, 32 + lo // 16)), V("rs", lo, lo + 128), A.add)
-        if t:
-            ahead["less"]()
-        else:
-            eyes(3)
-            ts(V("cl", L_Y, L_Y + 4), V("jj", L_Y, L_Y + 4), QY, A.add)
-            act(ul(R_P), V("sw", 3, 96, 4))
-        for b in range(4):
-            mm(b, V("eq", 128 * b, 128 * b + 128), V("ep", 128 * b, 128 * b + 128), row("xq%d" % t), row("xp%d" % t), C)
-        unpack(0)
-        unpack(1)
         if t == 0:
-            act(ur(R_N), V("sw", 99, 192, 4))
+            named("send")
+            send(bits(row("lq")), bits(row("xq0")), "aq0", t)
+            send(row("lp"), row("xp0"), "ap0", t)
+        unpack("fh", 0, "xq%d" % t, "xp%d" % t)
+        named("twice")
+        for b in range(2):
+            for lo in (0, H):
+                move(part("fb", b, lo, lo + H), part("fh", b, lo, lo + H), 2.0)
+        for lo in range(0, C, 128):
+            named("here")
+            act(V("rs", lo, lo + 128), ind(row("sg"), V(P, 24 + lo // 16, 32 + lo // 16)), F.Identity, scale=MC, bias=BC)
+            named("there")
+            tt(rows(RB, lo, lo + 128), ind(row("sg"), V(pk, 24 + lo // 16, 32 + lo // 16)), V("rs", lo, lo + 128), A.add)
+        named(None)
         turn2("ta", RB)
-        act(V("s0", B0 + 1, B0 + 144, 3), pick("ta", L_F, 3), F.Abs, scale=0.5)
-        act(terms(2, 144, 3), pick("ta", L_Y, 3), scale=0.25)
-        unpack(2)
-        unpack(3, 0, H)
-        if t == 0:
-            ahead["rest"]()
         scan(V("uu", UL + R_N - 12, UL + R_N + 372, 4), V("ta", 0, C, 4), V("sw", 96, 192))
         scan(V("uu", UR + R_P - 12, UR + R_P + 372, 4), V("ta", 0, C, 4), V("sw", 0, 96))
-        ts(V("s0", 1, 96, 2), pick("ta", L_A, 3), 0.0, A.not_equal)
-        if t:
-            ahead["rest"]()
         turn(V("wd", 0, C), V("uu", UL, UL + C))
-        scan(V("sb", 0, 144), V("s0", B0, B0 + 144), V("s1", B0, B0 + 144))
         turn(V("wd", C, 2 * C), V("uu", UR, UR + C))
-        ts(V("c2", 0, 24), V("sb", 5, 144, 6), -1.0, A.mult, MID, A.add)
-        scan(V("so", 0, 96), V("s0", 0, 96), V("s1", 0, 96))
-        halves(RA, WD, "c2", 0)
-        unpack(3, H, C)
+        named("flag")
+        move(terms(2, 144, 3), pick("ta", L_Y, 3), 0.25)
+        flag(V("sf", B0 + 1, B0 + 144, 3), pick("ta", L_F, 3))
+        flag(V("sf", 1, 96, 2), pick("ta", L_A, 3))
+        named(None)
+        scan(V("sb", 0, 144), V("sf", B0, B0 + 144), V("st", B0, B0 + 144))
+        ts(V("cw", 0, 24), V("sb", 5, 144, 6), -1.0, A.mult, MID, A.add)
+        scan(V("so", 0, 96), V("sf", 0, 96), V("st", 0, 96))
         ts(V(tp, 0, 48), V("so", 1, 96, 2), MID, A.add)
-        place(1, 0, 1, 2, 3)
-        place(0, 0, 1, 2)
-        if last:
-            place(0, 3)
-            send(row("lr"), FR, "af2")
-            g.wait_ge(T.sem.pa, 16)
-            emit("g", lambda: g.dma_start(T.pf[:, 0:C], T.wd[R_P:128:16, C:2 * C], accum_op=A.add), [], [V("wd", C, 2 * C)], "pb", 16)
-            emit("g", lambda: g.dma_start(T.pf[:, C:2 * C], T.rr[R_N:128:16, RA:RA + C], accum_op=A.add), [], [FR], "pb", 16)
-            twice(0, 0)
-            turn2("tb", RA)
-            offsets(fp, "tb", L_D, 3)
-            quant(V("vq", 0, 128), V("vp", 0, 128), V("vin", 0, 512))
-            mix(1, 0, 1, 2, 3)
-            twice(0, 1)
-        else:
-            FW = V("fw%d" % t, 0, 24)
-            turn2("tb", RA)
-            copy(FW, V("tb", R_N, C, 16))
-            send(V("lf%d" % t, 0, 24), FW, "af%d" % t, eng if t else eng[::2])
-            if t:
-                base[1](copy)
-                offsets(fp, "tb", L_D, 3)
-                copy(ur(R_F), V("tb", R_N, C, 16))
-                mix(1, 0, 1, 2, 3)
-                base[0](copy)
-            else:
-                offsets(fp, "tb", L_D, 3)
-                emit("y", lambda: g.sync.dma_start(T.rr[R_P:128:16, RA:RA + C], T.nm[R_P:128:16, :]), [FR], [NM], "pc", 16)
-                base[1](copy)
-                mix(1, 0, 1, 2, 3)
-                base[2](copy)
-                copy(ur(R_F), V("tb", R_N, C, 16))
-        quant(UQ, UP, V("zt", 768, 1536))
-        send(bits(V(YQ, H, C)), bits(UQ), "aq%d" % t)
-        send(V(YP, H, C), UP, "ap%d" % t)
+        named("ref")
+        for lo, hi in ((160, 256), (256, C), (0, 160)):
+            move(rows(RA, lo, hi), ind(WD, V("cw", lo // 16, hi // 16)), *((WE, ME) if t == 0 else ()))
+        named(None)
+        turn(V("tc", UP0, 576), rows(RA, 160, C))
+        turn(V("tc", 576, 800), rows(RA, 176, 400))
+        turn(V("tc", H, UP0), rows(RA, 0, 160))
+        turn(V("tc", 0, H), rows(RA, -16, 176))
+        offsets(fp, "tc", L_U, 3)
+        named("fu")
+        ts(V(tp, 48, 64), ind(V("tc", UP0, 800), V("cl", L_V, L_V + 1)), MID, A.add)
+        named("fw")
         if t == 0:
-            place(0, 3)
-            base[3](act)
-            act(row("mk"), row("one"), scale=MS)
-            base[0](act)
-            for b in range(2):
-                act(part("fb", b), part("fh", b), scale=2.0)
-            mix(0, 0, 1, 2, 3)
-            lower()
-            layer(0, 0, 1, 2, 3)
-            emit("v", lambda: g.vector.tensor_copy(ind(EJ, V(tp, 24, 48))[1], FR[1]), [EJ], [FR, V(tp, 24, 48)])
-            cast("s", 0, 0, 1, 2, 3)
-            table()
-            turn2("ta", RB)
-            turn(row("a2"), V("uu", UR, UR + C))
-            offsets("iv", "ta", L_D, 3)
-            fill(V("po", 0, 48), MID)
-            emit("y", lambda: g.sync.dma_start(T.pf[:], T.po[:]), [], [V("po", 0, 48)], "pa", 16)
-            load("g", "v", V("vin", 0, 512), T.v[:])
-            layer(1, 0, 1, 3, 2)
-            halves(RB, row("a2"), "iv", 0)
-            pairs()
-            cast("s", 1, 0, 3, 2)
-            turn2("ta", RB)
-            offsets(eu, "ta", L_I, 2)
-            cast("v", 1, 1)
+            ts(V(tp, 64, 88), WF, MID, A.add)
         elif t == 1:
-            mix(0, 0)
-            table()
-            place(0, 3)
-            turn(row("a2"), V("uu", UR, UR + C))
-            act(row("ef"), ind(row("a2"), FU), F.Identity, scale=MW, bias=MS)
-            pairs()
-            mix(0, 1, 2, 3)
-            scan(row("es"), row("mk"), row("ef"), -MID - 1)
-            act(row("eg"), ind(row("es"), TU))
-            lower()
-            layer(0, 0, 1, 2)
-            twice(1, 0)
-            base[2](copy)
-            base[3](copy)
-            twice(0, 1)
-            cast("v", 0, 0, 1)
-            halves(RB, row("eg"), "iv", 24)
-            cast("s", 0, 2)
-            layer(1, 0, 1, 2)
-            layer(2, 3)
-            cast("s", 1, 0, 1, 2)
-            cast("s", 2, 3)
-            turn2("ta", RB)
-            twice(0, 0)
-            offsets(eu, "ta", L_I, 3)
-            twice(1, 1)
+            move(V("fw", 0, 24), WF)
+        named("send")
+        send(*((V("lm", 0, 52), V(tp, 36, 88)), (V("lf", 0, 24), V("fw", 0, 24)), (row("lr"), FR))[t], "af%d" % t, t)
+        if not last:
+            named("base")
+            move(V("st", 49, 96, 2), V("so", 49, 96, 2))
+            move(V("sw", 3, 96, 4), ur(R_P))
+            copy(terms(4), V(fp, 0, 24))
+            move(ul(R_P), ur(R_P))
+            move(ur(R_F), WF)
+        if t == 0:
+            unpack("fs", 4, "lq", "lp")
+        for h in (1, 0):
+            lo, hi = H * h, H * h + H
+            win, one, two = "fh", V(tp, 24 + 12 * h, 36 + 12 * h), V(tp, 52, 64) if h else V(fp, 24, 36)
+            if h and t == 0:
+                win, one, two = "fs", V("lm", 0, 12), V("lm", 16, 28)
+            for b in range(4):
+                named("gG"[h])
+                move(part("gb", b, lo, hi), ind(part(win, b), one))
+                named("zZ"[h])
+                tt(lane("zt", b, lo, hi), ind(part(win, b), two), part("gb", b, lo, hi), A.add)
+            named("qQ"[h])
+            if h and t:
+                UQ, UP = V("zq%d" % t, 0, H), V("zp%d" % t, 0, H)
+                quant(UQ, UP, V("zt", 4 * lo, 4 * hi))
+                named("send")
+                send(bits(V(YQ, H, C)), bits(UQ), "aq%d" % t, t)
+                send(V(YP, H, C), UP, "ap%d" % t, t)
+            else:
+                quant(V(YQ, lo, hi), V(YP, lo, hi), V("zt", 4 * lo, 4 * hi))
+        for h in range(2):
+            for b in range(4):
+                named("wW"[h])
+                mm(at[h][b], "w", 128 * b, V(YQ, H * h, H * h + H), V(YP, H * h, H * h + H), H)
+                named("bB"[h])
+                move(part("bb", b, H * h, H * h + H), bank(at[h][b], 0, H), 0.03125)
+        named("inv")
+        if t == 0:
+            scan(row("es"), row("mk"), FR, -MID - 1)
+            to = ind(rows(RC), V(tp, 24, 48))
+            emit({"v": lambda: g.vector.tensor_copy(to[1], T.es[:])}, [rows(RC)], [row("es"), V(tp, 24, 48)])
+            turn2("td", RC)
+            offsets("iv", "td", L_I, 3)
+        elif t == 1:
+            halves(lambda lo, hi: rows(RC, lo, hi), V("wd", 0, C), "iv", 0)
+            turn2("td", RC)
+            offsets("iw", "td", L_D, 2)
+        if not last:
+            named("tab")
+            if t == 0:
+                ts(ur(R_E), V("lm", 28, 52), -MID, A.add)
+            else:
+                move(ur(R_E), V("lf", 0, 24))
+            turn(row("tab"), V("uu", UR, UR + C))
+        named("e")
+        if t == 1:
+            halves(lambda lo, hi: V("ef", lo, hi), row("tab"), fp, 0)
+        if last:
+            move(row("ef"), ind(row("lr"), V(fp, 0, 24)))
+            move(row("eg"), ind(row("ef"), V(tp, 0, 24)))
+        halves(lambda lo, hi: rows(RD, lo, hi), *((row("tab"), "iv", 24), (row("ef"), "iw", 0), (row("eg"), "iw", 0))[t])
+        named(None)
+        turn2("te", RD)
+        offsets(eu, "te", L_D if last else L_I, 2)
+        if t == 0:
+            named("load")
+            dma("y", "ld_v", T.vin[:], T.v[:], [V("vin", 0, 512)], [V("lm", 0, 1)])
+            dma("y", "pa", T.pf[:], T.po[:], [mark("pf")], [V("po", 0, 48), V("lm", 0, 1)])
+        if last:
+            quant(V("vq", 0, 128), V("vp", 0, 128), V("vin", 0, 512))
+            named("store")
+            dma("g", "pb", T.pf[:, 0:C], T.wd[R_P:128:16, C:2 * C], [], [V("wd", C, 2 * C), mark("pf")], accum_op=A.add)
+            dma("g", "pb", T.pf[:, C:2 * C], T.rr[R_N:128:16, RA:RA + C], [], [FR, mark("pf")], accum_op=A.add)
         else:
-            act(row("ef"), ind(row("lr"), FU))
-            act(row("eg"), ind(row("ef"), TU))
-            mix(0, 0, 1, 2, 3)
-            twice(1, 0)
-            lower()
-            layer(0, 2, 1, 0, 3)
-            halves(RB, row("eg"), "eu1", 24)
-            cast("s", 0, 2, 0, 3)
-            cast("v", 0, 1)
-            layer(1, 0, 1, 2, 3)
-            turn2("ta", RB)
-            twice(1, 1)
-            offsets(eu, "ta", L_D, 2)
-            cast("s", 1, 0)
-            cast("v", 1, 1)
-            cast("s", 1, 2, 3)
-        b1, b2 = (2, 3) if last else (3, 2)
-        for b, h in ((2, 0), (3, 0), (b1, 1), (b2, 1)):
-            act(part("bg", b, cut[h], cut[h + 1]), ind(part("bb", b), V(eu, cut[h] // 16, cut[h + 1] // 16)))
+            pairs(t + 1, row("tab"))
+        named("x")
         for b in range(2):
             tt(lane("xt", b, 0, C), ind(part("bb", b), V(eu, 0, 24)), part("fb", b), A.add)
-        for b, h in ((2, 0), (3, 0), (b1, 1)):
-            add(b, h)
         for h in range(2):
-            pack(h)
-            if last:
-                lo, hi = cut[h], cut[h + 1]
-                store(T.oc[:, 4 * lo:4 * hi], bits(V("xq3", lo, hi)))
-                mm(4 + h, V("vq", 0, 128), V("vp", 0, 128), V("xq3", lo, hi), V("xp3", lo, hi), hi - lo)
-                scaled("sv"[h], V("yo", lo, hi), bank(4 + h, 0, hi - lo), 1.0)
-            else:
-                signs(t + 1, h)
-            if h == 0:
-                add(b2, 1)
-        if not last:
-            turn2("tb", RA)
-            ahead["wide"]()
-            ahead["pair"]()
-            offsets("pk%d" % (t + 1), "tb", L_D, 3)
-            for k in ("sum", "refs", "turns"):
-                ahead[k]()
+            lo, hi = H * h, H * h + H
+            for b in (2, 3):
+                named("bg")
+                move(part("bg", b, lo, hi), ind(part("bb", b), V(eu, lo // 16, hi // 16)))
+                named("add")
+                tt(lane("xt", b, lo, hi), part("bg", b, lo, hi), bank(b, lo, hi), A.add)
+            state(t + 1, h, "xt")
 
+    named("store")
     for k in range(4):
-        store(T.osc[4 * k:4 * k + 4, :], (row("xp3")[0], T.xp3[32 * k:32 * k + 4, :]), "s")
-    store(T.y[:], row("yo"))
+        dma("s", "out", T.osc[4 * k:4 * k + 4, :], T.xp3[32 * k:32 * k + 4, :], [], [row("xp3")])
+    dma("y", "out", T.y[:], T.yo[:], [], [row("yo")])
+
+    seen = {}
+    for c in calls:
+        seen.setdefault(c["name"], []).append(c)
+    by = {(k[0], k[1] + (str(i) if len(l) > 1 else "")): c for k, l in seen.items() for i, c in enumerate(l)}
+    line = {}
+    for q in queue:
+        line[q] = []
+        for word in ORDER[q].split():
+            if word[0] == "@":
+                stage = word[1]
+            else:
+                line[q].append(by[stage, word])
+                line[q][-1]["q"] = q
+    assert sum(len(l) for l in line.values()) == len(calls) and all("q" in c for c in calls)
+    count, know = {}, {k: {} for k in queue}
+    while any(line.values()):
+        ready = [q for q in queue if line[q] and all("done" in calls[d] for d in line[q][0]["hard"] | line[q][0]["soft"])]
+        q = ready[0]
+        c, recs = line[q].pop(0), {}
+        for d in c["hard"] | {d for d in c["soft"] if calls[d]["q"] != q}:
+            s, v, snap = calls[d]["done"]
+            if s not in recs or recs[s][1] < v:
+                recs[s] = (s, v, snap)
+        recs = list(recs.values())
+        for s, v, snap in recs:
+            if know[q].get(s, 0) < v and not any(o[2].get(s, 0) >= v and o[0] != s and know[q].get(o[0], 0) < o[1] for o in recs):
+                queue[q].wait_ge(T.sem[s], v)
+                know[q][s] = v
+        for s, v, snap in recs:
+            for k in snap:
+                know[q][k] = max(know[q].get(k, 0), snap[k])
+        s = c["s"] or "q" + q
+        count[s] = count.get(s, 0) + c["n"]
+        if c["far"]:
+            c["ways"][q]()
+            count["sent"] = count.get("sent", 0) + c["n"]
+            c["done"] = (s, count[s], {s: count[s]})
+        else:
+            c["ways"][q]().then_inc(T.sem[s], c["n"])
+            c["done"] = (s, count[s], dict(know[q], **{s: count[s]}))
     for s in count:
         if know["g"].get(s, 0) < count[s]:
             g.wait_ge(T.sem[s], count[s])

@@ -5,24 +5,26 @@ MID = 192.0
 BF, FL, U16, I32, CODE = "bfloat16", "float32", "uint16", "int32", "float8_e4m3fn_x4"
 T2 = 384
 R_E, R_N, R_P, R_F = 6, 8, 10, 12
-L_A, L_I, L_D, L_W, NL, L_F, L_Y, L_U, L_V = 0, 4, 8, 12, 16, 16, 20, 24, 28
+L_I, L_D, L_X, L_S, L_B, NL, L_W, L_U, L_V = 0, 4, 8, 12, 16, 20, 20, 24, 28
 UP0 = 352
 RA, RB, RC, RD, RE = 16, 416, 816, 1216, 1616
-UL, UR = 16, 400
+UL, UR = 16, 416
+CUT = 256
 
 SCRATCH = {"ps": ("psum", [128, 4096], "float32")}
 for _n, _c, _d in (
-        [("xin", 1536, BF), ("uin", 512, BF), ("vin", 512, BF), ("pl", C, I32), ("pri", 72, I32), ("sj", 24, I32), ("su", 24, U16)]
+        [("xin", 1536, BF), ("uin", 512, BF), ("vin", 512, BF), ("pl", C, I32), ("pri", 72, I32), ("su", 24, U16)]
         + [("wq", 512, CODE), ("wp", 512, "uint8"), ("uq", 128, CODE), ("up", 128, "uint8"), ("uuq", 128, CODE), ("uup", 128, "uint8")]
         + [("vq", 128, CODE), ("vp", 128, "uint8"), ("eq", 512, CODE), ("ep", 512, "uint8"), ("lq", C, CODE), ("lp", C, "uint8")]
-        + [("one", 516, BF), ("eye", 516, BF), ("uoi", 8, I32), ("uo", 8, U16), ("col", 24, FL)]
-        + [(k, 2, I32) for k in ("pid", "pse", "pmi", "pei", "phi")] + [("jj", NL + 8, I32), ("cl", NL + 14, U16)]
-        + [(k, NL, FL) for k in ("jf", "ge", "cc", "cr")] + [("cu", 4, FL), ("cv", 4, FL)]
+        + [("one", 516, BF), ("eye", 516, BF), ("uo", 8, U16), ("col", 24, FL)]
+        + [(k, 2, I32) for k in ("pid", "pse", "pmi", "phi")] + [("jj", NL, FL), ("cl", 30, U16)]
+        + [(k, NL, FL) for k in ("jf", "ge", "cc")] + [("cu", 4, FL), ("cv", 4, FL)]
         + [(k, 1536, BF) for k in ("fh", "fs", "gb", "bb", "bg", "zt", "xt")] + [("fb", 768, BF)]
         + [(k, C, BF) for k in ("nm", "sg", "rs", "tab", "ef", "eg", "es", "mk", "mi", "lr")]
-        + [("uu", 784, BF), ("wd", 768, BF), ("rr", 2016, BF)] + [(k, 800, BF) for k in ("ta", "tb", "tc", "td", "te")]
-        + [("sf", 384, FL), ("st", 384, FL), ("sw", 192, FL), ("so", 96, FL), ("sb", 144, FL), ("su2", 32, FL)]
-        + [("ni", 24, I32), ("nx", 24, FL), ("po", 48, FL), ("yo", C, FL), ("fw", 24, BF), ("lf", 24, BF), ("lm", 52, U16)]
+        + [("uu", 800, BF), ("wd", 768, BF), ("rr", 2016, BF)] + [(k, 800, BF) for k in ("ta", "tb", "tc", "td", "te")]
+        + [("sf", 112, FL), ("st", 96, FL), ("sx", 280, FL), ("sw", 192, FL), ("so", 96, FL), ("sb", 120, FL), ("su2", 32, FL)]
+        + [("ni", 24, BF), ("nx", 24, FL), ("cp", 48, FL), ("qt", 72, FL), ("qu", 72, FL), ("kq", 72, FL), ("po", 48, FL), ("yo", C, FL), ("lm", 52, U16)]
+        + [(k, 24, BF) for k in ("fw", "lf")]
         + [("ku", 72, U16), ("pu", 48, U16), ("cw", 24, U16), ("iv", 48, U16), ("iw", 32, U16)]
         + [("xq%d" % t, C, CODE) for t in range(4)] + [("xp%d" % t, C, "uint8") for t in range(4)]
         + [("%s%d" % (k, t), n, U16) for k, n in (("tp", 88), ("fp", 48), ("pk", 48), ("eu", 32)) for t in range(3)]
@@ -30,29 +32,29 @@ for _n, _c, _d in (
         + [("zp%d" % t, H, "uint8") for t in (1, 2)] + [("yp%d" % t, C, "uint8") for t in range(3)]):
     SCRATCH[_n] = ("sbuf", [128, _c], _d)
 LOADS = ["x", "u", "v", "pp", "rf", "pr", "wc", "ws"]
-SEMAPHORES = (["qv", "qs", "qt", "qg", "sent", "out", "pa", "pb"] + ["ld_" + k for k in LOADS]
+SEMAPHORES = (["qv", "qs", "qt", "qg", "sent", "out", "pa", "pb", "ax"] + ["ld_" + k for k in LOADS]
               + ["%s%d" % (k, t) for k in ("af", "aq", "ap") for t in range(3)])
 
 ORDER = {
-    "v": """@s pl pmi one col1 col0 col2 phi col3 col4 nm jf zero0 col6 col5 ge pei su uo cr2 col7 col23 po uq eq0 eq3 uuq first0 cc ku eq1 first1 cl0
-pack0 pack1 cl1 first2 pair1 first3 pair2 cl2 eq2 pair3 diff1 diff0 @0 there0 @s wrap0 @0 there1 there2 @s cv cl3 wrap1 @0 ta0 ta1 @s wrap2 @0 uu0 uu1
-@s wrap3 diff2 @0 wd0 sb wd1 cw @s cu @0 so ref2 @s cl5 @0 tp @s cl4 @0 tc2 tc3 tc0 tc1 inv0 fw fu fp inv1 z0 z2 inv3 z1 z3 inv2 tab0 q inv4 Z1 Z0 Z2
-Z3 tab1 Q e1 base3 te1 te0 base1 eu base2 twice1 x1 x0 add0 add1 add3 add2 pack0 pack1 pair1 pair2 diff1 pair3 diff2 wrap0 diff0 wrap1 @1 there0
-there1 there2 @0 wrap2 @1 ta0 ta1 uu1 uu0 @0 wrap3 @1 flag0 wd0 sb wd1 cw so ref1 tp twice2 tc0 tc1 base1 tc2 fu tc3 fw Z0 Z1 Z2 Z3 fp Q z2 z3 z0 z1
-inv3 tab1 q inv2 e1 inv4 b2 e3 b3 te1 te0 base2 twice0 eu B1 x0 x1 add0 add1 add2 add3 pack0 pack1 pair1 pair2 diff0 diff1 base3 pair3 wrap0 diff2
-wrap1 @2 there0 there1 there2 @1 wrap2 @2 ta0 ta1 uu0 uu1 @1 wrap3 @2 flag0 wd0 sb so wd1 cw twice3 tp ref1 ref2 tc0 tc1 tc2 fu tc3 Z3 Z2 Z1 Z0 fp Q
-z0 z1 z2 z3 twice0 q vq e3 b2 te1 te0 twice2 eu B1 x0 x1 add0 add1 add2 add3 pack0 pack1 sign1""",
-    "s": """@s load0 zero14 zero10 col12 zero6 col10 zero12 col8 mi col13 zero9 col11 col22 zero4 col14 col17 cr1 cr0 col18 col9 col15 zero13 col24 col19 mk uup
-zero1 col21 pair0 first6 col16 sign0 sign1 first5 first8 @0 here0 here1 here2 @s first7 col20 @0 fh2 fh1 @s first4 @0 twice3 flag0 flag1 twice2 flag2 fh0
-ref0 ref1 fh3 g1 base4 g0 g3 g2 twice0 fs1 fs2 fs3 fs0 G1 G0 G2 G3 b1 b0 base0 e0 b2 B0 B1 B2 b3 B3 bg0 bg1 bg3 bg2 pair0 sign0 sign1 @1 here0 here1
-here2 fh2 fh1 fh0 flag1 fh3 flag2 ref0 ref2 G0 G1 G2 G3 g2 g3 inv1 g0 g1 inv0 base4 tab0 e0 twice1 e2 base0 b1 twice3 b0 B0 B2 B3 bg0 bg1 bg2 bg3
-pair0 sign0 sign1 @2 here0 here1 here2 fh2 fh3 fh1 flag1 flag2 fh0 twice1 ref0 G3 G2 G1 G0 g2 g3 g0 g1 e0 e1 e2 b3 b0 b1 B0 B2 B3 bg0 bg1 bg2 bg3
-sign0 store4 store5 store6 store7""",
-    "t": """@s score0 score1 @0 eye1 eye0 eye2 eye3 eye5 eye6 eye7 eye4 w1 w0 w2 W0 W1 W2 w3 W3 score0 score1 @1 eye0 eye2 eye1 eye3 w2 w3 w1 w0 W0 W1 W2 W3
-score0 score1 @2 eye3 eye2 eye1 eye0 w2 w3 w0 w1 W0 W2 W1 W3 score0 score1""",
-    "g": """@s pid0 pid1 jj0 sj pse uoi jj1 eye zero3 jj2 zero5 zero7 zero2 zero11 zero8 @0 send0 send1 send2 @1 send0 send1 send2 @2 send0 send1 send2 store0
-store1""",
-    "y": """@s load1 load2 load3 load4 load5 load6 @0 load0 load1 @2 store2 store3 store8""",
+    "v": """@s pl one pmi phi zero0 col0 col1 nm col4 col5 col7 col8 col6 uo su ge uq col16 cc uuq cl0 first0 ku cl1 cv first2 first1 pack0 pack1 pack2 eq0 pair1
+pair2 first4 kq1 diff0 eq2 eq3 cu pk eq1 wrap0 diff2 @0 there0 there1 ta1 ta0 ta2 ta3 @s diff1 wrap3 @0 uu0 flag0 uu1 wd0 sb wd1 cw twice1 so ref2 @s
+cl2 cl3 @0 tp tc2 tc3 tc0 tc1 inv0 fw fp fu inv1 z2 z1 z3 z0 inv3 inv2 tab0 q inv4 Z1 tab1 Z0 Z2 Z3 b1 Q te0 te1 b3 eu B2 x0 x1 add0 add1 add3 add2
+pack0 pack1 pack2 pair2 pair1 base2 cp diff0 wrap0 pk diff1 diff2 wrap1 @1 there0 there1 ta1 ta0 ta2 ta3 @0 wrap3 @1 uu0 flag0 uu1 wd0 sb wd1 cw
+twice3 so ref1 tp tc1 tc0 tc2 fu tc3 Z0 Z1 Z2 Z3 fp Q z2 z0 z3 z1 tab1 inv2 q inv3 twice1 base2 inv4 b2 e3 twice0 te1 te0 B2 eu B1 x0 x1 add0 add1
+add2 add3 pack0 pack1 pack2 pair1 pair2 diff0 cp pk wrap0 diff1 diff2 wrap1 @2 there0 there1 ta0 ta1 ta2 ta3 @1 wrap3 @2 uu1 flag0 uu0 wd1 sb wd0 cw
+so ref1 tp twice2 tc0 tc1 g1 fu tc2 tc3 Z2 Z3 Z1 Z0 fp Q z0 z3 z1 z2 twice0 q vq e3 b3 te1 te0 B1 eu B3 x1 x0 add1 add0 add2 add3 pack1 pack0 pack2
+sign0 sign2""",
+    "s": """@s load0 zero10 zero2 zero3 zero9 col3 col9 col2 jf mi col15 zero6 kq0 col11 zero5 col10 col17 mk col12 uup col13 pair0 first3 first7 first5 first6
+sign0 sign1 sign2 cp @0 here0 here1 @s zero12 wrap1 first9 @0 fh0 @s wrap2 first8 @0 fh2 flag1 flag2 fh3 @s col14 @0 base1 ref0 ref1 fh1 g0 g2 @s kq2
+@0 g1 g3 fs1 fs0 fs2 fs3 fs5 fs4 fs6 G1 fs7 G0 G2 G3 b0 e1 e0 b2 twice0 twice3 twice2 B0 B1 B3 bg0 bg1 bg3 bg2 pair0 sign0 sign1 sign2 @1 here0 here1
+fh0 @0 wrap2 @1 fh2 fh1 flag1 fh3 flag2 ref0 ref2 G0 G1 G2 G3 g2 g0 g3 g1 inv0 tab0 inv1 twice2 base1 e1 e0 e2 b3 b1 b0 base0 B0 B3 bg0 bg1 bg2 bg3
+pair0 sign0 sign1 sign2 @2 here0 here1 fh3 @1 wrap2 @2 fh2 fh0 flag1 flag2 fh1 ref0 ref2 G2 G3 G1 G0 g0 g3 g2 e0 e1 twice3 e2 twice1 b2 b0 b1 B0 B2
+bg1 bg0 bg2 bg3 store3 store4 store5 sign1 store6""",
+    "t": """@s score0 score1 score2 @0 eye0 eye2 eye1 eye3 eye5 eye4 eye6 eye7 eye9 eye8 eye10 eye11 w1 w0 w2 w3 W0 W2 W1 W3 score0 score1 score2 @1 eye0 eye2
+eye1 eye3 w2 w0 w1 w3 W2 W0 W1 W3 score0 score1 score2 @2 eye3 eye0 eye2 eye1 w3 w2 w1 w0 W1 W0 W3 W2 score1 score0 score2""",
+    "g": """@s pid0 pid1 pse qt jj1 jj0 zero7 eye zero4 zero8 zero11 zero1 @0 send0 send1 send2 send3 base3 base4 base0 load0 @s kq3 po @1 fw send0 base4
+base3 send1 send2 @2 send0 send1 send2 store0 store1""",
+    "y": """@s load1 load2 load3 load4 load5 load6 @0 load1 @2 store2 store7""",
 }
 
 
@@ -147,6 +149,10 @@ def rank_program(g, core, T, topo):
             ways = {"v": ts_way(out, in_, scale, A.mult, bias, A.add), "s": act_way(out, in_, F.Identity, scale=scale, bias=bias)}
         emit(ways, [out], [in_] + [x for x in (scale, bias) if isinstance(x, tuple)])
 
+    def short(out, in_):
+        emit({"v": lambda: g.vector.tensor_copy(out[1], in_[1]), "s": act_way(out, in_, F.Copy),
+              "g": lambda: g.affine_select(out[1], in_[1], [[0, 24]], A.is_ge, 0.0, 0, 0)}, [out], [in_])
+
     def flag(out, in_):
         emit({"v": ts_way(out, in_, 0.0, A.not_equal), "s": act_way(out, in_, F.Abs, scale=0.5)}, [out], [in_])
 
@@ -166,7 +172,7 @@ def rank_program(g, core, T, topo):
         emit({q: lambda: queue[q].dma_start(out, in_, **kw)}, w, r, s, 16)
 
     def iota(out, pattern, base, cmul=0):
-        emit({"g": lambda: g.iota(out[1], pattern, base, cmul)}, [out], [])
+        emit({"g": lambda: g.iota(out[1], pattern, base, cmul, allow_small_or_imprecise_dtypes=True)}, [out], [])
 
     def turn(out, in_):
         emit({"v": lambda: g.vector.transpose(out[1], in_[1])}, [out], [in_])
@@ -199,11 +205,10 @@ def rank_program(g, core, T, topo):
         (rid, pnc), eng = topo.addr(other)[:2], topo.engines(core, other)
         emit({"g": lambda: g.remote_dma(dst[1], src[1], T.sem[s], T.sem.sent, pnc, rid, topo.mask(core, other))}, [dst], [src], s, len(eng), True)
 
-    PM, MC, BC, P24, PH, UX, PAR, MS, MB, MW, SG, QA, QB, QC, QF, QY, PA, PB, PU, PV, ME, WE = [V("col", k, k + 1) for k in range(22)]
-    B0 = 192
+    PM, MC, BC, P24, PH, UA, UY, PAR, MS, MB, MW, SG, QC, PU, PV, ME, WE = [V("col", k, k + 1) for k in range(17)]
 
-    def terms(k, n=144, step=6):
-        return V("st", B0 + k, B0 + n, step)
+    def terms(k, n=24):
+        return V("sx", 120 + k, 120 + 5 * n, 5)
 
     ONE, EYE, NM, PL = V("one", 0, 516), V("eye", 0, 516), row("nm"), row("pl")
     fill(PL, 0)
@@ -221,68 +226,54 @@ def rank_program(g, core, T, topo):
     fill(ONE, 1.0)
     iota(V("pid", 0, 1), [[0, 1]], 0, 1)
     iota(V("pid", 1, 2), [[0, 1]], 0, 128)
-    iota(V("sj", 0, 24), [[1, 24]], 0)
     iota(V("pse", 0, 2), [[0, 2]], 0, 17)
-    iota(V("jj", L_I, NL), [[2, 3], [256, 4]], R_E)
-    iota(V("jj", L_A, L_I), [[256, 4]], R_F)
-    iota(V("jj", L_F, L_F + 8), [[14, 2], [128, 4]], 0)
-    iota(V("uoi", 0, 8), [[16, 8]], 0)
+    iota(V("jj", L_I, L_B), [[2, 4], [256, 4]], R_E)
+    iota(V("jj", L_B, NL), [[256, 4]], 13)
+    iota(V("qt", 0, 72), [[0, 3], [16, 24]], 13)
     emit({"g": lambda: g.affine_select(EYE[1], ONE[1], [[-1, 516]], A.is_equal, 0.0, 3, 4)}, [EYE], [ONE])
     named("zero")
     for lo in range(0, 2016, 400):
         const("rr", lo, lo + 16, 1, 0)
     for name, lo, hi, step in (("sw", 0, 192, 1), ("uu", 0, UR, 1), ("uu", UR, UR + C, 1), ("sf", 0, 96, 2)):
         const(name, lo, hi, step, 0)
-    for name, k, x in (("sf", 0, 0), ("sf", 2, 1), ("sf", 3, 1), ("sf", 5, -1), ("st", 3, 0)):
-        const(name, B0 + k, B0 + 144, 6, x)
+    for k, x in ((0, 0), (2, -1), (4, 1)):
+        const("sx", k, 120, 5, x)
     named(None)
     ts(V("pmi", 0, 2), V("pid", 0, 2), 15 + 128 * 7, A.bitwise_and)
-    ts(V("pei", 0, 2), V("pid", 0, 2), 18 + 128 * 14, A.bitwise_and)
     ts(V("phi", 0, 2), V("pse", 0, 2), 4, A.arith_shift_right, 1, A.bitwise_and)
     scan(NM, row("one"), row("one"), -MID - 1)
     ts(PM, V("pmi", 0, 1), -13.0, A.add)
     ts(MS, V("pmi", 1, 2), 0.0, A.is_equal)
-    ts(P24, V("pmi", 0, 1), 24.0, A.mult)
-    ts(PH, V("pmi", 0, 1), 16.0, A.mult)
+    move(P24, PM, 24.0, 13 * 24.0 - 13 / 16)
+    move(PH, PM, 16.0, 13 * 16.0)
     ts(MB, PM, R_N - 12.5, A.is_gt, -MID, A.mult)
-    ts(UX, PM, -0.5, A.is_gt)
+    ts(UA, PM, -0.5, A.is_lt)
+    ts(UY, PM, 0.5, A.is_gt, -float(C), A.mult)
+    ts(QC, PM, -5.0, A.is_equal, 8.0, A.subtract)
     ts(PAR, V("phi", 0, 1), T2 + 16.0, A.mult)
-    copy(V("col", 16, 18), V("pei", 0, 2))
     move(MW, MS, -1.0, 1.0)
-    move(SG, MS, None, -2.0 ** -93)
-    move(QC, PM, 1 / 32, 13 / 32)
-    move(QC, QC, MS)
-    act(MC, PM, F.Relu, scale=768.0, bias=1.0)
-    act(MC, MC, F.Abs, bias=-1.0)
-    move(MC, MC, MW, QC)
-    act(BC, MC, F.Sign, bias=-0.5)
-    move(BC, BC, 0.5, -0.5)
-    move(QA, PA, -(T2 + 16) / 32, 18 * (T2 + 16) / 32)
-    move(QB, PA, QA)
-    move(QF, PB, 9 / 128, QB)
-    move(QY, PB, 8 / 128, QB)
+    move(SG, MW, -2.0 ** -93)
+    move(MC, UA, None, UY)
+    act(BC, MC, F.Abs, scale=3.0, bias=-1.0)
+    move(BC, QC, 0.25, BC)
     move(PU, PAR, -176.0 / (T2 + 16), float(H))
     move(PV, PAR, float(C) / (T2 + 16))
     ts(ME, PM, R_E - 13.0, A.is_equal)
     move(WE, ME, -1.0, 1.0)
     move(row("mi"), NM, MS, MB)
     move(row("mk"), row("one"), ME)
-    ts(V("su", 0, 24), V("sj", 0, 24), P24, A.add)
-    ts(V("uo", 0, 8), V("uoi", 0, 8), UX, A.add)
-    ts(V("jf", 0, NL), V("jj", 0, NL), PH, A.add)
-    ts(V("ge", 0, NL), V("jf", 0, NL), C - 0.5, A.is_gt)
-    for lo, hi, step in ((L_A, L_I, 0), (L_I, L_W, R_P - R_N), (L_W, NL, R_N - R_P)):
-        move(V("cr", lo, hi), V("ge", lo, hi), float(step - C))
-    tt(V("cc", 0, NL), V("jf", 0, NL), V("cr", 0, NL), A.add)
+    ts(V("su", 0, 24), V("qt", 0, 24), 1 / 16, A.mult, P24, A.add)
+    ts(V("uo", 0, 8), V("qt", 0, 8), -12.0, A.add, UA, A.subtract)
+    move(V("jf", 0, NL), V("jj", 0, NL), None, PH)
+    ts(V("ge", 0, NL), V("jf", 0, NL), C - 0.5, A.is_gt, 2.0 - C, A.mult)
+    tt(V("cc", 0, NL), V("jf", 0, NL), V("ge", 0, NL), A.add)
     ts(V("cv", 0, 4), V("cc", L_D, L_D + 4), 175.5, A.is_gt, PV, A.mult)
     tt(V("cu", 0, 4), V("cc", L_D, L_D + 4), V("cv", 0, 4), A.add)
-    copy(V("cl", L_W, NL), V("cc", L_W, NL))
-    ts(V("cl", L_A, L_W), V("cc", L_A, L_W), PAR, A.add)
-    ts(V("cl", L_F, L_F + 4), V("jj", L_F, L_F + 4), QF, A.add, PM, A.subtract)
-    ts(V("cl", L_Y, L_Y + 4), V("jj", L_Y, L_Y + 4), QY, A.add)
+    copy(V("cl", L_W, L_W + 4), V("cc", L_D, L_D + 4))
+    ts(V("cl", 0, NL), V("cc", 0, NL), PAR, A.add)
     ts(V("cl", L_U, L_U + 4), V("cu", 0, 4), PU, A.add)
     ts(V("cl", L_V, L_V + 1), V("cu", 2, 3), PU, A.add, -float(UP0), A.add)
-    fill(V("po", 0, 48), MID)
+    const("po", 0, 48, 1, H)
     for b in range(4):
         quant(V("eq", 128 * b, 128 * b + 128), V("ep", 128 * b, 128 * b + 128), V("eye", 3 - b, 515 - b))
 
@@ -294,53 +285,60 @@ def rank_program(g, core, T, topo):
     first = ind(PL, V("su", 0, 24))
     tt(rows(RC), (first[0] + [("rows", 3)], first[1]), row("mi"), A.add)
     turn2("td", RC)
-    offsets("pu", "td", L_D, 3)
-    move(terms(4, 192), pick("td", L_A, 2), None, MID)
-    move(V("st", 1, 96, 2), pick("td", L_D, 3))
+    move(V("cp", 0, 48), pick("td", L_X, 3))
+    ts(V("pu", 24, 48), V("cp", 0, 24), MID, A.add)
+    move(terms(4), V("cp", 24, 48), None, -float(C))
+    move(V("st", 49, 96, 2), V("cp", 0, 24))
     move(V("sw", 3, 192, 4), pick("td", L_W, 3, C))
-    move(ul(R_P), V("sw", 3, 96, 4))
-    move(ur(R_N), V("sw", 99, 192, 4))
+    move(ul(R_P), V("sw", 99, 192, 4))
+    move(ur(R_N), V("sw", 3, 96, 4))
+    named("kq")
+    move(V("qu", 0, 72), V("qt", 0, 72), None, PM)
+    tt(V("kq", 0, 72), V("pri", 0, 72), V("qu", 0, 72), A.subtract)
+    move(V("st", 1, 48, 2), V("qu", 0, 24), None, -MID)
+    short(V("st", 0, 48, 2), V("kq", 48, 72))
 
     def pairs(t, table):
         named("pair")
         move(rows(RE), ind(table, V("ku", 24 * t, 24 * t + 24)))
         turn2("tb", RE)
-        offsets("pk%d" % t, "tb", L_D, 3)
+        named("cp")
+        move(V("cp", 0, 48), pick("tb", L_X, 3))
+        named("pk")
+        ts(V("pk%d" % t, 24, 48), V("cp", 0, 24), MID, A.add)
         named("diff")
         tt(V("sw", 0, 192, 4), pick("tb", L_W, 3, C), V("sw", 3, 192, 4), A.subtract)
-        tt(V("st", 0, 96, 2), pick("tb", L_D, 3), V("st", 1, 96, 2), A.subtract)
-        tt(terms(1, 192), pick("tb", L_A, 2), terms(4, 192), A.subtract)
+        tt(V("st", 48, 96, 2), V("cp", 0, 24), V("st", 49, 96, 2), A.subtract)
+        tt(terms(2), V("cp", 24, 48), terms(4), A.subtract)
         named("wrap")
-        tt(V("su2", 0, 32), pick("tb", L_A, 2), V("st", 0, 64, 2), A.subtract)
-        ts(V("ni", 0, 24), V("su2", 0, 24), 0.5, A.add, 1.0 / C, A.mult)
-        ts(V("nx", 0, 24), V("ni", 0, 24), -float(C), A.mult, float(C), A.add)
-        tt(terms(0), V("nx", 0, 24), V("st", 0, 48, 2), A.subtract)
+        KQ = V("kq", 24 * t, 24 * t + 24)
+        tt(V("su2", 0, 24), V("cp", 24, 48), KQ, A.subtract)
+        move(V("ni", 0, 24), V("su2", 0, 24), 1.0 / C, MID + 0.5 / C)
+        move(V("nx", 0, 24), V("ni", 0, 24), -float(C), C * (MID + 1))
+        tt(terms(0), V("nx", 0, 24), KQ, A.subtract)
 
-    def state(t, h, tile):
-        lo, hi = H * h, H * h + H
-        XQ, XP = V("xq%d" % t, lo, hi), V("xp%d" % t, lo, hi)
-        named("pack")
-        quant(XQ, XP, V(tile, 4 * lo, 4 * hi))
-        named("score")
-        mm(4 + 2 * h, "uu" if t < 3 else "v", 0, XQ, XP, H)
-        named("sign")
-        if t < 3:
-            act(V("sg", lo, hi), bank(4 + 2 * h, 0, H), F.Sign, scale=MW, bias=SG)
-        else:
-            move(V("yo", lo, hi), bank(4 + 2 * h, 0, H))
-            named("store")
-            dma("y", "out", T.oc[:, 4 * lo:4 * hi], bits(XQ)[1], [], [XQ])
+    def state(t, tile):
+        for k, lo in enumerate(range(0, C, 128)):
+            XQ, XP = V("xq%d" % t, lo, lo + 128), V("xp%d" % t, lo, lo + 128)
+            named("pack")
+            quant(XQ, XP, V(tile, 4 * lo, 4 * lo + 512))
+            named("score")
+            mm(4 + k, "uu" if t < 3 else "v", 0, XQ, XP, 128)
+            named("sign")
+            if t < 3:
+                act(V("sg", lo, lo + 128), bank(4 + k, 0, 128), F.Sign, scale=MW, bias=SG)
+            else:
+                move(V("yo", lo, lo + 128), bank(4 + k, 0, 128))
 
-    def unpack(name, at, xq, xp):
+    def unpack(name, at, xq, xp, lo=0, hi=C):
         for b in range(4):
             named("eye")
-            mm(at + b, "e", 128 * b, row(xq), row(xp), C)
+            mm(at + b, "e", 128 * b, V(xq, lo, hi), V(xp, lo, hi), hi - lo)
             named(name)
-            move(part(name, b), bank(at + b), 0.5)
+            move(part(name, b, lo, hi), bank(at + b, 0, hi - lo), 0.5)
 
     pairs(0, rows(RC))
-    for h in range(2):
-        state(0, h, "xin")
+    state(0, "xin")
 
     for t in range(3):
         now["stage"], last = str(t), t == 2
@@ -351,33 +349,38 @@ def rank_program(g, core, T, topo):
 
         if t == 0:
             named("send")
-            send(bits(row("lq")), bits(row("xq0")), "aq0", t)
             send(row("lp"), row("xp0"), "ap0", t)
+            send(bits(V("lq", 0, H)), bits(V("xq0", 0, H)), "ax", t)
+            send(bits(V("lq", H, C)), bits(V("xq0", H, C)), "aq0", t)
         unpack("fh", 0, "xq%d" % t, "xp%d" % t)
         named("twice")
         for b in range(2):
             for lo in (0, H):
                 move(part("fb", b, lo, lo + H), part("fh", b, lo, lo + H), 2.0)
-        for lo in range(0, C, 128):
+        for lo in (H, 0):
             named("here")
-            act(V("rs", lo, lo + 128), ind(row("sg"), V(P, 24 + lo // 16, 32 + lo // 16)), F.Identity, scale=MC, bias=BC)
+            move(V("rs", lo, lo + H), ind(row("sg"), V(P, 24 + lo // 16, 36 + lo // 16)), MC, BC)
             named("there")
-            tt(rows(RB, lo, lo + 128), ind(row("sg"), V(pk, 24 + lo // 16, 32 + lo // 16)), V("rs", lo, lo + 128), A.add)
+            tt(rows(RB, lo, lo + H), ind(row("sg"), V(pk, 24 + lo // 16, 36 + lo // 16)), V("rs", lo, lo + H), A.add)
         named(None)
-        turn2("ta", RB)
-        scan(V("uu", UL + R_N - 12, UL + R_N + 372, 4), V("ta", 0, C, 4), V("sw", 96, 192))
-        scan(V("uu", UR + R_P - 12, UR + R_P + 372, 4), V("ta", 0, C, 4), V("sw", 0, 96))
+        turn(V("ta", H, C), rows(RB, H, C))
+        turn(V("ta", T2 + 224, T2 + 416), rows(RB, 208, 400))
+        turn(V("ta", 0, H), rows(RB, 0, H))
+        turn(V("ta", T2, T2 + 224), rows(RB, -16, 208))
+        scan(V("uu", UL + R_N - 12, UL + R_N + 372, 4), V("ta", 0, C, 4), V("sw", 0, 96))
+        scan(V("uu", UR + R_P - 12, UR + R_P + 372, 4), V("ta", 0, C, 4), V("sw", 96, 192))
         turn(V("wd", 0, C), V("uu", UL, UL + C))
         turn(V("wd", C, 2 * C), V("uu", UR, UR + C))
         named("flag")
-        move(terms(2, 144, 3), pick("ta", L_Y, 3), 0.25)
-        flag(V("sf", B0 + 1, B0 + 144, 3), pick("ta", L_F, 3))
-        flag(V("sf", 1, 96, 2), pick("ta", L_A, 3))
+        move(V("sx", 1, 240, 5), pick("ta", L_B, 3), 0.5)
+        act(V("sx", 3, 240, 5), pick("ta", L_S, 3), F.Abs, scale=0.5)
+        a = 0 if last else 48
+        flag(V("sf", a + 1, a + (96 if last else 64), 2), pick("ta", L_X, 3 if last else 2))
         named(None)
-        scan(V("sb", 0, 144), V("sf", B0, B0 + 144), V("st", B0, B0 + 144))
-        ts(V("cw", 0, 24), V("sb", 5, 144, 6), -1.0, A.mult, MID, A.add)
-        scan(V("so", 0, 96), V("sf", 0, 96), V("st", 0, 96))
-        ts(V(tp, 0, 48), V("so", 1, 96, 2), MID, A.add)
+        scan(V("sb", 0, 120), V("sx", 0, 120), V("sx", 120, 240))
+        ts(V("cw", 0, 24), V("sb", 4, 120, 5), MID, A.add)
+        scan(V("so", a, 96), V("sf", a, 96), V("st", a, 96))
+        ts(V(tp, a // 2, 48), V("so", a + 1, 96, 2), MID, A.add)
         named("ref")
         for lo, hi in ((160, 256), (256, C), (0, 160)):
             move(rows(RA, lo, hi), ind(WD, V("cw", lo // 16, hi // 16)), *((WE, ME) if t == 0 else ()))
@@ -393,18 +396,19 @@ def rank_program(g, core, T, topo):
         if t == 0:
             ts(V(tp, 64, 88), WF, MID, A.add)
         elif t == 1:
-            move(V("fw", 0, 24), WF)
+            short(V("fw", 0, 24), WF)
         named("send")
         send(*((V("lm", 0, 52), V(tp, 36, 88)), (V("lf", 0, 24), V("fw", 0, 24)), (row("lr"), FR))[t], "af%d" % t, t)
         if not last:
             named("base")
-            move(V("st", 49, 96, 2), V("so", 49, 96, 2))
-            move(V("sw", 3, 96, 4), ur(R_P))
-            copy(terms(4), V(fp, 0, 24))
-            move(ul(R_P), ur(R_P))
-            move(ur(R_F), WF)
+            short(V("st", 49, 96, 2), V("so", 49, 96, 2))
+            move(V("sw", 99, 192, 4), ur(R_P))
+            ts(terms(4), V(fp, 0, 24), -float(C + H), A.add)
+            short(ul(R_P), ur(R_P))
+            short(ur(R_F), WF)
         if t == 0:
-            unpack("fs", 4, "lq", "lp")
+            unpack("fs", 4, "lq", "lp", 0, H)
+            unpack("fs", 4, "lq", "lp", H, C)
         for h in (1, 0):
             lo, hi = H * h, H * h + H
             win, one, two = "fh", V(tp, 24 + 12 * h, 36 + 12 * h), V(tp, 52, 64) if h else V(fp, 24, 36)
@@ -446,7 +450,7 @@ def rank_program(g, core, T, topo):
             if t == 0:
                 ts(ur(R_E), V("lm", 28, 52), -MID, A.add)
             else:
-                move(ur(R_E), V("lf", 0, 24))
+                short(ur(R_E), V("lf", 0, 24))
             turn(row("tab"), V("uu", UR, UR + C))
         named("e")
         if t == 1:
@@ -460,7 +464,7 @@ def rank_program(g, core, T, topo):
         offsets(eu, "te", L_D if last else L_I, 2)
         if t == 0:
             named("load")
-            dma("y", "ld_v", T.vin[:], T.v[:], [V("vin", 0, 512)], [V("lm", 0, 1)])
+            dma("g", "ld_v", T.vin[:], T.v[:], [V("vin", 0, 512)], [V("lm", 0, 1)])
             dma("y", "pa", T.pf[:], T.po[:], [mark("pf")], [V("po", 0, 48), V("lm", 0, 1)])
         if last:
             quant(V("vq", 0, 128), V("vp", 0, 128), V("vin", 0, 512))
@@ -472,16 +476,16 @@ def rank_program(g, core, T, topo):
         named("x")
         for b in range(2):
             tt(lane("xt", b, 0, C), ind(part("bb", b), V(eu, 0, 24)), part("fb", b), A.add)
-        for h in range(2):
-            lo, hi = H * h, H * h + H
+        for lo, hi in ((0, CUT), (CUT, C)):
             for b in (2, 3):
                 named("bg")
                 move(part("bg", b, lo, hi), ind(part("bb", b), V(eu, lo // 16, hi // 16)))
                 named("add")
                 tt(lane("xt", b, lo, hi), part("bg", b, lo, hi), bank(b, lo, hi), A.add)
-            state(t + 1, h, "xt")
+        state(t + 1, "xt")
 
     named("store")
+    dma("y", "out", T.oc[:], bits(row("xq3"))[1], [], [row("xq3")])
     for k in range(4):
         dma("s", "out", T.osc[4 * k:4 * k + 4, :], T.xp3[32 * k:32 * k + 4, :], [], [row("xp3")])
     dma("y", "out", T.y[:], T.yo[:], [], [row("yo")])

from concourse.mybir import dt, AluOpType as A, ActivationFunctionType as F

C, H, STEP = 384, 192, [1, 2, 4]
MID = 192.0
BF, FL, U16, I32, CODE = "bfloat16", "float32", "uint16", "int32", "float8_e4m3fn_x4"
T2 = 384
R_E, R_N, R_P, R_F = 6, 8, 10, 12
L_I, L_D, L_X, L_S, L_B, NL, L_W, L_U, L_V = 0, 4, 8, 12, 16, 20, 20, 24, 28
UP0 = 352
RA, RB, RC, RD, RE = 16, 416, 816, 1216, 1616
UL, UR = 16, 416
CUT = 256

SCRATCH = {"ps": ("psum", [128, 4096], "float32")}
for _n, _c, _d in (
        [("xin", 1536, BF), ("uin", 512, BF), ("vin", 512, BF), ("pl", C, I32), ("pri", 72, I32), ("su", 24, U16)]
        + [("wq", 512, CODE), ("wp", 512, "uint8"), ("uq", 128, CODE), ("up", 128, "uint8"), ("uuq", 128, CODE), ("uup", 128, "uint8")]
        + [("vq", 128, CODE), ("vp", 128, "uint8"), ("eq", 512, CODE), ("ep", 512, "uint8"), ("lq", C, CODE), ("lp", C, "uint8")]
        + [("one", 516, BF), ("eye", 516, BF), ("uo", 8, U16), ("col", 24, FL)]
        + [(k, 2, I32) for k in ("pid", "pse", "pmi", "phi")] + [("jj", NL, FL), ("cl", 30, U16)]
        + [(k, NL, FL) for k in ("jf", "ge", "cc")] + [("cu", 4, FL), ("cv", 4, FL)]
        + [(k, 1536, BF) for k in ("fh", "fs", "gb", "bb", "bg", "zt", "xt")] + [("fb", 768, BF)]
        + [(k, C, BF) for k in ("nm", "sg", "rs", "tab", "ef", "eg", "es", "mk", "mi", "lr")]
        + [("uu", 800, BF), ("wd", 768, BF), ("rr", 2016, BF)] + [(k, 800, BF) for k in ("ta", "tb", "tc", "td", "te")]
        + [("sf", 112, FL), ("st", 96, FL), ("sx", 280, FL), ("sw", 192, FL), ("so", 96, FL), ("sb", 120, FL), ("su2", 32, FL)]
        + [("ni", 24, BF), ("nx", 24, FL), ("cp", 48, FL), ("qt", 72, FL), ("qu", 72, FL), ("kq", 72, FL), ("po", 48, FL), ("yo", C, FL), ("lm", 52, U16)]
        + [(k, 24, BF) for k in ("fw", "lf")]
        + [("ku", 72, U16), ("pu", 48, U16), ("cw", 24, U16), ("iv", 48, U16), ("iw", 32, U16)]
        + [("xq%d" % t, C, CODE) for t in range(4)] + [("xp%d" % t, C, "uint8") for t in range(4)]
        + [("%s%d" % (k, t), n, U16) for k, n in (("tp", 88), ("fp", 48), ("pk", 48), ("eu", 32)) for t in range(3)]
        + [("zq%d" % t, H, CODE) for t in (1, 2)] + [("yq%d" % t, C, CODE) for t in range(3)]
        + [("zp%d" % t, H, "uint8") for t in (1, 2)] + [("yp%d" % t, C, "uint8") for t in range(3)]):
    SCRATCH[_n] = ("sbuf", [128, _c], _d)
LOADS = ["x", "u", "v", "pp", "rf", "pr", "wc", "ws"]
SEMAPHORES = (["qv", "qs", "qt", "qg", "sent", "out", "pa", "pb", "ax"] + ["ld_" + k for k in LOADS]
              + ["%s%d" % (k, t) for k in ("af", "aq", "ap") for t in range(3)])

ORDER = {
    "v": """@s pl one pmi phi zero0 col0 col1 nm col4 col5 col7 col8 col6 uo su ge uq col16 cc uuq cl0 first0 ku cl1 cv first2 first1 pack0 pack1 pack2 eq0 pair1
pair2 first4 kq1 diff0 eq2 eq3 cu pk eq1 wrap0 diff2 @0 there0 there1 ta1 ta0 ta2 ta3 @s diff1 wrap3 @0 uu0 flag0 uu1 wd0 sb wd1 cw twice1 so ref2 @s
cl2 cl3 @0 tp tc2 tc3 tc0 tc1 inv0 fw fp fu inv1 z2 z1 z3 z0 inv3 inv2 tab0 q inv4 Z1 tab1 Z0 Z2 Z3 b1 Q te0 te1 b3 eu B2 x0 x1 add0 add1 add3 add2
pack0 pack1 pack2 pair2 pair1 base2 cp diff0 wrap0 pk diff1 diff2 wrap1 @1 there0 there1 ta1 ta0 ta2 ta3 @0 wrap3 @1 uu0 flag0 uu1 wd0 sb wd1 cw
twice3 so ref1 tp tc1 tc0 tc2 fu tc3 Z0 Z1 Z2 Z3 fp Q z2 z0 z3 z1 tab1 inv2 q inv3 twice1 base2 inv4 b2 e3 twice0 te1 te0 B2 eu B1 x0 x1 add0 add1
add2 add3 pack0 pack1 pack2 pair1 pair2 diff0 cp pk wrap0 diff1 diff2 wrap1 @2 there0 there1 ta0 ta1 ta2 ta3 @1 wrap3 @2 uu1 flag0 uu0 wd1 sb wd0 cw
so ref1 tp twice2 tc0 tc1 g1 fu tc2 tc3 Z2 Z3 Z1 Z0 fp Q z0 z3 z1 z2 twice0 q vq e3 b3 te1 te0 B1 eu B3 x1 x0 add1 add0 add2 add3 pack1 pack0 pack2
sign0 sign2""",
    "s": """@s load0 zero10 zero2 zero3 zero9 col3 col9 col2 jf mi col15 zero6 kq0 col11 zero5 col10 col17 mk col12 uup col13 pair0 first3 first7 first5 first6
sign0 sign1 sign2 cp @0 here0 here1 @s zero12 wrap1 first9 @0 fh0 @s wrap2 first8 @0 fh2 flag1 flag2 fh3 @s col14 @0 base1 ref0 ref1 fh1 g0 g2 @s kq2
@0 g1 g3 fs1 fs0 fs2 fs3 fs5 fs4 fs6 G1 fs7 G0 G2 G3 b0 e1 e0 b2 twice0 twice3 twice2 B0 B1 B3 bg0 bg1 bg3 bg2 pair0 sign0 sign1 sign2 @1 here0 here1
fh0 @0 wrap2 @1 fh2 fh1 flag1 fh3 flag2 ref0 ref2 G0 G1 G2 G3 g2 g0 g3 g1 inv0 tab0 inv1 twice2 base1 e1 e0 e2 b3 b1 b0 base0 B0 B3 bg0 bg1 bg2 bg3
pair0 sign0 sign1 sign2 @2 here0 here1 fh3 @1 wrap2 @2 fh2 fh0 flag1 flag2 fh1 ref0 ref2 G2 G3 G1 G0 g0 g3 g2 e0 e1 twice3 e2 twice1 b2 b0 b1 B0 B2
bg1 bg0 bg2 bg3 store3 store4 store5 sign1 store6""",
    "t": """@s score0 score1 score2 @0 eye0 eye2 eye1 eye3 eye5 eye4 eye6 eye7 eye9 eye8 eye10 eye11 w1 w0 w2 w3 W0 W2 W1 W3 score0 score1 score2 @1 eye0 eye2
eye1 eye3 w2 w0 w1 w3 W2 W0 W1 W3 score0 score1 score2 @2 eye3 eye0 eye2 eye1 w3 w2 w1 w0 W1 W0 W3 W2 score1 score0 score2""",
    "g": """@s pid0 pid1 pse qt jj1 jj0 zero7 eye zero4 zero8 zero11 zero1 @0 send0 send1 send2 send3 base3 base4 base0 load0 @s kq3 po @1 fw send0 base4
base3 send1 send2 @2 send0 send1 send2 store0 store1""",
    "y": """@s load1 load2 load3 load4 load5 load6 @0 load1 @2 store2 store7""",
}


def rank_program(g, core, T, topo):
    rank = T.rank_of(core)
    if rank is None:
        return
    queue = {"v": g.vector, "s": g.scalar, "t": g.tensor, "g": g, "y": g.sync}
    calls, acc, now = [], {}, {"stage": "s", "name": None}

    def V(name, lo, hi, step=1):
        cols = range(lo // 512, -(-hi // 512)) if name == "ps" else range(lo, hi, step)
        return ([(name, sum(1 << c for c in cols))], T[name][:, lo:hi] if step == 1 else T[name][:, lo:hi:step])

    def mark(name, k=0):
        return ([(name, 1 << k)], None)

    def lane(name, b, lo, hi):
        return V(name, 4 * lo + b, 4 * hi, 4)

    def part(name, b, lo=0, hi=C):
        return V(name, C * b + lo, C * b + hi)

    def row(name):
        return V(name, 0, C)

    def rows(r, lo=0, hi=C):
        return V("rr", r + lo, r + hi)

    def bank(b, lo=0, hi=C):
        return V("ps", 512 * b + lo, 512 * b + hi)

    def bits(v, d=dt.uint8):
        return (v[0], v[1].bitcast(d))

    def ind(win, off):
        return (win[0] + off[0], win[1].indirect(off[1]))

    def named(name):
        now["name"] = name

    def emit(ways, w, r, s=None, n=1, far=False):
        hard, soft = set(), set()
        use = [(x, True) for v in w for x in v[0]] + [(x, False) for v in r for x in v[0]]
        for (nm, m), wr in use:
            for e in acc.get(nm, []):
                if e[0] & m and (wr or e[1]):
                    hard.add(e[2])
                elif e[0] & m and nm == "ps":
                    soft.add(e[2])
        for (nm, m), wr in use:
            l = acc.setdefault(nm, [])
            if wr:
                l[:] = [e for e in l if e[0] & ~m]
            l.append((m, wr, len(calls)))
        name = now["name"] or use[0][0][0].rstrip("0123")
        calls.append(dict(ways=ways, hard=hard, soft=soft - hard, s=s, n=n, far=far, name=(now["stage"], name)))

    def copy(out, in_):
        emit({"v": lambda: g.vector.tensor_copy(out[1], in_[1])}, [out], [in_])

    def fill(out, x):
        emit({"v": lambda: g.vector.memset(out[1], x)}, [out], [])

    def tt(out, a, b, op):
        emit({"v": lambda: g.vector.tensor_tensor(out[1], a[1], b[1], op)}, [out], [a, b])

    def ts_way(out, a, s1, op0, s2=None, op1=None):
        x1, x2 = [x[1] if isinstance(x, tuple) else x for x in (s1, s2)]
        if op1 is None:
            return lambda: g.vector.tensor_scalar(out[1], a[1], x1, None, op0)
        return lambda: g.vector.tensor_scalar(out[1], a[1], x1, x2, op0, op1)

    def ts(out, a, s1, op0, s2=None, op1=None):
        emit({"v": ts_way(out, a, s1, op0, s2, op1)}, [out], [a] + [x for x in (s1, s2) if isinstance(x, tuple)])

    def act_way(out, in_, func, **kw):
        kw = {k: x[1] if isinstance(x, tuple) else x for k, x in kw.items()}
        return lambda: g.scalar.activation(out[1], in_[1], func, **kw)

    def act(out, in_, func=F.Copy, **kw):
        emit({"s": act_way(out, in_, func, **kw)}, [out], [in_] + [x for x in kw.values() if isinstance(x, tuple)])

    def move(out, in_, scale=None, bias=None):
        if scale is None and bias is None:
            ways = {"v": lambda: g.vector.tensor_copy(out[1], in_[1]), "s": act_way(out, in_, F.Copy)}
        elif bias is None:
            ways = {"v": ts_way(out, in_, scale, A.mult), "s": act_way(out, in_, F.Copy, scale=scale)}
        elif scale is None:
            ways = {"v": ts_way(out, in_, bias, A.add), "s": act_way(out, in_, F.Identity, bias=bias)}
        else:
            ways = {"v": ts_way(out, in_, scale, A.mult, bias, A.add), "s": act_way(out, in_, F.Identity, scale=scale, bias=bias)}
        emit(ways, [out], [in_] + [x for x in (scale, bias) if isinstance(x, tuple)])

    def short(out, in_):
        emit({"v": lambda: g.vector.tensor_copy(out[1], in_[1]), "s": act_way(out, in_, F.Copy),
              "g": lambda: g.affine_select(out[1], in_[1], [[0, 24]], A.is_ge, 0.0, 0, 0)}, [out], [in_])

    def flag(out, in_):
        emit({"v": ts_way(out, in_, 0.0, A.not_equal), "s": act_way(out, in_, F.Abs, scale=0.5)}, [out], [in_])

    def const(name, lo, hi, step, x):
        out, n = V(name, lo, hi, step), len(range(lo, hi, step))
        emit({"g": lambda: g.iota(out[1], [[0, n]], x, 0, allow_small_or_imprecise_dtypes=True), "v": ts_way(out, V("one", 0, n), float(x), A.mult),
              "s": act_way(out, V("one", 0, n), F.Copy, scale=float(x))}, [out], [V("one", 0, n)])

    def quant(c, p, in_):
        emit({"v": lambda: g.vector.quantize_mx(c[1], p[1], in_[1])}, [c, p], [in_])

    def mm(b, w, lo, x, xp, n):
        o, wq, wp = bank(b, 0, n), V(w + "q", lo, lo + 128), V(w + "p", lo, lo + 128)
        emit({"t": lambda: g.tensor.matmul_mx(o[1], wq[1], wp[1], x[1], xp[1], True, True)}, [o], [wq, wp, x, xp])

    def dma(q, s, out, in_, w, r, **kw):
        emit({q: lambda: queue[q].dma_start(out, in_, **kw)}, w, r, s, 16)

    def iota(out, pattern, base, cmul=0):
        emit({"g": lambda: g.iota(out[1], pattern, base, cmul, allow_small_or_imprecise_dtypes=True)}, [out], [])

    def turn(out, in_):
        emit({"v": lambda: g.vector.transpose(out[1], in_[1])}, [out], [in_])

    def scan(out, a, b, first=0.0):
        emit({"v": lambda: g.vector.tensor_tensor_scan(out[1], a[1], b[1], first, A.mult, A.add)}, [out], [a, b])

    def turn2(to, r):
        turn(V(to, 0, C), rows(r))
        turn(V(to, T2, T2 + 416), rows(r, -16, 400))

    def pick(tile, lo, n, wide=800):
        return ind(V(tile, 0, wide), V("cl", lo, lo + n))

    def offsets(name, tile, lo, n):
        ts(V(name, 0, 16 * n), pick(tile, lo, n), MID, A.add)

    def halves(to, win, off, at):
        for lo in (0, H):
            move(to(lo, lo + H), ind(win, V(off, at + lo // 16, at + lo // 16 + 12)))

    def ul(r):
        return V("uu", UL + r, UL + C, 16)

    def ur(r):
        return V("uu", UR + r, UR + C, 16)

    def send(dst, src, s, t):
        other = T.cores[rank ^ STEP[t]]
        (rid, pnc), eng = topo.addr(other)[:2], topo.engines(core, other)
        emit({"g": lambda: g.remote_dma(dst[1], src[1], T.sem[s], T.sem.sent, pnc, rid, topo.mask(core, other))}, [dst], [src], s, len(eng), True)

    PM, MC, BC, P24, PH, UA, UY, PAR, MS, MB, MW, SG, QC, PU, PV, ME, WE = [V("col", k, k + 1) for k in range(17)]

    def terms(k, n=24):
        return V("sx", 120 + k, 120 + 5 * n, 5)

    ONE, EYE, NM, PL = V("one", 0, 516), V("eye", 0, 516), row("nm"), row("pl")
    fill(PL, 0)
    named("load")
    dma("s", "ld_u", T.uin[:], T.u[:], [V("uin", 0, 512)], [])
    dma("y", "ld_pp", T.pl[R_P:128:16, :], T.pp[:], [mark("rows", 0)], [PL])
    dma("y", "ld_rf", T.pl[R_F:128:16, :], T.rf[:], [mark("rows", 1)], [PL])
    dma("y", "ld_pr", T.pri[:], T.pr[:], [V("pri", 0, 72)], [])
    dma("y", "ld_x", T.xin[:], T.x[:], [V("xin", 0, 1536)], [])
    XIN = V("xin", 0, 1)
    dma("y", "ld_wc", bits(V("wq", 0, 512))[1], T.wc[:], [V("wq", 0, 512)], [XIN])
    dma("y", "ld_ws", T.wp[:], T.ws[:], [V("wp", 0, 512)], [XIN])
    named(None)

    fill(ONE, 1.0)
    iota(V("pid", 0, 1), [[0, 1]], 0, 1)
    iota(V("pid", 1, 2), [[0, 1]], 0, 128)
    iota(V("pse", 0, 2), [[0, 2]], 0, 17)
    iota(V("jj", L_I, L_B), [[2, 4], [256, 4]], R_E)
    iota(V("jj", L_B, NL), [[256, 4]], 13)
    iota(V("qt", 0, 72), [[0, 3], [16, 24]], 13)
    emit({"g": lambda: g.affine_select(EYE[1], ONE[1], [[-1, 516]], A.is_equal, 0.0, 3, 4)}, [EYE], [ONE])
    named("zero")
    for lo in range(0, 2016, 400):
        const("rr", lo, lo + 16, 1, 0)
    for name, lo, hi, step in (("sw", 0, 192, 1), ("uu", 0, UR, 1), ("uu", UR, UR + C, 1), ("sf", 0, 96, 2)):
        const(name, lo, hi, step, 0)
    for k, x in ((0, 0), (2, -1), (4, 1)):
        const("sx", k, 120, 5, x)
    named(None)
    ts(V("pmi", 0, 2), V("pid", 0, 2), 15 + 128 * 7, A.bitwise_and)
    ts(V("phi", 0, 2), V("pse", 0, 2), 4, A.arith_shift_right, 1, A.bitwise_and)
    scan(NM, row("one"), row("one"), -MID - 1)
    ts(PM, V("pmi", 0, 1), -13.0, A.add)
    ts(MS, V("pmi", 1, 2), 0.0, A.is_equal)
    move(P24, PM, 24.0, 13 * 24.0 - 13 / 16)
    move(PH, PM, 16.0, 13 * 16.0)
    ts(MB, PM, R_N - 12.5, A.is_gt, -MID, A.mult)
    ts(UA, PM, -0.5, A.is_lt)
    ts(UY, PM, 0.5, A.is_gt, -float(C), A.mult)
    ts(QC, PM, -5.0, A.is_equal, 8.0, A.subtract)
    ts(PAR, V("phi", 0, 1), T2 + 16.0, A.mult)
    move(MW, MS, -1.0, 1.0)
    move(SG, MW, -2.0 ** -93)
    move(MC, UA, None, UY)
    act(BC, MC, F.Abs, scale=3.0, bias=-1.0)
    move(BC, QC, 0.25, BC)
    move(PU, PAR, -176.0 / (T2 + 16), float(H))
    move(PV, PAR, float(C) / (T2 + 16))
    ts(ME, PM, R_E - 13.0, A.is_equal)
    move(WE, ME, -1.0, 1.0)
    move(row("mi"), NM, MS, MB)
    move(row("mk"), row("one"), ME)
    ts(V("su", 0, 24), V("qt", 0, 24), 1 / 16, A.mult, P24, A.add)
    ts(V("uo", 0, 8), V("qt", 0, 8), -12.0, A.add, UA, A.subtract)
    move(V("jf", 0, NL), V("jj", 0, NL), None, PH)
    ts(V("ge", 0, NL), V("jf", 0, NL), C - 0.5, A.is_gt, 2.0 - C, A.mult)
    tt(V("cc", 0, NL), V("jf", 0, NL), V("ge", 0, NL), A.add)
    ts(V("cv", 0, 4), V("cc", L_D, L_D + 4), 175.5, A.is_gt, PV, A.mult)
    tt(V("cu", 0, 4), V("cc", L_D, L_D + 4), V("cv", 0, 4), A.add)
    copy(V("cl", L_W, L_W + 4), V("cc", L_D, L_D + 4))
    ts(V("cl", 0, NL), V("cc", 0, NL), PAR, A.add)
    ts(V("cl", L_U, L_U + 4), V("cu", 0, 4), PU, A.add)
    ts(V("cl", L_V, L_V + 1), V("cu", 2, 3), PU, A.add, -float(UP0), A.add)
    const("po", 0, 48, 1, H)
    for b in range(4):
        quant(V("eq", 128 * b, 128 * b + 128), V("ep", 128 * b, 128 * b + 128), V("eye", 3 - b, 515 - b))

    quant(V("uq", 0, 128), V("up", 0, 128), V("uin", 0, 512))
    act(V("uup", 0, 128), ind(V("up", 0, 128), V("uo", 0, 8)))
    copy(bits(V("uuq", 0, 128), dt.uint32), ind(bits(V("uq", 0, 128), dt.uint32), V("uo", 0, 8)))
    copy(V("ku", 0, 72), V("pri", 0, 72))
    named("first")
    first = ind(PL, V("su", 0, 24))
    tt(rows(RC), (first[0] + [("rows", 3)], first[1]), row("mi"), A.add)
    turn2("td", RC)
    move(V("cp", 0, 48), pick("td", L_X, 3))
    ts(V("pu", 24, 48), V("cp", 0, 24), MID, A.add)
    move(terms(4), V("cp", 24, 48), None, -float(C))
    move(V("st", 49, 96, 2), V("cp", 0, 24))
    move(V("sw", 3, 192, 4), pick("td", L_W, 3, C))
    move(ul(R_P), V("sw", 99, 192, 4))
    move(ur(R_N), V("sw", 3, 96, 4))
    named("kq")
    move(V("qu", 0, 72), V("qt", 0, 72), None, PM)
    tt(V("kq", 0, 72), V("pri", 0, 72), V("qu", 0, 72), A.subtract)
    move(V("st", 1, 48, 2), V("qu", 0, 24), None, -MID)
    short(V("st", 0, 48, 2), V("kq", 48, 72))

    def pairs(t, table):
        named("pair")
        move(rows(RE), ind(table, V("ku", 24 * t, 24 * t + 24)))
        turn2("tb", RE)
        named("cp")
        move(V("cp", 0, 48), pick("tb", L_X, 3))
        named("pk")
        ts(V("pk%d" % t, 24, 48), V("cp", 0, 24), MID, A.add)
        named("diff")
        tt(V("sw", 0, 192, 4), pick("tb", L_W, 3, C), V("sw", 3, 192, 4), A.subtract)
        tt(V("st", 48, 96, 2), V("cp", 0, 24), V("st", 49, 96, 2), A.subtract)
        tt(terms(2), V("cp", 24, 48), terms(4), A.subtract)
        named("wrap")
        KQ = V("kq", 24 * t, 24 * t + 24)
        tt(V("su2", 0, 24), V("cp", 24, 48), KQ, A.subtract)
        move(V("ni", 0, 24), V("su2", 0, 24), 1.0 / C, MID + 0.5 / C)
        move(V("nx", 0, 24), V("ni", 0, 24), -float(C), C * (MID + 1))
        tt(terms(0), V("nx", 0, 24), KQ, A.subtract)

    def state(t, tile):
        for k, lo in enumerate(range(0, C, 128)):
            XQ, XP = V("xq%d" % t, lo, lo + 128), V("xp%d" % t, lo, lo + 128)
            named("pack")
            quant(XQ, XP, V(tile, 4 * lo, 4 * lo + 512))
            named("score")
            mm(4 + k, "uu" if t < 3 else "v", 0, XQ, XP, 128)
            named("sign")
            if t < 3:
                act(V("sg", lo, lo + 128), bank(4 + k, 0, 128), F.Sign, scale=MW, bias=SG)
            else:
                move(V("yo", lo, lo + 128), bank(4 + k, 0, 128))

    def unpack(name, at, xq, xp, lo=0, hi=C):
        for b in range(4):
            named("eye")
            mm(at + b, "e", 128 * b, V(xq, lo, hi), V(xp, lo, hi), hi - lo)
            named(name)
            move(part(name, b, lo, hi), bank(at + b, 0, hi - lo), 0.5)

    pairs(0, rows(RC))
    state(0, "xin")

    for t in range(3):
        now["stage"], last = str(t), t == 2
        tp, fp, pk, eu, YQ, YP = ["%s%d" % (k, t) for k in ("tp", "fp", "pk", "eu", "yq", "yp")]
        P = "tp%d" % (t - 1) if t else "pu"
        WD, FR, WF = V("wd", 0, 2 * C), rows(RA), V("tc", H + R_N, H + C, 16)
        at = ((0, 1, 0, 1), (4, 5, 6, 7)) if t == 0 else ((4, 5, 6, 7), (0, 1, 6, 7))

        if t == 0:
            named("send")
            send(row("lp"), row("xp0"), "ap0", t)
            send(bits(V("lq", 0, H)), bits(V("xq0", 0, H)), "ax", t)
            send(bits(V("lq", H, C)), bits(V("xq0", H, C)), "aq0", t)
        unpack("fh", 0, "xq%d" % t, "xp%d" % t)
        named("twice")
        for b in range(2):
            for lo in (0, H):
                move(part("fb", b, lo, lo + H), part("fh", b, lo, lo + H), 2.0)
        for lo in (H, 0):
            named("here")
            move(V("rs", lo, lo + H), ind(row("sg"), V(P, 24 + lo // 16, 36 + lo // 16)), MC, BC)
            named("there")
            tt(rows(RB, lo, lo + H), ind(row("sg"), V(pk, 24 + lo // 16, 36 + lo // 16)), V("rs", lo, lo + H), A.add)
        named(None)
        turn(V("ta", H, C), rows(RB, H, C))
        turn(V("ta", T2 + 224, T2 + 416), rows(RB, 208, 400))
        turn(V("ta", 0, H), rows(RB, 0, H))
        turn(V("ta", T2, T2 + 224), rows(RB, -16, 208))
        scan(V("uu", UL + R_N - 12, UL + R_N + 372, 4), V("ta", 0, C, 4), V("sw", 0, 96))
        scan(V("uu", UR + R_P - 12, UR + R_P + 372, 4), V("ta", 0, C, 4), V("sw", 96, 192))
        turn(V("wd", 0, C), V("uu", UL, UL + C))
        turn(V("wd", C, 2 * C), V("uu", UR, UR + C))
        named("flag")
        move(V("sx", 1, 240, 5), pick("ta", L_B, 3), 0.5)
        act(V("sx", 3, 240, 5), pick("ta", L_S, 3), F.Abs, scale=0.5)
        a = 0 if last else 48
        flag(V("sf", a + 1, a + (96 if last else 64), 2), pick("ta", L_X, 3 if last else 2))
        named(None)
        scan(V("sb", 0, 120), V("sx", 0, 120), V("sx", 120, 240))
        ts(V("cw", 0, 24), V("sb", 4, 120, 5), MID, A.add)
        scan(V("so", a, 96), V("sf", a, 96), V("st", a, 96))
        ts(V(tp, a // 2, 48), V("so", a + 1, 96, 2), MID, A.add)
        named("ref")
        for lo, hi in ((160, 256), (256, C), (0, 160)):
            move(rows(RA, lo, hi), ind(WD, V("cw", lo // 16, hi // 16)), *((WE, ME) if t == 0 else ()))
        named(None)
        turn(V("tc", UP0, 576), rows(RA, 160, C))
        turn(V("tc", 576, 800), rows(RA, 176, 400))
        turn(V("tc", H, UP0), rows(RA, 0, 160))
        turn(V("tc", 0, H), rows(RA, -16, 176))
        offsets(fp, "tc", L_U, 3)
        named("fu")
        ts(V(tp, 48, 64), ind(V("tc", UP0, 800), V("cl", L_V, L_V + 1)), MID, A.add)
        named("fw")
        if t == 0:
            ts(V(tp, 64, 88), WF, MID, A.add)
        elif t == 1:
            short(V("fw", 0, 24), WF)
        named("send")
        send(*((V("lm", 0, 52), V(tp, 36, 88)), (V("lf", 0, 24), V("fw", 0, 24)), (row("lr"), FR))[t], "af%d" % t, t)
        if not last:
            named("base")
            short(V("st", 49, 96, 2), V("so", 49, 96, 2))
            move(V("sw", 99, 192, 4), ur(R_P))
            ts(terms(4), V(fp, 0, 24), -float(C + H), A.add)
            short(ul(R_P), ur(R_P))
            short(ur(R_F), WF)
        if t == 0:
            unpack("fs", 4, "lq", "lp", 0, H)
            unpack("fs", 4, "lq", "lp", H, C)
        for h in (1, 0):
            lo, hi = H * h, H * h + H
            win, one, two = "fh", V(tp, 24 + 12 * h, 36 + 12 * h), V(tp, 52, 64) if h else V(fp, 24, 36)
            if h and t == 0:
                win, one, two = "fs", V("lm", 0, 12), V("lm", 16, 28)
            for b in range(4):
                named("gG"[h])
                move(part("gb", b, lo, hi), ind(part(win, b), one))
                named("zZ"[h])
                tt(lane("zt", b, lo, hi), ind(part(win, b), two), part("gb", b, lo, hi), A.add)
            named("qQ"[h])
            if h and t:
                UQ, UP = V("zq%d" % t, 0, H), V("zp%d" % t, 0, H)
                quant(UQ, UP, V("zt", 4 * lo, 4 * hi))
                named("send")
                send(bits(V(YQ, H, C)), bits(UQ), "aq%d" % t, t)
                send(V(YP, H, C), UP, "ap%d" % t, t)
            else:
                quant(V(YQ, lo, hi), V(YP, lo, hi), V("zt", 4 * lo, 4 * hi))
        for h in range(2):
            for b in range(4):
                named("wW"[h])
                mm(at[h][b], "w", 128 * b, V(YQ, H * h, H * h + H), V(YP, H * h, H * h + H), H)
                named("bB"[h])
                move(part("bb", b, H * h, H * h + H), bank(at[h][b], 0, H), 0.03125)
        named("inv")
        if t == 0:
            scan(row("es"), row("mk"), FR, -MID - 1)
            to = ind(rows(RC), V(tp, 24, 48))
            emit({"v": lambda: g.vector.tensor_copy(to[1], T.es[:])}, [rows(RC)], [row("es"), V(tp, 24, 48)])
            turn2("td", RC)
            offsets("iv", "td", L_I, 3)
        elif t == 1:
            halves(lambda lo, hi: rows(RC, lo, hi), V("wd", 0, C), "iv", 0)
            turn2("td", RC)
            offsets("iw", "td", L_D, 2)
        if not last:
            named("tab")
            if t == 0:
                ts(ur(R_E), V("lm", 28, 52), -MID, A.add)
            else:
                short(ur(R_E), V("lf", 0, 24))
            turn(row("tab"), V("uu", UR, UR + C))
        named("e")
        if t == 1:
            halves(lambda lo, hi: V("ef", lo, hi), row("tab"), fp, 0)
        if last:
            move(row("ef"), ind(row("lr"), V(fp, 0, 24)))
            move(row("eg"), ind(row("ef"), V(tp, 0, 24)))
        halves(lambda lo, hi: rows(RD, lo, hi), *((row("tab"), "iv", 24), (row("ef"), "iw", 0), (row("eg"), "iw", 0))[t])
        named(None)
        turn2("te", RD)
        offsets(eu, "te", L_D if last else L_I, 2)
        if t == 0:
            named("load")
            dma("g", "ld_v", T.vin[:], T.v[:], [V("vin", 0, 512)], [V("lm", 0, 1)])
            dma("y", "pa", T.pf[:], T.po[:], [mark("pf")], [V("po", 0, 48), V("lm", 0, 1)])
        if last:
            quant(V("vq", 0, 128), V("vp", 0, 128), V("vin", 0, 512))
            named("store")
            dma("g", "pb", T.pf[:, 0:C], T.wd[R_P:128:16, C:2 * C], [], [V("wd", C, 2 * C), mark("pf")], accum_op=A.add)
            dma("g", "pb", T.pf[:, C:2 * C], T.rr[R_N:128:16, RA:RA + C], [], [FR, mark("pf")], accum_op=A.add)
        else:
            pairs(t + 1, row("tab"))
        named("x")
        for b in range(2):
            tt(lane("xt", b, 0, C), ind(part("bb", b), V(eu, 0, 24)), part("fb", b), A.add)
        for lo, hi in ((0, CUT), (CUT, C)):
            for b in (2, 3):
                named("bg")
                move(part("bg", b, lo, hi), ind(part("bb", b), V(eu, lo // 16, hi // 16)))
                named("add")
                tt(lane("xt", b, lo, hi), part("bg", b, lo, hi), bank(b, lo, hi), A.add)
        state(t + 1, "xt")

    named("store")
    dma("y", "out", T.oc[:], bits(row("xq3"))[1], [], [row("xq3")])
    for k in range(4):
        dma("s", "out", T.osc[4 * k:4 * k + 4, :], T.xp3[32 * k:32 * k + 4, :], [], [row("xp3")])
    dma("y", "out", T.y[:], T.yo[:], [], [row("yo")])

    seen = {}
    for c in calls:
        seen.setdefault(c["name"], []).append(c)
    by = {(k[0], k[1] + (str(i) if len(l) > 1 else "")): c for k, l in seen.items() for i, c in enumerate(l)}
    line = {}
    for q in queue:
        line[q] = []
        for word in ORDER[q].split():
            if word[0] == "@":
                stage = word[1]
            else:
                line[q].append(by[stage, word])
                line[q][-1]["q"] = q
    assert sum(len(l) for l in line.values()) == len(calls) and all("q" in c for c in calls)
    count, know = {}, {k: {} for k in queue}
    while any(line.values()):
        ready = [q for q in queue if line[q] and all("done" in calls[d] for d in line[q][0]["hard"] | line[q][0]["soft"])]
        q = ready[0]
        c, recs = line[q].pop(0), {}
        for d in c["hard"] | {d for d in c["soft"] if calls[d]["q"] != q}:
            s, v, snap = calls[d]["done"]
            if s not in recs or recs[s][1] < v:
                recs[s] = (s, v, snap)
        recs = list(recs.values())
        for s, v, snap in recs:
            if know[q].get(s, 0) < v and not any(o[2].get(s, 0) >= v and o[0] != s and know[q].get(o[0], 0) < o[1] for o in recs):
                queue[q].wait_ge(T.sem[s], v)
                know[q][s] = v
        for s, v, snap in recs:
            for k in snap:
                know[q][k] = max(know[q].get(k, 0), snap[k])
        s = c["s"] or "q" + q
        count[s] = count.get(s, 0) + c["n"]
        if c["far"]:
            c["ways"][q]()
            count["sent"] = count.get("sent", 0) + c["n"]
            c["done"] = (s, count[s], {s: count[s]})
        else:
            c["ways"][q]().then_inc(T.sem[s], c["n"])
            c["done"] = (s, count[s], dict(know[q], **{s: count[s]}))
    for s in count:
        if know["g"].get(s, 0) < count[s]:
            g.wait_ge(T.sem[s], count[s])
